import numpy as np
import ml_dtypes


def mxq(x, axis, fmt="e4m3"):
    dtype, down = {"e4m3": (ml_dtypes.float8_e4m3fn, 7), "e5m2": (ml_dtypes.float8_e5m2, 14)}[fmt]
    v = np.moveaxis(np.asarray(x, np.float32).astype(ml_dtypes.bfloat16).astype(np.float64), axis, -1)
    blocks = v.reshape(v.shape[:-1] + (-1, 32))
    amax = np.abs(blocks).max(-1, keepdims=True)
    byte = np.maximum(np.where(amax > 0, np.frexp(amax)[1] - 1 + 127, 0) - down, 1)
    scale = np.exp2(byte - 127.0)
    codes = (blocks / scale).astype(np.float32).astype(dtype).astype(np.float64)
    return np.moveaxis((codes * scale).reshape(v.shape), -1, axis)


WIDE = False


def mx_kscale(k):
    if not WIDE:
        return np.ones(k)
    levels = np.array([10, -10, 5, -5, 0])
    if k % 512:
        return np.exp2(np.random.permutation(np.resize(levels, k // 32))).repeat(32)
    a = np.empty((k // 512, 16))
    for p in range(k // 512):
        a[p, :8] = np.random.permutation(np.resize(levels, 8))
        for g in range(8):
            far = levels[np.abs(levels - a[p, g]) >= 10]
            a[p, g + 8] = far[np.random.randint(len(far))]
    return np.exp2(a.ravel()).repeat(32)


def f64(x):
    return np.asarray(x).astype(np.float64)


def striped(idx):
    return np.tile(idx.reshape(-1, 16).T, (8, 1)).astype(np.uint16)


def unstriped(offs):
    return offs[:16].T.reshape(-1).astype(np.int64)


E2M1 = np.array([0.0, 0.5, 1.0, 1.5, 2.0, 3.0, 4.0, 6.0, -0.0, -0.5, -1.0, -1.5, -2.0, -3.0, -4.0, -6.0])


def pack_weight(w, fmt):
    k, n = w.shape
    w = f64(np.asarray(w, np.float32).astype(ml_dtypes.bfloat16)).reshape(k // 32, 32, n)
    amax = np.abs(w).max(1)
    if fmt == "e4m3":
        byte = np.frexp(amax)[1] - 1 + 127 - 7
    else:
        mant, ex = np.frexp(amax / 6.0)
        byte = np.where(mant > 0.5, ex, ex - 1) + 127
    byte = np.clip(np.where(amax > 0, byte, 1), 1, 254)
    scaled = (w * np.exp2(127.0 - byte)[:, None, :]).reshape(k, n).astype(np.float32)
    by_word = np.ascontiguousarray(scaled.reshape(k // 512, 128, 4, n).transpose(0, 1, 3, 2))
    if fmt == "e4m3":
        words = by_word.astype(ml_dtypes.float8_e4m3fn).view(np.uint8)
    else:
        c = by_word.astype(ml_dtypes.float4_e2m1fn).view(np.uint8) & 0xF
        words = (c[..., 0::2] | (c[..., 1::2] << 4)).reshape(k // 512, 128, 2 * n)
    return np.ascontiguousarray(words), np.ascontiguousarray(byte.astype(np.uint8).reshape(k // 512, 16, n))


def unpack_weight(words, scales, fmt):
    g, _, n = scales.shape
    words = np.ascontiguousarray(words).reshape(g, 128, n, -1)
    if fmt == "e4m3":
        vals = words.view(ml_dtypes.float8_e4m3fn).astype(np.float64)
    else:
        nib = np.empty((g, 128, n, 4), np.uint8)
        nib[..., 0::2] = words & 0xF
        nib[..., 1::2] = words >> 4
        vals = E2M1[nib]
    vals = vals * np.repeat(np.exp2(scales.astype(np.float64) - 127.0), 8, axis=1)[..., None]
    return vals.transpose(0, 1, 3, 2).reshape(g * 512, n)


def gelu(v):
    return 0.5 * v * (1.0 + np.tanh(np.sqrt(2.0 / np.pi) * (v + 0.044715 * v**3)))


def striped8(idx):
    return np.concatenate([v.reshape(-1, 16).T for v in idx]).astype(np.uint16)


def unstriped8(offs):
    return np.stack([offs[16 * g:16 * g + 16].T.reshape(-1) for g in range(8)]).astype(np.int64)


def runs(v, idx8):
    k = np.arange(v.shape[0])
    return v[k[:, None], idx8[k % 512 // 64]]


K, H, T, S = 1024, 512, 2048, 1024

def setup_inputs():
    n = np.random.standard_normal
    s = mx_kscale(K)[:, None]
    u = mx_kscale(H)[:, None]
    w = mx_kscale(S)
    tab_words, tab_scales = pack_weight(n((K, T)) * s, "e4m3")
    tab2_words, tab2_scales = pack_weight(n((K, T)) * s, "e4m3")
    wm_words, wm_scales = pack_weight(0.25 * n((K, H)) / np.sqrt(K) / s * u.T, "e2m1")
    return {
        "tab_words": tab_words, "tab_scales": tab_scales,
        "tab2_words": tab2_words, "tab2_scales": tab2_scales,
        "wm_words": wm_words, "wm_scales": wm_scales,
        "wb": (0.25 * n((K, H)) / np.sqrt(K) / s / u.T).astype(np.float32),
        "occ": (np.random.uniform(0.5, 1.5, S) * w).astype(np.float32),
        "dwell": (np.random.uniform(0.5, 1.5, S) / w).astype(np.float32),
        "gain": (np.random.uniform(0.3, 0.8, H) * u[:, 0]).astype(np.float32),
        "offs": striped8(np.stack([np.random.permutation(T)[:S] for _ in range(8)])),
        "offs2": striped(np.random.permutation(T)[:S]),
    }

def reference(tab_words, tab_scales, tab2_words, tab2_scales, wm_words, wm_scales,
              wb, occ, dwell, gain, offs, offs2):
    v = runs(unpack_weight(tab_words, tab_scales, "e4m3"), unstriped8(offs))
    v2 = unpack_weight(tab2_words, tab2_scales, "e4m3")[:, unstriped(offs2)]
    wm = unpack_weight(wm_words, wm_scales, "e2m1")
    h = wm.T @ v
    b = mxq(f64(wb), 0, "e4m3").T @ v2
    x = mxq(b, 0, "e4m3").T @ mxq(h, 0, "e4m3")
    loop = f64(occ)[:, None] / (1.0 + np.exp(-x))
    c = (b * f64(dwell)[None, :]).T
    y = mxq(c, 0, "e4m3").T @ mxq(loop, 0, "e4m3")
    return y * f64(gain)[:, None]

@@ -1,0 +1,303 @@
+from contextlib import ExitStack
+
+import concourse.mybir as mybir
+from concourse.masks import make_identity
+
+K, H, T, S = 1024, 512, 2048, 1024
+FLOPS = 2 * (K * H * S + K * H * S + H * S * S + S * H * S)
+
+F32 = mybir.dt.float32
+BF16 = mybir.dt.bfloat16
+I32 = mybir.dt.int32
+U32 = mybir.dt.uint32
+U16 = mybir.dt.uint16
+U8 = mybir.dt.uint8
+FP8X4 = mybir.dt.float8_e4m3fn_x4
+FP4X4 = mybir.dt.float4_e2m1fn_x4
+ACT = mybir.ActivationFunctionType
+MULT = mybir.AluOpType.mult
+
+P = 128
+PASSES = 2
+HALF = 512
+CHUNKS = [256, 256, 256, 128, 128]
+
+
+def tile_list_chromatin_loop_map_kernel(
+    tc, tab_words, tab_scales, tab2_words, tab2_scales, wm_words, wm_scales, wb, occ, dwell, gain, offs, offs2, out
+):
+    nc = tc.nc
+    with ExitStack() as ctx:
+        keep = ctx.enter_context(tc.tile_pool(name="keep", bufs=1))
+        ring = ctx.enter_context(tc.tile_pool(name="ring", bufs=3))
+        pair = ctx.enter_context(tc.tile_pool(name="pair", bufs=2))
+        psum = ctx.enter_context(tc.psum_pool(name="psum", bufs=6))
+        psum_y = ctx.enter_context(tc.psum_pool(name="psum_y", bufs=2))
+
+        def held(name, shape, dtype):
+            return keep.tile(shape, dtype, name=name, align_bytes=64)
+
+        lists = held("lists", [P, S // 16], U16)
+        list2 = held("list2", [P, S // 16], U16)
+        win1 = held("win1", [P, T], U8)
+        win2 = held("win2", [P, T], U8)
+        planes1 = held("planes1", [P, PASSES * S], U8)
+        wms_raw = held("wms_raw", [P, PASSES * H], U8)
+        rows = held("rows", [P, 2 * P], F32)
+        ident = held("ident", [P, P], F32)
+
+        nc.gpsimd.memset(win2[:].bitcast(I32), 0)
+        nc.gpsimd.memset(wms_raw[:].bitcast(I32), 0)
+        make_identity(nc, ident[:])
+        nc.vector.memset(rows[:], 0.0)
+        nc.vector.memset(win1[:].bitcast(I32), 0)
+        nc.vector.memset(planes1[:].bitcast(I32), 0)
+
+        wb_raw = [held("wb_raw0", [P, 4, H], F32), held("staging", [P, 4, H], F32)]
+        words2 = [held("words2_%d" % a, [P, T], I32) for a in range(PASSES)]
+        words1 = [held("words1_0", [P, T], I32)]
+        wm_raw = held("wm_raw", [P, PASSES, 2 * H], U8)
+        gains = held("gains", [P, 4], F32)
+
+        def load_words(tile, table, a):
+            nc.sync.dma_start(tile[:], table[a].rearrange("p t i -> p (t i)").bitcast(I32))
+
+        def load_vector(first, vec):
+            nc.sync.dma_start(
+                rows[first : first + 4, :].rearrange("t (g s) -> t g s", s=8),
+                vec.rearrange("(g t s) -> t g s", t=4, s=8),
+            )
+
+        nc.sync.dma_start(list2[:], offs2)
+        nc.sync.dma_start(lists[:], offs)
+        for d in range(4):
+            nc.sync.dma_start(
+                win2[32 * d : 32 * d + 8, :].bitcast(I32), tab2_scales[:, 4 * d : 4 * d + 4, :].bitcast(I32)
+            )
+        for a in range(PASSES):
+            nc.sync.dma_start(wb_raw[a][:], wb[HALF * a : HALF * (a + 1), :].rearrange("(p i) c -> p i c", i=4))
+        load_words(words2[0], tab2_words, 0)
+        load_vector(0, dwell)
+        for d in range(4):
+            nc.scalar.dma_start(
+                win1[32 * d + 12 : 32 * d + 20, :].bitcast(I32),
+                tab_scales[:, 4 * d : 4 * d + 4, :].rearrange("a i t -> i a t").bitcast(I32),
+            )
+        load_vector(4, occ)
+        load_words(words2[1], tab2_words, 1)
+        with nc.allow_non_contiguous_dma(reason="one gain for each partition and tile of output rows"):
+            nc.sync.dma_start(gains[:], gain.rearrange("(r p) -> p r", p=P))
+        nc.sync.dma_start(wm_raw[:].bitcast(I32), wm_words.rearrange("a p c -> p a c").bitcast(I32))
+        load_words(words1[0], tab_words, 0)
+        for d in range(4):
+            nc.gpsimd.dma_start(
+                wms_raw[32 * d : 32 * d + 4, :].bitcast(I32).rearrange("i (a c) -> i a c", a=PASSES),
+                wm_scales[:, 4 * d : 4 * d + 4, :].rearrange("a i c -> i a c").bitcast(I32),
+            )
+
+        picked2 = held("picked2", [P, S], U8)
+        nc.vector.tensor_copy(picked2[:], win2[:].indirect(list2[:]))
+        planes2 = held("planes2", [P, S], U8)
+        nc.vector.tensor_copy(
+            planes2[:].bitcast(I32).rearrange("p (h t i w) -> p h t i w", h=2, t=4, w=2),
+            picked2[:].bitcast(I32).rearrange("p (h i t w) -> p h t i w", h=2, t=4, w=2),
+        )
+        picked1 = held("picked1", [P, S], U8)
+        nc.vector.tensor_copy(picked1[:], win1[:].indirect(lists[:]))
+        for d in range(4):
+            nc.sync.dma_start(
+                planes1[32 * d : 32 * d + 4, :].bitcast(I32), picked1[32 * d + 12 : 32 * d + 20, :].bitcast(I32)
+            )
+
+        wb_codes = held("wb_codes", [P, PASSES * H], U32)
+        wb_scales = held("wb_scales", [P, PASSES * H], U8)
+        for a in range(PASSES):
+            woven = held("wb_woven%d" % a, [P, H, 4], BF16)
+            nc.scalar.copy(
+                woven[:].rearrange("p (c n) i -> p c i n", n=4), wb_raw[a][:].rearrange("p i (c n) -> p c i n", n=4)
+            )
+            nc.vector.quantize_mx(
+                out=wb_codes[:, H * a : H * (a + 1)].bitcast(FP8X4),
+                scales=wb_scales[:, H * a : H * (a + 1)],
+                in_=woven[:].rearrange("p c i -> p (c i)"),
+            )
+
+        words1.append(held("staging", [P, T], I32))
+        load_words(words1[1], tab_words, 1)
+
+        vec_bank = psum_y.tile([P, 512], F32, name="ybank")
+        for h in range(2):
+            nc.tensor.transpose(vec_bank[:, P * h : P * (h + 1)], rows[:, P * h : P * (h + 1)], ident[:])
+        vecs = held("vecs", [P, 2, 8], F32)
+        nc.scalar.copy(vecs[:], vec_bank[:, 0 : 2 * P].rearrange("p (h c) -> p h c", h=2)[:, :, 0:8])
+
+        wm_codes = held("wm_codes", [P, PASSES * 2 * H], U8)
+        nc.vector.tensor_copy(
+            wm_codes[:].bitcast(I32).rearrange("p (a t i w) -> p a t i w", a=PASSES, t=4, w=4),
+            wm_raw[:].bitcast(I32).rearrange("p a (i t w) -> p a t i w", t=4, w=4),
+        )
+        wm_planes = held("wm_planes", [P, PASSES * H], U8)
+        nc.vector.tensor_copy(
+            wm_planes[:].bitcast(I32).rearrange("p (a t i w) -> p a t i w", a=PASSES, t=4, w=2),
+            wms_raw[:].bitcast(I32).rearrange("p (a i t w) -> p a t i w", a=PASSES, t=4, w=2),
+        )
+
+        b_codes = held("b_codes", [P, S], U32)
+        b_scales = held("b_scales", [P, S], U8)
+        c_codes = held("c_codes", [P, 2 * H], U32)
+        c_scales = held("c_scales", [P, 2 * H], U8)
+
+        def motif_gather(h):
+            tiles = []
+            for a in range(PASSES):
+                v2 = pair.tile([P, HALF], U32, name="picked%d" % a, align_bytes=64)
+                nc.vector.tensor_copy(
+                    v2[:].rearrange("p (t i s) -> p i t s", t=4, s=8),
+                    words2[a][:].bitcast(U32).indirect(list2[:, 32 * h : 32 * (h + 1)]),
+                )
+                tiles.append(v2)
+            return tiles
+
+        def motif_stage(h, v2):
+            bt = held("bt%d" % h, [P, 4, 2, 256], BF16)
+            c_woven = held("c_woven%d" % h, [P, H, 4], BF16)
+            for r in range(4):
+                bank = psum.tile([P, 512], F32, name="bank")
+                for t in range(4):
+                    for a in range(PASSES):
+                        nc.tensor.matmul_mx(
+                            out=bank[:, P * t : P * (t + 1)],
+                            lhsT=v2[a][:, P * t : P * (t + 1)].bitcast(FP8X4),
+                            lhsT_scale=planes2[4 * a :, HALF * h + P * t : HALF * h + P * (t + 1)],
+                            rhs=wb_codes[:, H * a + P * r : H * a + P * (r + 1)].bitcast(FP8X4),
+                            rhs_scale=wb_scales[:, H * a + P * r : H * a + P * (r + 1)],
+                            start=(a == 0),
+                            stop=(a == PASSES - 1),
+                        )
+                nc.scalar.copy(
+                    bt[:, :, :, 64 * r : 64 * (r + 1)].rearrange("p t u (i s e) -> p t i u s e", i=4, e=2),
+                    bank[:].rearrange("p (t i u e s) -> p t i u s e", t=4, i=4, u=2, e=2),
+                )
+                nc.vector.tensor_tensor(
+                    c_woven[:, P * r : P * (r + 1), :],
+                    bank[:].rearrange("p (t c) -> p c t", t=4),
+                    vecs[:, h : h + 1, 0:4].to_broadcast([P, P, 4]),
+                    MULT,
+                )
+            nc.vector.quantize_mx(
+                out=c_codes[:, H * h : H * (h + 1)].bitcast(FP8X4),
+                scales=c_scales[:, H * h : H * (h + 1)],
+                in_=c_woven[:].rearrange("p c t -> p (c t)"),
+            )
+            b_woven = held("b_woven%d" % h, [P, HALF * 4], BF16)
+            pairs = bt[:].bitcast(F32)
+            for half in range(2):
+                bank = psum.tile([P, 512], F32, name="bank")
+                for t in range(2):
+                    for u in range(2):
+                        col = P * (2 * t + u)
+                        nc.tensor.transpose(bank[:, col : col + P], pairs[:, 2 * half + t, u, :], ident[:])
+                nc.scalar.copy(
+                    b_woven[:, 1024 * half : 1024 * (half + 1)].bitcast(F32).rearrange("p (t m u) -> p t m u", t=2, u=2),
+                    bank[:].rearrange("p (t u m) -> p t m u", t=2, u=2),
+                )
+            nc.vector.quantize_mx(
+                out=b_codes[:, HALF * h : HALF * (h + 1)].bitcast(FP8X4),
+                scales=b_scales[:, HALF * h : HALF * (h + 1)],
+                in_=b_woven[:],
+            )
+
+        h_codes = held("h_codes", [P, S], U32)
+        h_scales = held("h_scales", [P, S], U8)
+
+        def anchor_stage(j0, width):
+            v1 = []
+            for a in range(PASSES):
+                picked = pair.tile([P, width], U32, name="picked%d" % a, align_bytes=64)
+                nc.vector.tensor_copy(
+                    picked[:], words1[a][:].bitcast(U32).indirect(lists[:, j0 // 16 : (j0 + width) // 16])
+                )
+                v1.append(picked)
+            h_woven = pair.tile([P, width, 4], BF16, name="h_woven", align_bytes=64)
+            for j in range(0, width, P):
+                bank = psum.tile([P, 512], F32, name="bank")
+                for t in range(4):
+                    for a in range(PASSES):
+                        nc.tensor.matmul_mx(
+                            out=bank[:, P * t : P * (t + 1)],
+                            lhsT=wm_codes[:, 2 * (H * a + P * t) : 2 * (H * a + P * (t + 1))].bitcast(FP4X4),
+                            lhsT_scale=wm_planes[:, H * a + P * t : H * a + P * (t + 1)],
+                            rhs=v1[a][:, j : j + P].bitcast(FP8X4),
+                            rhs_scale=planes1[:, S * a + j0 + j : S * a + j0 + j + P],
+                            start=(a == 0),
+                            stop=(a == PASSES - 1),
+                        )
+                nc.scalar.copy(h_woven[:, j : j + P, :], bank[:].rearrange("p (t c) -> p c t", t=4))
+            nc.vector.quantize_mx(
+                out=h_codes[:, j0 : j0 + width].bitcast(FP8X4),
+                scales=h_scales[:, j0 : j0 + width],
+                in_=h_woven[:].rearrange("p c t -> p (c t)"),
+            )
+
+        def loop_stage(j0, width, h):
+            sig = ring.tile([P, width, 4], F32, name="sig", align_bytes=64)
+            for j in range(0, width, P):
+                bank = psum.tile([P, 512], F32, name="bank")
+                for t in range(4):
+                    cols = slice(HALF * h + P * t, HALF * h + P * (t + 1))
+                    nc.tensor.matmul_mx(
+                        out=bank[:, P * t : P * (t + 1)],
+                        lhsT=b_codes[:, cols].bitcast(FP8X4),
+                        lhsT_scale=b_scales[:, cols],
+                        rhs=h_codes[:, j0 + j : j0 + j + P].bitcast(FP8X4),
+                        rhs_scale=h_scales[:, j0 + j : j0 + j + P],
+                        start=True,
+                        stop=True,
+                    )
+                nc.scalar.activation(sig[:, j : j + P, :], bank[:].rearrange("p (t c) -> p c t", t=4), ACT.Sigmoid)
+            woven = ring.tile([P, width, 4], BF16, name="loop_woven", align_bytes=64)
+            nc.vector.tensor_tensor(woven[:], sig[:], vecs[:, h : h + 1, 4:8].to_broadcast([P, width, 4]), MULT)
+            codes = held("loop_codes%d_%d" % (j0, h), [P, width], U32)
+            scales = held("loop_scales%d_%d" % (j0, h), [P, width], U8)
+            nc.vector.quantize_mx(
+                out=codes[:].bitcast(FP8X4), scales=scales[:], in_=woven[:].rearrange("p c t -> p (c t)")
+            )
+            return codes, scales
+
+        def read_back(j0, width, loop):
+            result = ring.tile([P, 4, width], F32, name="result", align_bytes=64)
+            per_bank = 512 // width
+            for r0 in range(0, 4, per_bank):
+                bank = psum_y.tile([P, 512], F32, name="ybank")
+                for r in range(r0, r0 + per_bank):
+                    for h in range(2):
+                        cols = slice(H * h + P * r, H * h + P * (r + 1))
+                        nc.tensor.matmul_mx(
+                            out=bank[:, width * (r - r0) : width * (r - r0 + 1)],
+                            lhsT=c_codes[:, cols].bitcast(FP8X4),
+                            lhsT_scale=c_scales[:, cols],
+                            rhs=loop[h][0][:].bitcast(FP8X4),
+                            rhs_scale=loop[h][1][:],
+                            start=(h == 0),
+                            stop=(h == 1),
+                        )
+                for r in range(r0, r0 + per_bank):
+                    nc.scalar.activation(
+                        result[:, r, :],
+                        bank[:, width * (r - r0) : width * (r - r0 + 1)],
+                        ACT.Copy,
+                        scale=gains[:, r : r + 1],
+                    )
+            nc.sync.dma_start(out.rearrange("(r p) j -> p r j", p=P)[:, :, j0 : j0 + width], result[:])
+
+        v2 = [motif_gather(h) for h in range(2)]
+        for h in range(2):
+            motif_stage(h, v2[h])
+        anchor_stage(0, 256)
+        j0 = 0
+        for width in CHUNKS:
+            if j0 + 256 < S and j0 % 256 == 0:
+                anchor_stage(j0 + 256, 256)
+            loop = [loop_stage(j0, width, h) for h in range(2)]
+            read_back(j0, width, loop)
+            j0 = j0 + width

@@ -47,15 +47,17 @@ def tile_list_chromatin_loop_map_kernel(
         ident = held("ident", [P, P], F32)
 
         nc.gpsimd.memset(win2[:].bitcast(I32), 0)
-        nc.gpsimd.memset(wms_raw[:].bitcast(I32), 0)
-        make_identity(nc, ident[:])
-        nc.vector.memset(rows[:], 0.0)
         nc.vector.memset(win1[:].bitcast(I32), 0)
+        nc.vector.memset(rows[:], 0.0)
+        nc.vector.memset(wms_raw[:].bitcast(I32), 0)
         nc.vector.memset(planes1[:].bitcast(I32), 0)
+        make_identity(nc, ident[:])
+        warm = held("warm", [P, 1], F32)
+        nc.scalar.activation(warm[:], ident[:, 0:1], ACT.Sigmoid)
 
-        wb_raw = [held("wb_raw0", [P, 4, H], F32), held("staging", [P, 4, H], F32)]
+        wb_raw = [held("wb_raw%d" % a, [P, 4, H], F32) for a in range(PASSES)]
         words2 = [held("words2_%d" % a, [P, T], I32) for a in range(PASSES)]
-        words1 = [held("words1_0", [P, T], I32)]
+        words1 = [held("words1_%d" % a, [P, T], I32) for a in range(PASSES)]
         wm_raw = held("wm_raw", [P, PASSES, 2 * H], U8)
         gains = held("gains", [P, 4], F32)
 
@@ -68,32 +70,36 @@ def tile_list_chromatin_loop_map_kernel(
                 vec.rearrange("(g t s) -> t g s", t=4, s=8),
             )
 
+        def load_wb(a):
+            nc.sync.dma_start(wb_raw[a][:], wb[HALF * a : HALF * (a + 1), :].rearrange("(p i) c -> p i c", i=4))
+
         nc.sync.dma_start(list2[:], offs2)
         nc.sync.dma_start(lists[:], offs)
         for d in range(4):
             nc.sync.dma_start(
                 win2[32 * d : 32 * d + 8, :].bitcast(I32), tab2_scales[:, 4 * d : 4 * d + 4, :].bitcast(I32)
             )
-        for a in range(PASSES):
-            nc.sync.dma_start(wb_raw[a][:], wb[HALF * a : HALF * (a + 1), :].rearrange("(p i) c -> p i c", i=4))
         load_words(words2[0], tab2_words, 0)
-        load_vector(0, dwell)
+        load_wb(0)
         for d in range(4):
-            nc.scalar.dma_start(
+            nc.sync.dma_start(
                 win1[32 * d + 12 : 32 * d + 20, :].bitcast(I32),
                 tab_scales[:, 4 * d : 4 * d + 4, :].rearrange("a i t -> i a t").bitcast(I32),
             )
-        load_vector(4, occ)
+        load_wb(1)
         load_words(words2[1], tab2_words, 1)
-        with nc.allow_non_contiguous_dma(reason="one gain for each partition and tile of output rows"):
-            nc.sync.dma_start(gains[:], gain.rearrange("(r p) -> p r", p=P))
-        nc.sync.dma_start(wm_raw[:].bitcast(I32), wm_words.rearrange("a p c -> p a c").bitcast(I32))
+        load_vector(0, dwell)
+        load_vector(4, occ)
         load_words(words1[0], tab_words, 0)
+        nc.sync.dma_start(wm_raw[:].bitcast(I32), wm_words.rearrange("a p c -> p a c").bitcast(I32))
         for d in range(4):
-            nc.gpsimd.dma_start(
+            nc.sync.dma_start(
                 wms_raw[32 * d : 32 * d + 4, :].bitcast(I32).rearrange("i (a c) -> i a c", a=PASSES),
                 wm_scales[:, 4 * d : 4 * d + 4, :].rearrange("a i c -> i a c").bitcast(I32),
             )
+        load_words(words1[1], tab_words, 1)
+        with nc.allow_non_contiguous_dma(reason="one gain for each partition and tile of output rows"):
+            nc.sync.dma_start(gains[:], gain.rearrange("(r p) -> p r", p=P))
 
         picked2 = held("picked2", [P, S], U8)
         nc.vector.tensor_copy(picked2[:], win2[:].indirect(list2[:]))
@@ -122,9 +128,6 @@ def tile_list_chromatin_loop_map_kernel(
                 in_=woven[:].rearrange("p c i -> p (c i)"),
             )
 
-        words1.append(held("staging", [P, T], I32))
-        load_words(words1[1], tab_words, 1)
-
         vec_bank = psum_y.tile([P, 512], F32, name="ybank")
         for h in range(2):
             nc.tensor.transpose(vec_bank[:, P * h : P * (h + 1)], rows[:, P * h : P * (h + 1)], ident[:])
@@ -147,33 +150,36 @@ def tile_list_chromatin_loop_map_kernel(
         c_codes = held("c_codes", [P, 2 * H], U32)
         c_scales = held("c_scales", [P, 2 * H], U8)
 
-        def motif_gather(h):
-            tiles = []
-            for a in range(PASSES):
-                v2 = pair.tile([P, HALF], U32, name="picked%d" % a, align_bytes=64)
-                nc.vector.tensor_copy(
-                    v2[:].rearrange("p (t i s) -> p i t s", t=4, s=8),
-                    words2[a][:].bitcast(U32).indirect(list2[:, 32 * h : 32 * (h + 1)]),
-                )
-                tiles.append(v2)
-            return tiles
+        def motif_gather(a, h):
+            v2 = pair.tile([P, HALF], U32, name="picked%d" % a, align_bytes=64)
+            nc.vector.tensor_copy(
+                v2[:].rearrange("p (t i s) -> p i t s", t=4, s=8),
+                words2[a][:].bitcast(U32).indirect(list2[:, 32 * h : 32 * (h + 1)]),
+            )
+            return v2
 
         def motif_stage(h, v2):
             bt = held("bt%d" % h, [P, 4, 2, 256], BF16)
             c_woven = held("c_woven%d" % h, [P, H, 4], BF16)
-            for r in range(4):
-                bank = psum.tile([P, 512], F32, name="bank")
+            banks = [psum.tile([P, 512], F32, name="bank") for r in range(4)]
+
+            def passes(a, r):
                 for t in range(4):
-                    for a in range(PASSES):
-                        nc.tensor.matmul_mx(
-                            out=bank[:, P * t : P * (t + 1)],
-                            lhsT=v2[a][:, P * t : P * (t + 1)].bitcast(FP8X4),
-                            lhsT_scale=planes2[4 * a :, HALF * h + P * t : HALF * h + P * (t + 1)],
-                            rhs=wb_codes[:, H * a + P * r : H * a + P * (r + 1)].bitcast(FP8X4),
-                            rhs_scale=wb_scales[:, H * a + P * r : H * a + P * (r + 1)],
-                            start=(a == 0),
-                            stop=(a == PASSES - 1),
-                        )
+                    nc.tensor.matmul_mx(
+                        out=banks[r][:, P * t : P * (t + 1)],
+                        lhsT=v2[a][:, P * t : P * (t + 1)].bitcast(FP8X4),
+                        lhsT_scale=planes2[4 * a :, HALF * h + P * t : HALF * h + P * (t + 1)],
+                        rhs=wb_codes[:, H * a + P * r : H * a + P * (r + 1)].bitcast(FP8X4),
+                        rhs_scale=wb_scales[:, H * a + P * r : H * a + P * (r + 1)],
+                        start=(a == 0 and t == 0),
+                        stop=(a == PASSES - 1 and t == 3),
+                    )
+
+            for r in range(4):
+                passes(0, r)
+            for r in range(4):
+                bank = banks[r]
+                passes(1, r)
                 nc.scalar.copy(
                     bt[:, :, :, 64 * r : 64 * (r + 1)].rearrange("p t u (i s e) -> p t i u s e", i=4, e=2),
                     bank[:].rearrange("p (t i u e s) -> p t i u s e", t=4, i=4, u=2, e=2),
@@ -184,11 +190,6 @@ def tile_list_chromatin_loop_map_kernel(
                     vecs[:, h : h + 1, 0:4].to_broadcast([P, P, 4]),
                     MULT,
                 )
-            nc.vector.quantize_mx(
-                out=c_codes[:, H * h : H * (h + 1)].bitcast(FP8X4),
-                scales=c_scales[:, H * h : H * (h + 1)],
-                in_=c_woven[:].rearrange("p c t -> p (c t)"),
-            )
             b_woven = held("b_woven%d" % h, [P, HALF * 4], BF16)
             pairs = bt[:].bitcast(F32)
             for half in range(2):
@@ -205,6 +206,14 @@ def tile_list_chromatin_loop_map_kernel(
                 out=b_codes[:, HALF * h : HALF * (h + 1)].bitcast(FP8X4),
                 scales=b_scales[:, HALF * h : HALF * (h + 1)],
                 in_=b_woven[:],
+            )
+            return c_woven
+
+        def quantise_c(h, c_woven):
+            nc.vector.quantize_mx(
+                out=c_codes[:, H * h : H * (h + 1)].bitcast(FP8X4),
+                scales=c_scales[:, H * h : H * (h + 1)],
+                in_=c_woven[:].rearrange("p c t -> p (c t)"),
             )
 
         h_codes = held("h_codes", [P, S], U32)
@@ -240,7 +249,7 @@ def tile_list_chromatin_loop_map_kernel(
             )
 
         def loop_stage(j0, width, h):
-            sig = ring.tile([P, width, 4], F32, name="sig", align_bytes=64)
+            sig = ring.tile([P, width, 4], F32, name="sig", align_bytes=64, bufs=8)
             for j in range(0, width, P):
                 bank = psum.tile([P, 512], F32, name="bank")
                 for t in range(4):
@@ -257,6 +266,9 @@ def tile_list_chromatin_loop_map_kernel(
                 nc.scalar.activation(sig[:, j : j + P, :], bank[:].rearrange("p (t c) -> p c t", t=4), ACT.Sigmoid)
             woven = ring.tile([P, width, 4], BF16, name="loop_woven", align_bytes=64)
             nc.vector.tensor_tensor(woven[:], sig[:], vecs[:, h : h + 1, 4:8].to_broadcast([P, width, 4]), MULT)
+            return woven
+
+        def loop_quantise(j0, width, h, woven):
             codes = held("loop_codes%d_%d" % (j0, h), [P, width], U32)
             scales = held("loop_scales%d_%d" % (j0, h), [P, width], U8)
             nc.vector.quantize_mx(
@@ -265,39 +277,53 @@ def tile_list_chromatin_loop_map_kernel(
             return codes, scales
 
         def read_back(j0, width, loop):
-            result = ring.tile([P, 4, width], F32, name="result", align_bytes=64)
-            per_bank = 512 // width
-            for r0 in range(0, 4, per_bank):
+            last = j0 + width == S
+            for r0 in (0, 2):
                 bank = psum_y.tile([P, 512], F32, name="ybank")
-                for r in range(r0, r0 + per_bank):
-                    for h in range(2):
-                        cols = slice(H * h + P * r, H * h + P * (r + 1))
+                for h in range(2):
+                    for r in range(2):
+                        cols = slice(H * h + P * (r0 + r), H * h + P * (r0 + r + 1))
                         nc.tensor.matmul_mx(
-                            out=bank[:, width * (r - r0) : width * (r - r0 + 1)],
+                            out=bank[:, width * r : width * (r + 1)],
                             lhsT=c_codes[:, cols].bitcast(FP8X4),
                             lhsT_scale=c_scales[:, cols],
                             rhs=loop[h][0][:].bitcast(FP8X4),
                             rhs_scale=loop[h][1][:],
-                            start=(h == 0),
-                            stop=(h == 1),
+                            start=(h == 0 and r == 0),
+                            stop=(h == 1 and r == 1),
                         )
-                for r in range(r0, r0 + per_bank):
-                    nc.scalar.activation(
-                        result[:, r, :],
-                        bank[:, width * (r - r0) : width * (r - r0 + 1)],
-                        ACT.Copy,
-                        scale=gains[:, r : r + 1],
+                result = ring.tile([P, 2, width], F32, name="result", align_bytes=64, bufs=6)
+                if last and r0 == 0:
+                    nc.vector.tensor_tensor(
+                        result[:],
+                        bank[:, 0 : 2 * width].rearrange("p (r c) -> p r c", r=2),
+                        gains[:, r0 : r0 + 2].unsqueeze(2).to_broadcast([P, 2, width]),
+                        MULT,
                     )
-            nc.sync.dma_start(out.rearrange("(r p) j -> p r j", p=P)[:, :, j0 : j0 + width], result[:])
+                else:
+                    for r in range(2):
+                        nc.scalar.activation(
+                            result[:, r, :],
+                            bank[:, width * r : width * (r + 1)],
+                            ACT.Copy,
+                            scale=gains[:, r0 + r : r0 + r + 1],
+                        )
+                nc.sync.dma_start(
+                    out.rearrange("(r p) j -> p r j", p=P)[:, r0 : r0 + 2, j0 : j0 + width], result[:]
+                )
 
-        v2 = [motif_gather(h) for h in range(2)]
-        for h in range(2):
-            motif_stage(h, v2[h])
+        v2 = [[motif_gather(a, h) for h in range(2)] for a in range(PASSES)]
+        c_woven = motif_stage(0, [v2[a][0] for a in range(PASSES)])
         anchor_stage(0, 256)
+        quantise_c(0, c_woven)
+        c_woven = motif_stage(1, [v2[a][1] for a in range(PASSES)])
+        anchor_stage(256, 256)
+        quantise_c(1, c_woven)
         j0 = 0
         for width in CHUNKS:
-            if j0 + 256 < S and j0 % 256 == 0:
-                anchor_stage(j0 + 256, 256)
-            loop = [loop_stage(j0, width, h) for h in range(2)]
+            woven = [loop_stage(j0, width, h) for h in range(2)]
+            if j0 == 0:
+                anchor_stage(HALF, HALF)
+            loop = [loop_quantise(j0, width, h, woven[h]) for h in range(2)]
             read_back(j0, width, loop)
             j0 = j0 + width

@@ -30,9 +30,18 @@ def tile_list_chromatin_loop_map_kernel(
     with ExitStack() as ctx:
         keep = ctx.enter_context(tc.tile_pool(name="keep", bufs=1))
         ring = ctx.enter_context(tc.tile_pool(name="ring", bufs=3))
-        pair = ctx.enter_context(tc.tile_pool(name="pair", bufs=2))
-        psum = ctx.enter_context(tc.psum_pool(name="psum", bufs=6))
-        psum_y = ctx.enter_context(tc.psum_pool(name="psum_y", bufs=2))
+        psum = ctx.enter_context(tc.psum_pool(name="psum", bufs=1))
+
+        def take_bank(n):
+            return psum.tile([P, 512], F32, name="bank%d" % n)
+
+        streamed = []
+
+        def stream_banks(count):
+            order = [6, 7, 4, 5, 2, 3]
+            numbers = [order[(len(streamed) + n) % len(order)] for n in range(count)]
+            streamed.extend(numbers)
+            return numbers
 
         def held(name, shape, dtype):
             return keep.tile(shape, dtype, name=name, align_bytes=64)
@@ -59,7 +68,6 @@ def tile_list_chromatin_loop_map_kernel(
         words2 = [held("words2_%d" % a, [P, T], I32) for a in range(PASSES)]
         words1 = [held("words1_%d" % a, [P, T], I32) for a in range(PASSES)]
         wm_raw = held("wm_raw", [P, PASSES, 2 * H], U8)
-        gains = held("gains", [P, 4], F32)
 
         def load_words(tile, table, a):
             nc.sync.dma_start(tile[:], table[a].rearrange("p t i -> p (t i)").bitcast(I32))
@@ -90,6 +98,7 @@ def tile_list_chromatin_loop_map_kernel(
         load_words(words2[1], tab2_words, 1)
         load_vector(0, dwell)
         load_vector(4, occ)
+        nc.sync.dma_start(rows[8:12, 0:P], gain.rearrange("(r p) -> r p", p=P))
         load_words(words1[0], tab_words, 0)
         nc.sync.dma_start(wm_raw[:].bitcast(I32), wm_words.rearrange("a p c -> p a c").bitcast(I32))
         for d in range(4):
@@ -98,8 +107,6 @@ def tile_list_chromatin_loop_map_kernel(
                 wm_scales[:, 4 * d : 4 * d + 4, :].rearrange("a i c -> i a c").bitcast(I32),
             )
         load_words(words1[1], tab_words, 1)
-        with nc.allow_non_contiguous_dma(reason="one gain for each partition and tile of output rows"):
-            nc.sync.dma_start(gains[:], gain.rearrange("(r p) -> p r", p=P))
 
         picked2 = held("picked2", [P, S], U8)
         nc.vector.tensor_copy(picked2[:], win2[:].indirect(list2[:]))
@@ -128,11 +135,12 @@ def tile_list_chromatin_loop_map_kernel(
                 in_=woven[:].rearrange("p c i -> p (c i)"),
             )
 
-        vec_bank = psum_y.tile([P, 512], F32, name="ybank")
+        vec_bank = take_bank(7)
         for h in range(2):
             nc.tensor.transpose(vec_bank[:, P * h : P * (h + 1)], rows[:, P * h : P * (h + 1)], ident[:])
-        vecs = held("vecs", [P, 2, 8], F32)
-        nc.scalar.copy(vecs[:], vec_bank[:, 0 : 2 * P].rearrange("p (h c) -> p h c", h=2)[:, :, 0:8])
+        vecs = held("vecs", [P, 2, 12], F32)
+        nc.scalar.copy(vecs[:], vec_bank[:, 0 : 2 * P].rearrange("p (h c) -> p h c", h=2)[:, :, 0:12])
+        gains = vecs[:, 0, 8:12]
 
         wm_codes = held("wm_codes", [P, PASSES * 2 * H], U8)
         nc.vector.tensor_copy(
@@ -151,7 +159,7 @@ def tile_list_chromatin_loop_map_kernel(
         c_scales = held("c_scales", [P, 2 * H], U8)
 
         def motif_gather(a, h):
-            v2 = pair.tile([P, HALF], U32, name="picked%d" % a, align_bytes=64)
+            v2 = held("picked%d_%d" % (a, h), [P, HALF], U32)
             nc.vector.tensor_copy(
                 v2[:].rearrange("p (t i s) -> p i t s", t=4, s=8),
                 words2[a][:].bitcast(U32).indirect(list2[:, 32 * h : 32 * (h + 1)]),
@@ -161,7 +169,7 @@ def tile_list_chromatin_loop_map_kernel(
         def motif_stage(h, v2):
             bt = held("bt%d" % h, [P, 4, 2, 256], BF16)
             c_woven = held("c_woven%d" % h, [P, H, 4], BF16)
-            banks = [psum.tile([P, 512], F32, name="bank") for r in range(4)]
+            banks = [take_bank(4 * h + r) for r in range(4)]
 
             def passes(a, r):
                 for t in range(4):
@@ -185,22 +193,24 @@ def tile_list_chromatin_loop_map_kernel(
                     bank[:].rearrange("p (t i u e s) -> p t i u s e", t=4, i=4, u=2, e=2),
                 )
                 nc.vector.tensor_tensor(
-                    c_woven[:, P * r : P * (r + 1), :],
-                    bank[:].rearrange("p (t c) -> p c t", t=4),
-                    vecs[:, h : h + 1, 0:4].to_broadcast([P, P, 4]),
+                    c_woven[:, P * r : P * (r + 1), :].rearrange("p (c n) t -> p c t n", n=2),
+                    bank[:].rearrange("p (t c n) -> p c t n", t=4, n=2),
+                    vecs[:, h : h + 1, 0:4].unsqueeze(3).to_broadcast([P, P // 2, 4, 2]),
                     MULT,
                 )
             b_woven = held("b_woven%d" % h, [P, HALF * 4], BF16)
             pairs = bt[:].bitcast(F32)
             for half in range(2):
-                bank = psum.tile([P, 512], F32, name="bank")
+                bank = take_bank(4 * h + half)
                 for t in range(2):
                     for u in range(2):
                         col = P * (2 * t + u)
                         nc.tensor.transpose(bank[:, col : col + P], pairs[:, 2 * half + t, u, :], ident[:])
                 nc.scalar.copy(
-                    b_woven[:, 1024 * half : 1024 * (half + 1)].bitcast(F32).rearrange("p (t m u) -> p t m u", t=2, u=2),
-                    bank[:].rearrange("p (t u m) -> p t m u", t=2, u=2),
+                    b_woven[:, 1024 * half : 1024 * (half + 1)].bitcast(F32).rearrange(
+                        "p (t m n u) -> p t m u n", t=2, n=2, u=2
+                    ),
+                    bank[:].rearrange("p (t u m n) -> p t m u n", t=2, u=2, n=2),
                 )
             nc.vector.quantize_mx(
                 out=b_codes[:, HALF * h : HALF * (h + 1)].bitcast(FP8X4),
@@ -219,29 +229,37 @@ def tile_list_chromatin_loop_map_kernel(
         h_codes = held("h_codes", [P, S], U32)
         h_scales = held("h_scales", [P, S], U8)
 
-        def anchor_stage(j0, width):
+        def anchor_stage(chunk, bank_numbers):
+            width = 256
+            j0 = width * chunk
             v1 = []
             for a in range(PASSES):
-                picked = pair.tile([P, width], U32, name="picked%d" % a, align_bytes=64)
+                slot = "picked%d_%d" % (a, chunk) if chunk < 2 else "reused%d" % a
+                picked = held(slot, [P, width], U32)
                 nc.vector.tensor_copy(
                     picked[:], words1[a][:].bitcast(U32).indirect(lists[:, j0 // 16 : (j0 + width) // 16])
                 )
                 v1.append(picked)
-            h_woven = pair.tile([P, width, 4], BF16, name="h_woven", align_bytes=64)
-            for j in range(0, width, P):
-                bank = psum.tile([P, 512], F32, name="bank")
-                for t in range(4):
-                    for a in range(PASSES):
+            h_woven = held("reused%d" % chunk if chunk < 2 else "h_woven%d" % chunk, [P, width, 4], BF16)
+            banks = [take_bank(number) for number in bank_numbers]
+            for a in range(PASSES):
+                for n, bank in enumerate(banks):
+                    j = P * n
+                    for t in range(4):
                         nc.tensor.matmul_mx(
                             out=bank[:, P * t : P * (t + 1)],
                             lhsT=wm_codes[:, 2 * (H * a + P * t) : 2 * (H * a + P * (t + 1))].bitcast(FP4X4),
                             lhsT_scale=wm_planes[:, H * a + P * t : H * a + P * (t + 1)],
                             rhs=v1[a][:, j : j + P].bitcast(FP8X4),
                             rhs_scale=planes1[:, S * a + j0 + j : S * a + j0 + j + P],
-                            start=(a == 0),
-                            stop=(a == PASSES - 1),
+                            start=(a == 0 and t == 0),
+                            stop=(a == PASSES - 1 and t == 3),
                         )
-                nc.scalar.copy(h_woven[:, j : j + P, :], bank[:].rearrange("p (t c) -> p c t", t=4))
+            for n, bank in enumerate(banks):
+                nc.scalar.copy(
+                    h_woven[:, P * n : P * (n + 1), :].rearrange("p (c n) t -> p c t n", n=2),
+                    bank[:].rearrange("p (t c n) -> p c t n", t=4, n=2),
+                )
             nc.vector.quantize_mx(
                 out=h_codes[:, j0 : j0 + width].bitcast(FP8X4),
                 scales=h_scales[:, j0 : j0 + width],
@@ -249,9 +267,9 @@ def tile_list_chromatin_loop_map_kernel(
             )
 
         def loop_stage(j0, width, h):
-            sig = ring.tile([P, width, 4], F32, name="sig", align_bytes=64, bufs=8)
-            for j in range(0, width, P):
-                bank = psum.tile([P, 512], F32, name="bank")
+            sig = ring.tile([P, width // 2, 4, 2], F32, name="sig", align_bytes=64, bufs=8)
+            for j, number in zip(range(0, width, P), stream_banks(width // P)):
+                bank = take_bank(number)
                 for t in range(4):
                     cols = slice(HALF * h + P * t, HALF * h + P * (t + 1))
                     nc.tensor.matmul_mx(
@@ -263,9 +281,16 @@ def tile_list_chromatin_loop_map_kernel(
                         start=True,
                         stop=True,
                     )
-                nc.scalar.activation(sig[:, j : j + P, :], bank[:].rearrange("p (t c) -> p c t", t=4), ACT.Sigmoid)
+                nc.scalar.activation(
+                    sig[:, j // 2 : (j + P) // 2, :, :], bank[:].rearrange("p (t c n) -> p c t n", t=4, n=2), ACT.Sigmoid
+                )
             woven = ring.tile([P, width, 4], BF16, name="loop_woven", align_bytes=64)
-            nc.vector.tensor_tensor(woven[:], sig[:], vecs[:, h : h + 1, 4:8].to_broadcast([P, width, 4]), MULT)
+            nc.vector.tensor_tensor(
+                woven[:].rearrange("p (c n) t -> p c t n", n=2),
+                sig[:],
+                vecs[:, h : h + 1, 4:8].unsqueeze(3).to_broadcast([P, width // 2, 4, 2]),
+                MULT,
+            )
             return woven
 
         def loop_quantise(j0, width, h, woven):
@@ -278,20 +303,20 @@ def tile_list_chromatin_loop_map_kernel(
 
         def read_back(j0, width, loop):
             last = j0 + width == S
+            banks = [take_bank(number) for number in (stream_banks(2) if last else [0, 1])]
+            for h in range(2):
+                for r in range(4):
+                    nc.tensor.matmul_mx(
+                        out=banks[r // 2][:, width * (r % 2) : width * (r % 2 + 1)],
+                        lhsT=c_codes[:, H * h + P * r : H * h + P * (r + 1)].bitcast(FP8X4),
+                        lhsT_scale=c_scales[:, H * h + P * r : H * h + P * (r + 1)],
+                        rhs=loop[h][0][:].bitcast(FP8X4),
+                        rhs_scale=loop[h][1][:],
+                        start=(h == 0 and r % 2 == 0),
+                        stop=(h == 1 and r % 2 == 1),
+                    )
             for r0 in (0, 2):
-                bank = psum_y.tile([P, 512], F32, name="ybank")
-                for h in range(2):
-                    for r in range(2):
-                        cols = slice(H * h + P * (r0 + r), H * h + P * (r0 + r + 1))
-                        nc.tensor.matmul_mx(
-                            out=bank[:, width * r : width * (r + 1)],
-                            lhsT=c_codes[:, cols].bitcast(FP8X4),
-                            lhsT_scale=c_scales[:, cols],
-                            rhs=loop[h][0][:].bitcast(FP8X4),
-                            rhs_scale=loop[h][1][:],
-                            start=(h == 0 and r == 0),
-                            stop=(h == 1 and r == 1),
-                        )
+                bank = banks[r0 // 2]
                 result = ring.tile([P, 2, width], F32, name="result", align_bytes=64, bufs=6)
                 if last and r0 == 0:
                     nc.vector.tensor_tensor(
@@ -314,16 +339,16 @@ def tile_list_chromatin_loop_map_kernel(
 
         v2 = [[motif_gather(a, h) for h in range(2)] for a in range(PASSES)]
         c_woven = motif_stage(0, [v2[a][0] for a in range(PASSES)])
-        anchor_stage(0, 256)
+        anchor_stage(0, [2, 3])
         quantise_c(0, c_woven)
         c_woven = motif_stage(1, [v2[a][1] for a in range(PASSES)])
-        anchor_stage(256, 256)
+        anchor_stage(1, [0, 1])
         quantise_c(1, c_woven)
         j0 = 0
         for width in CHUNKS:
             woven = [loop_stage(j0, width, h) for h in range(2)]
-            if j0 == 0:
-                anchor_stage(HALF, HALF)
+            if j0 < HALF:
+                anchor_stage(2 + j0 // 256, stream_banks(2))
             loop = [loop_quantise(j0, width, h, woven[h]) for h in range(2)]
             read_back(j0, width, loop)
             j0 = j0 + width

@@ -38,7 +38,7 @@ def tile_list_chromatin_loop_map_kernel(
         streamed = []
 
         def stream_banks(count):
-            order = [6, 7, 4, 5, 2, 3]
+            order = [2, 3, 6, 7, 4, 5]
             numbers = [order[(len(streamed) + n) % len(order)] for n in range(count)]
             streamed.extend(numbers)
             return numbers
@@ -55,17 +55,16 @@ def tile_list_chromatin_loop_map_kernel(
         rows = held("rows", [P, 2 * P], F32)
         ident = held("ident", [P, P], F32)
 
-        nc.gpsimd.memset(win2[:].bitcast(I32), 0)
-        nc.vector.memset(win1[:].bitcast(I32), 0)
-        nc.vector.memset(rows[:], 0.0)
+        nc.gpsimd.memset(win1[:].bitcast(I32), 0)
         nc.vector.memset(wms_raw[:].bitcast(I32), 0)
+        nc.vector.memset(rows[:], 0.0)
+        nc.vector.memset(win2[:].bitcast(I32), 0)
         nc.vector.memset(planes1[:].bitcast(I32), 0)
         make_identity(nc, ident[:])
         warm = held("warm", [P, 1], F32)
-        nc.scalar.activation(warm[:], ident[:, 0:1], ACT.Sigmoid)
+        nc.scalar.activation(warm[32:64, :], rows[32:64, 0:1], ACT.Sigmoid)
 
-        wb_raw = [held("wb_raw%d" % a, [P, 4, H], F32) for a in range(PASSES)]
-        words2 = [held("words2_%d" % a, [P, T], I32) for a in range(PASSES)]
+        wb_raw = [held("wb_raw0", [P, 4, H], F32)]
         words1 = [held("words1_%d" % a, [P, T], I32) for a in range(PASSES)]
         wm_raw = held("wm_raw", [P, PASSES, 2 * H], U8)
 
@@ -73,7 +72,7 @@ def tile_list_chromatin_loop_map_kernel(
             nc.sync.dma_start(tile[:], table[a].rearrange("p t i -> p (t i)").bitcast(I32))
 
         def load_vector(first, vec):
-            nc.sync.dma_start(
+            nc.gpsimd.dma_start(
                 rows[first : first + 4, :].rearrange("t (g s) -> t g s", s=8),
                 vec.rearrange("(g t s) -> t g s", t=4, s=8),
             )
@@ -81,24 +80,12 @@ def tile_list_chromatin_loop_map_kernel(
         def load_wb(a):
             nc.sync.dma_start(wb_raw[a][:], wb[HALF * a : HALF * (a + 1), :].rearrange("(p i) c -> p i c", i=4))
 
-        nc.sync.dma_start(list2[:], offs2)
-        nc.sync.dma_start(lists[:], offs)
-        for d in range(4):
-            nc.sync.dma_start(
-                win2[32 * d : 32 * d + 8, :].bitcast(I32), tab2_scales[:, 4 * d : 4 * d + 4, :].bitcast(I32)
-            )
-        load_words(words2[0], tab2_words, 0)
-        load_wb(0)
-        for d in range(4):
-            nc.sync.dma_start(
-                win1[32 * d + 12 : 32 * d + 20, :].bitcast(I32),
-                tab_scales[:, 4 * d : 4 * d + 4, :].rearrange("a i t -> i a t").bitcast(I32),
-            )
-        load_wb(1)
-        load_words(words2[1], tab2_words, 1)
         load_vector(0, dwell)
         load_vector(4, occ)
-        nc.sync.dma_start(rows[8:12, 0:P], gain.rearrange("(r p) -> r p", p=P))
+        nc.gpsimd.dma_start(rows[8:12, 0:P], gain.rearrange("(r p) -> r p", p=P))
+        nc.sync.dma_start(lists[:], offs)
+        nc.sync.dma_start(list2[:], offs2)
+        nc.sync.dma_start(win1[0:P:4, :].bitcast(I32), tab_scales.rearrange("a q t -> q a t").bitcast(I32))
         load_words(words1[0], tab_words, 0)
         nc.sync.dma_start(wm_raw[:].bitcast(I32), wm_words.rearrange("a p c -> p a c").bitcast(I32))
         for d in range(4):
@@ -106,41 +93,53 @@ def tile_list_chromatin_loop_map_kernel(
                 wms_raw[32 * d : 32 * d + 4, :].bitcast(I32).rearrange("i (a c) -> i a c", a=PASSES),
                 wm_scales[:, 4 * d : 4 * d + 4, :].rearrange("a i c -> i a c").bitcast(I32),
             )
+        load_wb(0)
+        for d in range(4):
+            nc.sync.dma_start(
+                win2[32 * d : 32 * d + 8, :].bitcast(I32), tab2_scales[:, 4 * d : 4 * d + 4, :].bitcast(I32)
+            )
         load_words(words1[1], tab_words, 1)
 
-        picked2 = held("picked2", [P, S], U8)
-        nc.vector.tensor_copy(picked2[:], win2[:].indirect(list2[:]))
-        planes2 = held("planes2", [P, S], U8)
-        nc.vector.tensor_copy(
-            planes2[:].bitcast(I32).rearrange("p (h t i w) -> p h t i w", h=2, t=4, w=2),
-            picked2[:].bitcast(I32).rearrange("p (h i t w) -> p h t i w", h=2, t=4, w=2),
-        )
         picked1 = held("picked1", [P, S], U8)
         nc.vector.tensor_copy(picked1[:], win1[:].indirect(lists[:]))
         for d in range(4):
             nc.sync.dma_start(
-                planes1[32 * d : 32 * d + 4, :].bitcast(I32), picked1[32 * d + 12 : 32 * d + 20, :].bitcast(I32)
+                planes1[32 * d : 32 * d + 4, :].bitcast(I32), picked1[32 * d : 32 * d + 32 : 4, :].bitcast(I32)
+            )
+        wb_raw.append(held("win1", [P, 4, H], F32))
+        load_wb(1)
+
+        first_pass = held("anchors0", [P, S], U32)
+        nc.vector.tensor_copy(first_pass[:], words1[0][:].bitcast(U32).indirect(lists[:]))
+        words2 = [held("words1_0", [P, T], I32)]
+        load_words(words2[0], tab2_words, 0)
+
+        wb_codes = []
+        wb_scales = held("wb_scales", [P, PASSES * H], U8)
+        wb_woven = [held("wb_woven%d" % a, [P, H * 4], BF16) for a in range(PASSES)]
+        for a in range(PASSES):
+            nc.scalar.copy(
+                wb_woven[a][:].rearrange("p (c n i) -> p c i n", n=4, i=4),
+                wb_raw[a][:].rearrange("p i (c n) -> p c i n", n=4),
+            )
+        words2.append(held("wb_raw0", [P, T], I32))
+        load_words(words2[1], tab2_words, 1)
+
+        def quantise_wb(a, slot):
+            wb_codes.append(held(slot, [P, H], U32))
+            nc.vector.quantize_mx(
+                out=wb_codes[a][:].bitcast(FP8X4),
+                scales=wb_scales[:, H * a : H * (a + 1)],
+                in_=wb_woven[a][:],
             )
 
-        wb_codes = held("wb_codes", [P, PASSES * H], U32)
-        wb_scales = held("wb_scales", [P, PASSES * H], U8)
-        for a in range(PASSES):
-            woven = held("wb_woven%d" % a, [P, H, 4], BF16)
-            nc.scalar.copy(
-                woven[:].rearrange("p (c n) i -> p c i n", n=4), wb_raw[a][:].rearrange("p i (c n) -> p c i n", n=4)
-            )
-            nc.vector.quantize_mx(
-                out=wb_codes[:, H * a : H * (a + 1)].bitcast(FP8X4),
-                scales=wb_scales[:, H * a : H * (a + 1)],
-                in_=woven[:].rearrange("p c i -> p (c i)"),
-            )
+        vecs = held("vecs", [P, 2, 12], F32)
+        gains = vecs[:, 0, 8:12]
 
         vec_bank = take_bank(7)
         for h in range(2):
             nc.tensor.transpose(vec_bank[:, P * h : P * (h + 1)], rows[:, P * h : P * (h + 1)], ident[:])
-        vecs = held("vecs", [P, 2, 12], F32)
         nc.scalar.copy(vecs[:], vec_bank[:, 0 : 2 * P].rearrange("p (h c) -> p h c", h=2)[:, :, 0:12])
-        gains = vecs[:, 0, 8:12]
 
         wm_codes = held("wm_codes", [P, PASSES * 2 * H], U8)
         nc.vector.tensor_copy(
@@ -152,6 +151,16 @@ def tile_list_chromatin_loop_map_kernel(
             wm_planes[:].bitcast(I32).rearrange("p (a t i w) -> p a t i w", a=PASSES, t=4, w=2),
             wms_raw[:].bitcast(I32).rearrange("p (a i t w) -> p a t i w", a=PASSES, t=4, w=2),
         )
+
+        picked2 = held("picked2", [P, S], U8)
+        nc.vector.tensor_copy(picked2[:], win2[:].indirect(list2[:]))
+        planes2 = held("planes2", [P, S], U8)
+        nc.vector.tensor_copy(
+            planes2[:].bitcast(I32).rearrange("p (h t i w) -> p h t i w", h=2, t=4, w=2),
+            picked2[:].bitcast(I32).rearrange("p (h i t w) -> p h t i w", h=2, t=4, w=2),
+        )
+
+        quantise_wb(0, "win2")
 
         b_codes = held("b_codes", [P, S], U32)
         b_scales = held("b_scales", [P, S], U8)
@@ -166,10 +175,10 @@ def tile_list_chromatin_loop_map_kernel(
             )
             return v2
 
-        def motif_stage(h, v2):
+        def motif_stage(h, v2, product_banks, turn_banks):
             bt = held("bt%d" % h, [P, 4, 2, 256], BF16)
             c_woven = held("c_woven%d" % h, [P, H, 4], BF16)
-            banks = [take_bank(4 * h + r) for r in range(4)]
+            banks = [take_bank(number) for number in product_banks]
 
             def passes(a, r):
                 for t in range(4):
@@ -177,7 +186,7 @@ def tile_list_chromatin_loop_map_kernel(
                         out=banks[r][:, P * t : P * (t + 1)],
                         lhsT=v2[a][:, P * t : P * (t + 1)].bitcast(FP8X4),
                         lhsT_scale=planes2[4 * a :, HALF * h + P * t : HALF * h + P * (t + 1)],
-                        rhs=wb_codes[:, H * a + P * r : H * a + P * (r + 1)].bitcast(FP8X4),
+                        rhs=wb_codes[a][:, P * r : P * (r + 1)].bitcast(FP8X4),
                         rhs_scale=wb_scales[:, H * a + P * r : H * a + P * (r + 1)],
                         start=(a == 0 and t == 0),
                         stop=(a == PASSES - 1 and t == 3),
@@ -201,7 +210,7 @@ def tile_list_chromatin_loop_map_kernel(
             b_woven = held("b_woven%d" % h, [P, HALF * 4], BF16)
             pairs = bt[:].bitcast(F32)
             for half in range(2):
-                bank = take_bank(4 * h + half)
+                bank = take_bank(turn_banks[half])
                 for t in range(2):
                     for u in range(2):
                         col = P * (2 * t + u)
@@ -226,21 +235,19 @@ def tile_list_chromatin_loop_map_kernel(
                 in_=c_woven[:].rearrange("p c t -> p (c t)"),
             )
 
-        h_codes = held("h_codes", [P, S], U32)
+        h_codes = []
+        h_woven = [held("win1", [P, HALF, 4], BF16), held("h_woven1", [P, HALF, 4], BF16)]
         h_scales = held("h_scales", [P, S], U8)
 
-        def anchor_stage(chunk, bank_numbers):
+        def anchor_stage(chunk, first_pass, bank_numbers):
             width = 256
             j0 = width * chunk
-            v1 = []
-            for a in range(PASSES):
-                slot = "picked%d_%d" % (a, chunk) if chunk < 2 else "reused%d" % a
-                picked = held(slot, [P, width], U32)
-                nc.vector.tensor_copy(
-                    picked[:], words1[a][:].bitcast(U32).indirect(lists[:, j0 // 16 : (j0 + width) // 16])
-                )
-                v1.append(picked)
-            h_woven = held("reused%d" % chunk if chunk < 2 else "h_woven%d" % chunk, [P, width, 4], BF16)
+            picked = held("anchors1_%d" % chunk, [P, width], U32)
+            nc.vector.tensor_copy(
+                picked[:], words1[1][:].bitcast(U32).indirect(lists[:, j0 // 16 : (j0 + width) // 16])
+            )
+            v1 = [first_pass[:, j0 : j0 + width], picked[:]]
+            woven = h_woven[j0 // HALF][:, j0 % HALF : j0 % HALF + width, :]
             banks = [take_bank(number) for number in bank_numbers]
             for a in range(PASSES):
                 for n, bank in enumerate(banks):
@@ -257,17 +264,21 @@ def tile_list_chromatin_loop_map_kernel(
                         )
             for n, bank in enumerate(banks):
                 nc.scalar.copy(
-                    h_woven[:, P * n : P * (n + 1), :].rearrange("p (c n) t -> p c t n", n=2),
+                    woven[:, P * n : P * (n + 1), :].rearrange("p (c n) t -> p c t n", n=2),
                     bank[:].rearrange("p (t c n) -> p c t n", t=4, n=2),
                 )
+
+        def quantise_h(half, slot):
+            codes = held(slot, [P, HALF], U32)
             nc.vector.quantize_mx(
-                out=h_codes[:, j0 : j0 + width].bitcast(FP8X4),
-                scales=h_scales[:, j0 : j0 + width],
-                in_=h_woven[:].rearrange("p c t -> p (c t)"),
+                out=codes[:].bitcast(FP8X4),
+                scales=h_scales[:, HALF * half : HALF * (half + 1)],
+                in_=h_woven[half][:].rearrange("p c t -> p (c t)"),
             )
+            h_codes.append(codes)
 
         def loop_stage(j0, width, h):
-            sig = ring.tile([P, width // 2, 4, 2], F32, name="sig", align_bytes=64, bufs=8)
+            sig = ring.tile([P, width, 4], F32, name="sig", align_bytes=64, bufs=8)
             for j, number in zip(range(0, width, P), stream_banks(width // P)):
                 bank = take_bank(number)
                 for t in range(4):
@@ -276,20 +287,19 @@ def tile_list_chromatin_loop_map_kernel(
                         out=bank[:, P * t : P * (t + 1)],
                         lhsT=b_codes[:, cols].bitcast(FP8X4),
                         lhsT_scale=b_scales[:, cols],
-                        rhs=h_codes[:, j0 + j : j0 + j + P].bitcast(FP8X4),
+                        rhs=h_codes[j0 // HALF][:, j0 % HALF + j : j0 % HALF + j + P].bitcast(FP8X4),
                         rhs_scale=h_scales[:, j0 + j : j0 + j + P],
                         start=True,
                         stop=True,
                     )
                 nc.scalar.activation(
-                    sig[:, j // 2 : (j + P) // 2, :, :], bank[:].rearrange("p (t c n) -> p c t n", t=4, n=2), ACT.Sigmoid
+                    sig[:, j : j + P, :].rearrange("p (c n) t -> p c t n", n=2),
+                    bank[:].rearrange("p (t c n) -> p c t n", t=4, n=2),
+                    ACT.Sigmoid,
                 )
             woven = ring.tile([P, width, 4], BF16, name="loop_woven", align_bytes=64)
             nc.vector.tensor_tensor(
-                woven[:].rearrange("p (c n) t -> p c t n", n=2),
-                sig[:],
-                vecs[:, h : h + 1, 4:8].unsqueeze(3).to_broadcast([P, width // 2, 4, 2]),
-                MULT,
+                woven[:], sig[:], vecs[:, h : h + 1, 4:8].to_broadcast([P, width, 4]), MULT
             )
             return woven
 
@@ -337,18 +347,22 @@ def tile_list_chromatin_loop_map_kernel(
                     out.rearrange("(r p) j -> p r j", p=P)[:, r0 : r0 + 2, j0 : j0 + width], result[:]
                 )
 
-        v2 = [[motif_gather(a, h) for h in range(2)] for a in range(PASSES)]
-        c_woven = motif_stage(0, [v2[a][0] for a in range(PASSES)])
-        anchor_stage(0, [2, 3])
-        quantise_c(0, c_woven)
-        c_woven = motif_stage(1, [v2[a][1] for a in range(PASSES)])
-        anchor_stage(1, [0, 1])
-        quantise_c(1, c_woven)
+        for chunk in range(4):
+            anchor_stage(chunk, first_pass, [2 * chunk, 2 * chunk + 1])
+        v2 = [[motif_gather(0, h) for h in range(2)]]
+        quantise_wb(1, "wb_codes1")
+        quantise_h(0, "words1_0")
+        v2.append([motif_gather(1, h) for h in range(2)])
+        quantise_h(1, "wb_raw0")
+        c_woven = [
+            motif_stage(0, [v2[a][0] for a in range(PASSES)], [0, 1, 2, 3], [0, 1]),
+            motif_stage(1, [v2[a][1] for a in range(PASSES)], [4, 5, 6, 7], [4, 5]),
+        ]
+        for h in range(2):
+            quantise_c(h, c_woven[h])
         j0 = 0
         for width in CHUNKS:
             woven = [loop_stage(j0, width, h) for h in range(2)]
-            if j0 < HALF:
-                anchor_stage(2 + j0 // 256, stream_banks(2))
             loop = [loop_quantise(j0, width, h, woven[h]) for h in range(2)]
             read_back(j0, width, loop)
             j0 = j0 + width

@@ -202,9 +202,9 @@ def tile_list_chromatin_loop_map_kernel(
                     bank[:].rearrange("p (t i u e s) -> p t i u s e", t=4, i=4, u=2, e=2),
                 )
                 nc.vector.tensor_tensor(
-                    c_woven[:, P * r : P * (r + 1), :].rearrange("p (c n) t -> p c t n", n=2),
-                    bank[:].rearrange("p (t c n) -> p c t n", t=4, n=2),
-                    vecs[:, h : h + 1, 0:4].unsqueeze(3).to_broadcast([P, P // 2, 4, 2]),
+                    c_woven[:, P * r : P * (r + 1), :],
+                    bank[:].rearrange("p (t c) -> p c t", t=4),
+                    vecs[:, h : h + 1, 0:4].to_broadcast([P, P, 4]),
                     MULT,
                 )
             b_woven = held("b_woven%d" % h, [P, HALF * 4], BF16)
@@ -216,10 +216,8 @@ def tile_list_chromatin_loop_map_kernel(
                         col = P * (2 * t + u)
                         nc.tensor.transpose(bank[:, col : col + P], pairs[:, 2 * half + t, u, :], ident[:])
                 nc.scalar.copy(
-                    b_woven[:, 1024 * half : 1024 * (half + 1)].bitcast(F32).rearrange(
-                        "p (t m n u) -> p t m u n", t=2, n=2, u=2
-                    ),
-                    bank[:].rearrange("p (t u m n) -> p t m u n", t=2, u=2, n=2),
+                    b_woven[:, 1024 * half : 1024 * (half + 1)].bitcast(F32).rearrange("p (t m u) -> p t m u", t=2, u=2),
+                    bank[:].rearrange("p (t u m) -> p t m u", t=2, u=2),
                 )
             nc.vector.quantize_mx(
                 out=b_codes[:, HALF * h : HALF * (h + 1)].bitcast(FP8X4),
@@ -264,8 +262,7 @@ def tile_list_chromatin_loop_map_kernel(
                         )
             for n, bank in enumerate(banks):
                 nc.scalar.copy(
-                    woven[:, P * n : P * (n + 1), :].rearrange("p (c n) t -> p c t n", n=2),
-                    bank[:].rearrange("p (t c n) -> p c t n", t=4, n=2),
+                    woven[:, P * n : P * (n + 1), :], bank[:].rearrange("p (t c) -> p c t", t=4)
                 )
 
         def quantise_h(half, slot):
@@ -293,9 +290,7 @@ def tile_list_chromatin_loop_map_kernel(
                         stop=True,
                     )
                 nc.scalar.activation(
-                    sig[:, j : j + P, :].rearrange("p (c n) t -> p c t n", n=2),
-                    bank[:].rearrange("p (t c n) -> p c t n", t=4, n=2),
-                    ACT.Sigmoid,
+                    sig[:, j : j + P, :], bank[:].rearrange("p (t c) -> p c t", t=4), ACT.Sigmoid
                 )
             woven = ring.tile([P, width, 4], BF16, name="loop_woven", align_bytes=64)
             nc.vector.tensor_tensor(

@@ -20,6 +20,7 @@ MULT = mybir.AluOpType.mult
 P = 128
 PASSES = 2
 HALF = 512
+ANCHORS = 256
 CHUNKS = [256, 256, 256, 128, 128]
 
 
@@ -38,8 +39,7 @@ def tile_list_chromatin_loop_map_kernel(
         streamed = []
 
         def stream_banks(count):
-            order = [2, 3, 6, 7, 4, 5]
-            numbers = [order[(len(streamed) + n) % len(order)] for n in range(count)]
+            numbers = [(len(streamed) + n) % 6 for n in range(count)]
             streamed.extend(numbers)
             return numbers
 
@@ -51,228 +51,202 @@ def tile_list_chromatin_loop_map_kernel(
         win1 = held("win1", [P, T], U8)
         win2 = held("win2", [P, T], U8)
         planes1 = held("planes1", [P, PASSES * S], U8)
+        planes2 = held("planes2", [P, PASSES * S], U8)
         wms_raw = held("wms_raw", [P, PASSES * H], U8)
-        rows = held("rows", [P, 2 * P], F32)
         ident = held("ident", [P, P], F32)
+        dwell_rows = held("dwell_rows", [P, 8], F32)
 
+        warm = held("warm", [P, 2], F32)
         nc.gpsimd.memset(win1[:].bitcast(I32), 0)
-        nc.vector.memset(wms_raw[:].bitcast(I32), 0)
-        nc.vector.memset(rows[:], 0.0)
+        nc.vector.memset(warm[:, 0:1], 0.0)
         nc.vector.memset(win2[:].bitcast(I32), 0)
+        nc.vector.memset(wms_raw[:].bitcast(I32), 0)
         nc.vector.memset(planes1[:].bitcast(I32), 0)
+        nc.vector.memset(planes2[:].bitcast(I32), 0)
+        nc.scalar.activation(warm[:, 1:2], warm[:, 0:1], ACT.Sigmoid)
+
+        def load_words(slot, table, a):
+            words = held(slot, [P, T], I32)
+            nc.sync.dma_start(words[:], table[a].rearrange("p t i -> p (t i)").bitcast(I32))
+            return words
+
+        def load_wb(slot, a):
+            raw = held(slot, [P, 4, H], F32)
+            nc.sync.dma_start(raw[:], wb[HALF * a : HALF * (a + 1), :].rearrange("(p i) c -> p i c", i=4))
+            return raw
+
+        def load_scale_rows(window, scales):
+            nc.sync.dma_start(window[0:P:4, :].bitcast(I32), scales.rearrange("a q t -> q a t").bitcast(I32))
+
+        def gather_scales(name, window, offsets, planes):
+            picked = held(name, [P, S], U8)
+            nc.vector.tensor_copy(picked[:], window[:].indirect(offsets[:]))
+            for d in range(4):
+                nc.sync.dma_start(
+                    planes[32 * d : 32 * d + 4, :].bitcast(I32), picked[32 * d : 32 * d + 32 : 4, :].bitcast(I32)
+                )
+
+        nc.gpsimd.dma_start(dwell_rows[:], dwell.rearrange("(n c) -> n c", c=8))
+        occs = held("occs", [P, 2, 4], F32)
+        gains = held("gains", [P, 4], F32)
         make_identity(nc, ident[:])
-        warm = held("warm", [P, 1], F32)
-        nc.scalar.activation(warm[32:64, :], rows[32:64, 0:1], ACT.Sigmoid)
-
-        wb_raw = [held("wb_raw0", [P, 4, H], F32)]
-        words1 = [held("words1_%d" % a, [P, T], I32) for a in range(PASSES)]
-        wm_raw = held("wm_raw", [P, PASSES, 2 * H], U8)
-
-        def load_words(tile, table, a):
-            nc.sync.dma_start(tile[:], table[a].rearrange("p t i -> p (t i)").bitcast(I32))
-
-        def load_vector(first, vec):
-            nc.gpsimd.dma_start(
-                rows[first : first + 4, :].rearrange("t (g s) -> t g s", s=8),
-                vec.rearrange("(g t s) -> t g s", t=4, s=8),
-            )
-
-        def load_wb(a):
-            nc.sync.dma_start(wb_raw[a][:], wb[HALF * a : HALF * (a + 1), :].rearrange("(p i) c -> p i c", i=4))
-
-        load_vector(0, dwell)
-        load_vector(4, occ)
-        nc.gpsimd.dma_start(rows[8:12, 0:P], gain.rearrange("(r p) -> r p", p=P))
+        nc.gpsimd.dma_start(occs[:], occ.rearrange("(h p t) -> p h t", h=2, t=4))
+        nc.gpsimd.dma_start(gains[:], gain.rearrange("(q r) -> q r", r=4))
         nc.sync.dma_start(lists[:], offs)
         nc.sync.dma_start(list2[:], offs2)
-        nc.sync.dma_start(win1[0:P:4, :].bitcast(I32), tab_scales.rearrange("a q t -> q a t").bitcast(I32))
-        load_words(words1[0], tab_words, 0)
+        load_scale_rows(win1, tab_scales)
+        load_scale_rows(win2, tab2_scales)
+        words1 = [load_words("words1_0", tab_words, 0)]
+        wm_raw = held("wm_raw", [P, PASSES, 2 * H], U8)
         nc.sync.dma_start(wm_raw[:].bitcast(I32), wm_words.rearrange("a p c -> p a c").bitcast(I32))
         for d in range(4):
             nc.sync.dma_start(
                 wms_raw[32 * d : 32 * d + 4, :].bitcast(I32).rearrange("i (a c) -> i a c", a=PASSES),
                 wm_scales[:, 4 * d : 4 * d + 4, :].rearrange("a i c -> i a c").bitcast(I32),
             )
-        load_wb(0)
-        for d in range(4):
-            nc.sync.dma_start(
-                win2[32 * d : 32 * d + 8, :].bitcast(I32), tab2_scales[:, 4 * d : 4 * d + 4, :].bitcast(I32)
-            )
-        load_words(words1[1], tab_words, 1)
+        wb_raw = [load_wb("wb_raw0", 0)]
+        wb_raw.append(load_wb("wb_raw1", 1))
 
-        picked1 = held("picked1", [P, S], U8)
-        nc.vector.tensor_copy(picked1[:], win1[:].indirect(lists[:]))
-        for d in range(4):
-            nc.sync.dma_start(
-                planes1[32 * d : 32 * d + 4, :].bitcast(I32), picked1[32 * d : 32 * d + 32 : 4, :].bitcast(I32)
-            )
-        wb_raw.append(held("win1", [P, 4, H], F32))
-        load_wb(1)
-
+        gather_scales("picked1", win1, lists, planes1)
+        words1.append(load_words("win1", tab_words, 1))
         first_pass = held("anchors0", [P, S], U32)
         nc.vector.tensor_copy(first_pass[:], words1[0][:].bitcast(U32).indirect(lists[:]))
-        words2 = [held("words1_0", [P, T], I32)]
-        load_words(words2[0], tab2_words, 0)
-
-        wb_codes = []
-        wb_scales = held("wb_scales", [P, PASSES * H], U8)
-        wb_woven = [held("wb_woven%d" % a, [P, H * 4], BF16) for a in range(PASSES)]
-        for a in range(PASSES):
-            nc.scalar.copy(
-                wb_woven[a][:].rearrange("p (c n i) -> p c i n", n=4, i=4),
-                wb_raw[a][:].rearrange("p i (c n) -> p c i n", n=4),
-            )
-        words2.append(held("wb_raw0", [P, T], I32))
-        load_words(words2[1], tab2_words, 1)
-
-        def quantise_wb(a, slot):
-            wb_codes.append(held(slot, [P, H], U32))
-            nc.vector.quantize_mx(
-                out=wb_codes[a][:].bitcast(FP8X4),
-                scales=wb_scales[:, H * a : H * (a + 1)],
-                in_=wb_woven[a][:],
-            )
-
-        vecs = held("vecs", [P, 2, 12], F32)
-        gains = vecs[:, 0, 8:12]
-
-        vec_bank = take_bank(7)
-        for h in range(2):
-            nc.tensor.transpose(vec_bank[:, P * h : P * (h + 1)], rows[:, P * h : P * (h + 1)], ident[:])
-        nc.scalar.copy(vecs[:], vec_bank[:, 0 : 2 * P].rearrange("p (h c) -> p h c", h=2)[:, :, 0:12])
+        words2 = [load_words("words1_0", tab2_words, 0)]
 
         wm_codes = held("wm_codes", [P, PASSES * 2 * H], U8)
         nc.vector.tensor_copy(
             wm_codes[:].bitcast(I32).rearrange("p (a t i w) -> p a t i w", a=PASSES, t=4, w=4),
             wm_raw[:].bitcast(I32).rearrange("p a (i t w) -> p a t i w", t=4, w=4),
         )
+        words2.append(load_words("wm_raw", tab2_words, 1))
         wm_planes = held("wm_planes", [P, PASSES * H], U8)
         nc.vector.tensor_copy(
             wm_planes[:].bitcast(I32).rearrange("p (a t i w) -> p a t i w", a=PASSES, t=4, w=2),
             wms_raw[:].bitcast(I32).rearrange("p (a i t w) -> p a t i w", a=PASSES, t=4, w=2),
         )
 
-        picked2 = held("picked2", [P, S], U8)
-        nc.vector.tensor_copy(picked2[:], win2[:].indirect(list2[:]))
-        planes2 = held("planes2", [P, S], U8)
-        nc.vector.tensor_copy(
-            planes2[:].bitcast(I32).rearrange("p (h t i w) -> p h t i w", h=2, t=4, w=2),
-            picked2[:].bitcast(I32).rearrange("p (h i t w) -> p h t i w", h=2, t=4, w=2),
-        )
+        gather_scales("picked2", win2, list2, planes2)
 
-        quantise_wb(0, "win2")
+        wb_woven = [held("wb_woven%d" % a, [P, H * 4], BF16) for a in range(PASSES)]
+        for a in range(PASSES):
+            for g in range(2):
+                nc.scalar.copy(
+                    wb_woven[a][:].rearrange("p (t i g s k) -> p g i t k s", t=4, g=2, s=4, k=4)[:, g],
+                    wb_raw[a][:].rearrange("p k (i t g s) -> p g i t k s", t=4, g=2, s=4)[:, g],
+                )
+
+        dwells = held("dwells", [P, 8, 2, 64], F32)
+        for u in range(2):
+            bank = take_bank(6 + u)
+            for g in range(2):
+                for e in range(2):
+                    c = 4 * g + 2 * u + e
+                    col = P * (2 * g + e)
+                    nc.tensor.transpose(bank[:, col : col + P], dwell_rows[:, c : c + 1].to_broadcast([P, P]), ident[:])
+            nc.scalar.copy(
+                dwells[:, :, u, :].rearrange("p b (n g e) -> p b n g e", g=2, e=2),
+                bank[:].rearrange("p (g e b n) -> p b n g e", g=2, e=2, b=8),
+            )
+
+        wb_codes = []
+        wb_scales = held("wb_scales", [P, PASSES * H], U8)
+
+        def quantise_wb(a, slot):
+            wb_codes.append(held(slot, [P, H], U32))
+            nc.vector.quantize_mx(
+                out=wb_codes[a][:].bitcast(FP8X4), scales=wb_scales[:, H * a : H * (a + 1)], in_=wb_woven[a][:]
+            )
+
+        def motif_gather(a, h):
+            v2 = held("motifs%d_%d" % (a, h), [P, HALF], U32)
+            nc.vector.tensor_copy(v2[:], words2[a][:].bitcast(U32).indirect(list2[:, 32 * h : 32 * (h + 1)]))
+            return v2
 
         b_codes = held("b_codes", [P, S], U32)
         b_scales = held("b_scales", [P, S], U8)
         c_codes = held("c_codes", [P, 2 * H], U32)
         c_scales = held("c_scales", [P, 2 * H], U8)
 
-        def motif_gather(a, h):
-            v2 = held("picked%d_%d" % (a, h), [P, HALF], U32)
-            nc.vector.tensor_copy(
-                v2[:].rearrange("p (t i s) -> p i t s", t=4, s=8),
-                words2[a][:].bitcast(U32).indirect(list2[:, 32 * h : 32 * (h + 1)]),
-            )
-            return v2
+        def motif_stage(h, v2):
+            b_woven = held("b_woven%d" % h, [P, 4, P, 4], BF16)
+            c_pairs = held("c_pairs%d" % h, [P, 2, 4, 256], BF16)
+            banks = [take_bank(4 * h + n) for n in range(4)]
 
-        def motif_stage(h, v2, product_banks, turn_banks):
-            bt = held("bt%d" % h, [P, 4, 2, 256], BF16)
-            c_woven = held("c_woven%d" % h, [P, H, 4], BF16)
-            banks = [take_bank(number) for number in product_banks]
-
-            def passes(a, r):
+            def passes(a, n):
                 for t in range(4):
                     nc.tensor.matmul_mx(
-                        out=banks[r][:, P * t : P * (t + 1)],
-                        lhsT=v2[a][:, P * t : P * (t + 1)].bitcast(FP8X4),
-                        lhsT_scale=planes2[4 * a :, HALF * h + P * t : HALF * h + P * (t + 1)],
-                        rhs=wb_codes[a][:, P * r : P * (r + 1)].bitcast(FP8X4),
-                        rhs_scale=wb_scales[:, H * a + P * r : H * a + P * (r + 1)],
+                        out=banks[n][:, P * t : P * (t + 1)],
+                        lhsT=wb_codes[a][:, P * t : P * (t + 1)].bitcast(FP8X4),
+                        lhsT_scale=wb_scales[:, H * a + P * t : H * a + P * (t + 1)],
+                        rhs=v2[a][:, P * n : P * (n + 1)].bitcast(FP8X4),
+                        rhs_scale=planes2[:, S * a + HALF * h + P * n : S * a + HALF * h + P * (n + 1)],
                         start=(a == 0 and t == 0),
                         stop=(a == PASSES - 1 and t == 3),
                     )
 
-            for r in range(4):
-                passes(0, r)
-            for r in range(4):
-                bank = banks[r]
-                passes(1, r)
+            for n in range(4):
+                passes(0, n)
+            for n in range(4):
+                passes(1, n)
                 nc.scalar.copy(
-                    bt[:, :, :, 64 * r : 64 * (r + 1)].rearrange("p t u (i s e) -> p t i u s e", i=4, e=2),
-                    bank[:].rearrange("p (t i u e s) -> p t i u s e", t=4, i=4, u=2, e=2),
-                )
-                nc.vector.tensor_tensor(
-                    c_woven[:, P * r : P * (r + 1), :],
-                    bank[:].rearrange("p (t c) -> p c t", t=4),
-                    vecs[:, h : h + 1, 0:4].to_broadcast([P, P, 4]),
-                    MULT,
-                )
-            b_woven = held("b_woven%d" % h, [P, HALF * 4], BF16)
-            pairs = bt[:].bitcast(F32)
-            for half in range(2):
-                bank = take_bank(turn_banks[half])
-                for t in range(2):
-                    for u in range(2):
-                        col = P * (2 * t + u)
-                        nc.tensor.transpose(bank[:, col : col + P], pairs[:, 2 * half + t, u, :], ident[:])
-                nc.scalar.copy(
-                    b_woven[:, 1024 * half : 1024 * (half + 1)].bitcast(F32).rearrange("p (t m u) -> p t m u", t=2, u=2),
-                    bank[:].rearrange("p (t u m) -> p t m u", t=2, u=2),
+                    b_woven[:, :, 32 * n : 32 * (n + 1), :], banks[n][:].rearrange("p (t q v) -> p v q t", t=4, v=4)
                 )
             nc.vector.quantize_mx(
                 out=b_codes[:, HALF * h : HALF * (h + 1)].bitcast(FP8X4),
                 scales=b_scales[:, HALF * h : HALF * (h + 1)],
-                in_=b_woven[:],
+                in_=b_woven[:].rearrange("p v q t -> p (v q t)"),
             )
-            return c_woven
+            for n in range(4):
+                nc.vector.tensor_tensor(
+                    c_pairs[:, :, :, 64 * n : 64 * (n + 1)].rearrange("p u t (q e) -> p u t q e", e=2),
+                    banks[n][:].rearrange("p (t q u e) -> p u t q e", t=4, u=2, e=2),
+                    dwells[:, 4 * h + n, :, :].unsqueeze(2).to_broadcast([P, 2, 4, 64]).rearrange("p u t (q e) -> p u t q e", e=2),
+                    MULT,
+                )
+            return c_pairs
 
-        def quantise_c(h, c_woven):
-            nc.vector.quantize_mx(
-                out=c_codes[:, H * h : H * (h + 1)].bitcast(FP8X4),
-                scales=c_scales[:, H * h : H * (h + 1)],
-                in_=c_woven[:].rearrange("p c t -> p (c t)"),
-            )
-
-        h_codes = []
-        h_woven = [held("win1", [P, HALF, 4], BF16), held("h_woven1", [P, HALF, 4], BF16)]
-        h_scales = held("h_scales", [P, S], U8)
-
-        def anchor_stage(chunk, first_pass, bank_numbers):
-            width = 256
-            j0 = width * chunk
-            picked = held("anchors1_%d" % chunk, [P, width], U32)
-            nc.vector.tensor_copy(
-                picked[:], words1[1][:].bitcast(U32).indirect(lists[:, j0 // 16 : (j0 + width) // 16])
-            )
-            v1 = [first_pass[:, j0 : j0 + width], picked[:]]
-            woven = h_woven[j0 // HALF][:, j0 % HALF : j0 % HALF + width, :]
-            banks = [take_bank(number) for number in bank_numbers]
-            for a in range(PASSES):
-                for n, bank in enumerate(banks):
-                    j = P * n
-                    for t in range(4):
-                        nc.tensor.matmul_mx(
-                            out=bank[:, P * t : P * (t + 1)],
-                            lhsT=wm_codes[:, 2 * (H * a + P * t) : 2 * (H * a + P * (t + 1))].bitcast(FP4X4),
-                            lhsT_scale=wm_planes[:, H * a + P * t : H * a + P * (t + 1)],
-                            rhs=v1[a][:, j : j + P].bitcast(FP8X4),
-                            rhs_scale=planes1[:, S * a + j0 + j : S * a + j0 + j + P],
-                            start=(a == 0 and t == 0),
-                            stop=(a == PASSES - 1 and t == 3),
-                        )
-            for n, bank in enumerate(banks):
+        def turn_c(h, c_pairs, bank_numbers):
+            c_woven = held("c_woven%d" % h, [P, H * 4], BF16)
+            pairs = c_pairs[:].bitcast(F32)
+            for g, number in enumerate(bank_numbers):
+                bank = take_bank(number)
+                for u in range(2):
+                    for t in range(2):
+                        col = P * (2 * u + t)
+                        nc.tensor.transpose(bank[:, col : col + P], pairs[:, u, 2 * g + t, :], ident[:])
                 nc.scalar.copy(
-                    woven[:, P * n : P * (n + 1), :], bank[:].rearrange("p (t c) -> p c t", t=4)
+                    c_woven[:].bitcast(F32).rearrange("p (r i g t s u) -> p g r t i s u", r=4, g=2, t=2, s=2, u=2)[:, g],
+                    bank[:].rearrange("p (u t i s r) -> p r t i s u", u=2, t=2, s=2, r=4),
+                )
+            nc.vector.quantize_mx(
+                out=c_codes[:, H * h : H * (h + 1)].bitcast(FP8X4), scales=c_scales[:, H * h : H * (h + 1)], in_=c_woven[:]
+            )
+
+        h_scales = held("h_scales", [P, S], U8)
+        h_woven = held("h_woven", [P, S, 4], BF16)
+
+        def anchor_passes(a, bank, j, picked):
+            for t in range(4):
+                nc.tensor.matmul_mx(
+                    out=bank[:, P * t : P * (t + 1)],
+                    lhsT=wm_codes[:, 2 * (H * a + P * t) : 2 * (H * a + P * (t + 1))].bitcast(FP4X4),
+                    lhsT_scale=wm_planes[:, H * a + P * t : H * a + P * (t + 1)],
+                    rhs=picked.bitcast(FP8X4),
+                    rhs_scale=planes1[:, S * a + j : S * a + j + P],
+                    start=(a == 0 and t == 0),
+                    stop=(a == PASSES - 1 and t == 3),
                 )
 
-        def quantise_h(half, slot):
-            codes = held(slot, [P, HALF], U32)
-            nc.vector.quantize_mx(
-                out=codes[:].bitcast(FP8X4),
-                scales=h_scales[:, HALF * half : HALF * (half + 1)],
-                in_=h_woven[half][:].rearrange("p c t -> p (c t)"),
+        def anchor_stage(chunk, banks):
+            j0 = ANCHORS * chunk
+            picked = held("anchors1_%d" % chunk, [P, ANCHORS], U32)
+            nc.vector.tensor_copy(
+                picked[:], words1[1][:].bitcast(U32).indirect(lists[:, j0 // 16 : (j0 + ANCHORS) // 16])
             )
-            h_codes.append(codes)
+            for n, bank in enumerate(banks):
+                j = j0 + P * n
+                anchor_passes(1, bank, j, picked[:, P * n : P * (n + 1)])
+                nc.scalar.copy(h_woven[:, j : j + P, :], bank[:].rearrange("p (t c) -> p c t", t=4))
 
         def loop_stage(j0, width, h):
             sig = ring.tile([P, width, 4], F32, name="sig", align_bytes=64, bufs=8)
@@ -284,18 +258,14 @@ def tile_list_chromatin_loop_map_kernel(
                         out=bank[:, P * t : P * (t + 1)],
                         lhsT=b_codes[:, cols].bitcast(FP8X4),
                         lhsT_scale=b_scales[:, cols],
-                        rhs=h_codes[j0 // HALF][:, j0 % HALF + j : j0 % HALF + j + P].bitcast(FP8X4),
+                        rhs=h_codes[:, j0 + j : j0 + j + P].bitcast(FP8X4),
                         rhs_scale=h_scales[:, j0 + j : j0 + j + P],
                         start=True,
                         stop=True,
                     )
-                nc.scalar.activation(
-                    sig[:, j : j + P, :], bank[:].rearrange("p (t c) -> p c t", t=4), ACT.Sigmoid
-                )
+                nc.scalar.activation(sig[:, j : j + P, :], bank[:].rearrange("p (t c) -> p c t", t=4), ACT.Sigmoid)
             woven = ring.tile([P, width, 4], BF16, name="loop_woven", align_bytes=64)
-            nc.vector.tensor_tensor(
-                woven[:], sig[:], vecs[:, h : h + 1, 4:8].to_broadcast([P, width, 4]), MULT
-            )
+            nc.vector.tensor_tensor(woven[:], sig[:], occs[:, h : h + 1, :].to_broadcast([P, width, 4]), MULT)
             return woven
 
         def loop_quantise(j0, width, h, woven):
@@ -308,7 +278,7 @@ def tile_list_chromatin_loop_map_kernel(
 
         def read_back(j0, width, loop):
             last = j0 + width == S
-            banks = [take_bank(number) for number in (stream_banks(2) if last else [0, 1])]
+            banks = [take_bank(number) for number in (stream_banks(2) if last else [6, 7])]
             for h in range(2):
                 for r in range(4):
                     nc.tensor.matmul_mx(
@@ -339,25 +309,30 @@ def tile_list_chromatin_loop_map_kernel(
                             scale=gains[:, r0 + r : r0 + r + 1],
                         )
                 nc.sync.dma_start(
-                    out.rearrange("(r p) j -> p r j", p=P)[:, r0 : r0 + 2, j0 : j0 + width], result[:]
+                    out.rearrange("(q r) j -> q r j", r=4)[:, r0 : r0 + 2, j0 : j0 + width], result[:]
                 )
 
+        quantise_wb(0, "win2")
+        h_banks = [take_bank(n) for n in range(8)]
+        for n, bank in enumerate(h_banks):
+            anchor_passes(0, bank, P * n, first_pass[:, P * n : P * (n + 1)])
         for chunk in range(4):
-            anchor_stage(chunk, first_pass, [2 * chunk, 2 * chunk + 1])
-        v2 = [[motif_gather(0, h) for h in range(2)]]
+            anchor_stage(chunk, h_banks[2 * chunk : 2 * chunk + 2])
         quantise_wb(1, "wb_codes1")
-        quantise_h(0, "words1_0")
+        v2 = [[motif_gather(0, h) for h in range(2)]]
         v2.append([motif_gather(1, h) for h in range(2)])
-        quantise_h(1, "wb_raw0")
-        c_woven = [
-            motif_stage(0, [v2[a][0] for a in range(PASSES)], [0, 1, 2, 3], [0, 1]),
-            motif_stage(1, [v2[a][1] for a in range(PASSES)], [4, 5, 6, 7], [4, 5]),
-        ]
-        for h in range(2):
-            quantise_c(h, c_woven[h])
+        h_codes = held("wm_raw", [P, S], U32)
+        nc.vector.quantize_mx(
+            out=h_codes[:].bitcast(FP8X4), scales=h_scales[:], in_=h_woven[:].rearrange("p c t -> p (c t)")
+        )
+        c_pairs = [motif_stage(h, [v2[a][h] for a in range(PASSES)]) for h in range(2)]
         j0 = 0
         for width in CHUNKS:
-            woven = [loop_stage(j0, width, h) for h in range(2)]
+            woven = []
+            for h in range(2):
+                woven.append(loop_stage(j0, width, h))
+                if j0 == 0:
+                    turn_c(h, c_pairs[h], [6, 7] if h else stream_banks(2))
             loop = [loop_quantise(j0, width, h, woven[h]) for h in range(2)]
             read_back(j0, width, loop)
             j0 = j0 + width

@@ -19,9 +19,20 @@ MULT = mybir.AluOpType.mult
 
 P = 128
 PASSES = 2
-HALF = 512
+PASS = 512
+BANKS = 8
 ANCHORS = 256
-CHUNKS = [256, 256, 256, 128, 128]
+ROUNDS = [256, 256, 256, 128, 128]
+STREAM_BANKS = 6
+RESULT_BANKS = [6, 7]
+SIGMOID_BUFS = 8
+LOOP_BUFS = 3
+RESULT_BUFS = 6
+
+SHARED_A = "shared_a"
+SHARED_B = "shared_b"
+SHARED_C = "shared_c"
+SHARED_D = "shared_d"
 
 
 def tile_list_chromatin_loop_map_kernel(
@@ -30,56 +41,56 @@ def tile_list_chromatin_loop_map_kernel(
     nc = tc.nc
     with ExitStack() as ctx:
         keep = ctx.enter_context(tc.tile_pool(name="keep", bufs=1))
-        ring = ctx.enter_context(tc.tile_pool(name="ring", bufs=3))
+        ring = ctx.enter_context(tc.tile_pool(name="ring", bufs=LOOP_BUFS))
         psum = ctx.enter_context(tc.psum_pool(name="psum", bufs=1))
 
-        def take_bank(n):
-            return psum.tile([P, 512], F32, name="bank%d" % n)
+        def take_bank(number):
+            return psum.tile([P, 512], F32, name="bank%d" % number)
 
         streamed = []
 
         def stream_banks(count):
-            numbers = [(len(streamed) + n) % 6 for n in range(count)]
+            numbers = [(len(streamed) + n) % STREAM_BANKS for n in range(count)]
             streamed.extend(numbers)
             return numbers
 
-        def held(name, shape, dtype):
-            return keep.tile(shape, dtype, name=name, align_bytes=64)
+        def held(tag, shape, dtype):
+            return keep.tile(shape, dtype, name=tag, align_bytes=64)
 
         lists = held("lists", [P, S // 16], U16)
         list2 = held("list2", [P, S // 16], U16)
-        win1 = held("win1", [P, T], U8)
-        win2 = held("win2", [P, T], U8)
+        scale_rows1 = held(SHARED_A, [P, T], U8)
+        scale_rows2 = held(SHARED_B, [P, T], U8)
         planes1 = held("planes1", [P, PASSES * S], U8)
         planes2 = held("planes2", [P, PASSES * S], U8)
-        wms_raw = held("wms_raw", [P, PASSES * H], U8)
+        wm_scale_rows = held("wm_scale_rows", [P, PASSES * H], U8)
         ident = held("ident", [P, P], F32)
         dwell_rows = held("dwell_rows", [P, 8], F32)
 
         warm = held("warm", [P, 2], F32)
-        nc.gpsimd.memset(win1[:].bitcast(I32), 0)
+        nc.gpsimd.memset(scale_rows1[:].bitcast(I32), 0)
         nc.vector.memset(warm[:, 0:1], 0.0)
-        nc.vector.memset(win2[:].bitcast(I32), 0)
-        nc.vector.memset(wms_raw[:].bitcast(I32), 0)
+        nc.vector.memset(scale_rows2[:].bitcast(I32), 0)
+        nc.vector.memset(wm_scale_rows[:].bitcast(I32), 0)
         nc.vector.memset(planes1[:].bitcast(I32), 0)
         nc.vector.memset(planes2[:].bitcast(I32), 0)
         nc.scalar.activation(warm[:, 1:2], warm[:, 0:1], ACT.Sigmoid)
 
-        def load_words(slot, table, a):
-            words = held(slot, [P, T], I32)
+        def load_words(tag, table, a):
+            words = held(tag, [P, T], I32)
             nc.sync.dma_start(words[:], table[a].rearrange("p t i -> p (t i)").bitcast(I32))
             return words
 
-        def load_wb(slot, a):
-            raw = held(slot, [P, 4, H], F32)
-            nc.sync.dma_start(raw[:], wb[HALF * a : HALF * (a + 1), :].rearrange("(p i) c -> p i c", i=4))
-            return raw
+        def load_wb(tag, a, c0, width):
+            raw = held(tag, [P, 4, width], F32)
+            nc.sync.dma_start(raw[:], wb[PASS * a : PASS * (a + 1), c0 : c0 + width].rearrange("(p i) c -> p i c", i=4))
+            return a, c0, width, raw
 
         def load_scale_rows(window, scales):
             nc.sync.dma_start(window[0:P:4, :].bitcast(I32), scales.rearrange("a q t -> q a t").bitcast(I32))
 
-        def gather_scales(name, window, offsets, planes):
-            picked = held(name, [P, S], U8)
+        def gather_scales(tag, window, offsets, planes):
+            picked = held(tag, [P, S], U8)
             nc.vector.tensor_copy(picked[:], window[:].indirect(offsets[:]))
             for d in range(4):
                 nc.sync.dma_start(
@@ -92,52 +103,54 @@ def tile_list_chromatin_loop_map_kernel(
         make_identity(nc, ident[:])
         nc.gpsimd.dma_start(occs[:], occ.rearrange("(h p t) -> p h t", h=2, t=4))
         nc.gpsimd.dma_start(gains[:], gain.rearrange("(q r) -> q r", r=4))
+
         nc.sync.dma_start(lists[:], offs)
         nc.sync.dma_start(list2[:], offs2)
-        load_scale_rows(win1, tab_scales)
-        load_scale_rows(win2, tab2_scales)
-        words1 = [load_words("words1_0", tab_words, 0)]
-        wm_raw = held("wm_raw", [P, PASSES, 2 * H], U8)
+        load_scale_rows(scale_rows1, tab_scales)
+        load_scale_rows(scale_rows2, tab2_scales)
+        words1 = [load_words(SHARED_C, tab_words, 0)]
+        wm_raw = held(SHARED_D, [P, PASSES, 2 * H], U8)
         nc.sync.dma_start(wm_raw[:].bitcast(I32), wm_words.rearrange("a p c -> p a c").bitcast(I32))
         for d in range(4):
             nc.sync.dma_start(
-                wms_raw[32 * d : 32 * d + 4, :].bitcast(I32).rearrange("i (a c) -> i a c", a=PASSES),
+                wm_scale_rows[32 * d : 32 * d + 4, :].bitcast(I32).rearrange("i (a c) -> i a c", a=PASSES),
                 wm_scales[:, 4 * d : 4 * d + 4, :].rearrange("a i c -> i a c").bitcast(I32),
             )
-        wb_raw = [load_wb("wb_raw0", 0)]
-        wb_raw.append(load_wb("wb_raw1", 1))
+        wb_raw = [load_wb("wb_raw0", 0, 0, H), load_wb("wb_raw1", 1, 0, H // 2)]
 
-        gather_scales("picked1", win1, lists, planes1)
-        words1.append(load_words("win1", tab_words, 1))
+        gather_scales("picked1", scale_rows1, lists, planes1)
+        words1.append(load_words(SHARED_A, tab_words, 1))
         first_pass = held("anchors0", [P, S], U32)
         nc.vector.tensor_copy(first_pass[:], words1[0][:].bitcast(U32).indirect(lists[:]))
-        words2 = [load_words("words1_0", tab2_words, 0)]
+        wb_raw.append(load_wb(SHARED_C, 1, H // 2, H // 2))
 
         wm_codes = held("wm_codes", [P, PASSES * 2 * H], U8)
         nc.vector.tensor_copy(
             wm_codes[:].bitcast(I32).rearrange("p (a t i w) -> p a t i w", a=PASSES, t=4, w=4),
             wm_raw[:].bitcast(I32).rearrange("p a (i t w) -> p a t i w", t=4, w=4),
         )
-        words2.append(load_words("wm_raw", tab2_words, 1))
+        words2 = [load_words(SHARED_D, tab2_words, 0)]
         wm_planes = held("wm_planes", [P, PASSES * H], U8)
         nc.vector.tensor_copy(
             wm_planes[:].bitcast(I32).rearrange("p (a t i w) -> p a t i w", a=PASSES, t=4, w=2),
-            wms_raw[:].bitcast(I32).rearrange("p (a i t w) -> p a t i w", a=PASSES, t=4, w=2),
+            wm_scale_rows[:].bitcast(I32).rearrange("p (a i t w) -> p a t i w", a=PASSES, t=4, w=2),
         )
 
-        gather_scales("picked2", win2, list2, planes2)
+        gather_scales("picked2", scale_rows2, list2, planes2)
+        words2.append(load_words(SHARED_B, tab2_words, 1))
 
         wb_woven = [held("wb_woven%d" % a, [P, H * 4], BF16) for a in range(PASSES)]
-        for a in range(PASSES):
+        for a, c0, width, raw in wb_raw:
+            dealt = wb_woven[a][:].rearrange("p (t i g n k) -> p g i t k n", t=4, g=2, n=4, k=4)
             for g in range(2):
                 nc.scalar.copy(
-                    wb_woven[a][:].rearrange("p (t i g s k) -> p g i t k s", t=4, g=2, s=4, k=4)[:, g],
-                    wb_raw[a][:].rearrange("p k (i t g s) -> p g i t k s", t=4, g=2, s=4)[:, g],
+                    dealt[:, g, c0 // 32 : (c0 + width) // 32],
+                    raw[:].rearrange("p k (i t g n) -> p g i t k n", t=4, g=2, n=4)[:, g],
                 )
 
         dwells = held("dwells", [P, 8, 2, 64], F32)
         for u in range(2):
-            bank = take_bank(6 + u)
+            bank = take_bank(RESULT_BANKS[u])
             for g in range(2):
                 for e in range(2):
                     c = 4 * g + 2 * u + e
@@ -151,35 +164,37 @@ def tile_list_chromatin_loop_map_kernel(
         wb_codes = []
         wb_scales = held("wb_scales", [P, PASSES * H], U8)
 
-        def quantise_wb(a, slot):
-            wb_codes.append(held(slot, [P, H], U32))
+        def quantise_wb(a, tag):
+            wb_codes.append(held(tag, [P, H], U32))
             nc.vector.quantize_mx(
                 out=wb_codes[a][:].bitcast(FP8X4), scales=wb_scales[:, H * a : H * (a + 1)], in_=wb_woven[a][:]
             )
 
-        def motif_gather(a, h):
-            v2 = held("motifs%d_%d" % (a, h), [P, HALF], U32)
-            nc.vector.tensor_copy(v2[:], words2[a][:].bitcast(U32).indirect(list2[:, 32 * h : 32 * (h + 1)]))
-            return v2
+        def motif_gather(a, half):
+            picked = held("motifs%d_%d" % (a, half), [P, PASS], U32)
+            offsets = list2[:, PASS * half // 16 : PASS * (half + 1) // 16]
+            nc.vector.tensor_copy(picked[:], words2[a][:].bitcast(U32).indirect(offsets))
+            return picked
 
         b_codes = held("b_codes", [P, S], U32)
         b_scales = held("b_scales", [P, S], U8)
         c_codes = held("c_codes", [P, 2 * H], U32)
         c_scales = held("c_scales", [P, 2 * H], U8)
 
-        def motif_stage(h, v2):
-            b_woven = held("b_woven%d" % h, [P, 4, P, 4], BF16)
-            c_pairs = held("c_pairs%d" % h, [P, 2, 4, 256], BF16)
-            banks = [take_bank(4 * h + n) for n in range(4)]
+        def motif_stage(half, picked):
+            b_woven = held("b_woven%d" % half, [P, 4, P, 4], BF16)
+            c_pairs = held("c_pairs%d" % half, [P, 2, 4, 256], BF16)
+            banks = [take_bank(4 * half + n) for n in range(4)]
 
             def passes(a, n):
+                m0 = PASS * half + P * n
                 for t in range(4):
                     nc.tensor.matmul_mx(
                         out=banks[n][:, P * t : P * (t + 1)],
                         lhsT=wb_codes[a][:, P * t : P * (t + 1)].bitcast(FP8X4),
                         lhsT_scale=wb_scales[:, H * a + P * t : H * a + P * (t + 1)],
-                        rhs=v2[a][:, P * n : P * (n + 1)].bitcast(FP8X4),
-                        rhs_scale=planes2[:, S * a + HALF * h + P * n : S * a + HALF * h + P * (n + 1)],
+                        rhs=picked[a][:, P * n : P * (n + 1)].bitcast(FP8X4),
+                        rhs_scale=planes2[:, S * a + m0 : S * a + m0 + P],
                         start=(a == 0 and t == 0),
                         stop=(a == PASSES - 1 and t == 3),
                     )
@@ -192,38 +207,39 @@ def tile_list_chromatin_loop_map_kernel(
                     b_woven[:, :, 32 * n : 32 * (n + 1), :], banks[n][:].rearrange("p (t q v) -> p v q t", t=4, v=4)
                 )
             nc.vector.quantize_mx(
-                out=b_codes[:, HALF * h : HALF * (h + 1)].bitcast(FP8X4),
-                scales=b_scales[:, HALF * h : HALF * (h + 1)],
+                out=b_codes[:, PASS * half : PASS * (half + 1)].bitcast(FP8X4),
+                scales=b_scales[:, PASS * half : PASS * (half + 1)],
                 in_=b_woven[:].rearrange("p v q t -> p (v q t)"),
             )
             for n in range(4):
+                factors = dwells[:, 4 * half + n, :, :].unsqueeze(2).to_broadcast([P, 2, 4, 64])
                 nc.vector.tensor_tensor(
                     c_pairs[:, :, :, 64 * n : 64 * (n + 1)].rearrange("p u t (q e) -> p u t q e", e=2),
                     banks[n][:].rearrange("p (t q u e) -> p u t q e", t=4, u=2, e=2),
-                    dwells[:, 4 * h + n, :, :].unsqueeze(2).to_broadcast([P, 2, 4, 64]).rearrange("p u t (q e) -> p u t q e", e=2),
+                    factors.rearrange("p u t (q e) -> p u t q e", e=2),
                     MULT,
                 )
             return c_pairs
 
-        def turn_c(h, c_pairs, bank_numbers):
-            c_woven = held("c_woven%d" % h, [P, H * 4], BF16)
+        def turn_c(half, c_pairs, bank_numbers):
+            c_woven = held("c_woven%d" % half, [P, H * 4], BF16)
             pairs = c_pairs[:].bitcast(F32)
+            dealt = c_woven[:].bitcast(F32).rearrange("p (w i g x y u) -> p g w x i y u", w=4, g=2, x=2, y=2, u=2)
             for g, number in enumerate(bank_numbers):
                 bank = take_bank(number)
                 for u in range(2):
-                    for t in range(2):
-                        col = P * (2 * u + t)
-                        nc.tensor.transpose(bank[:, col : col + P], pairs[:, u, 2 * g + t, :], ident[:])
-                nc.scalar.copy(
-                    c_woven[:].bitcast(F32).rearrange("p (r i g t s u) -> p g r t i s u", r=4, g=2, t=2, s=2, u=2)[:, g],
-                    bank[:].rearrange("p (u t i s r) -> p r t i s u", u=2, t=2, s=2, r=4),
-                )
+                    for x in range(2):
+                        col = P * (2 * u + x)
+                        nc.tensor.transpose(bank[:, col : col + P], pairs[:, u, 2 * g + x, :], ident[:])
+                nc.scalar.copy(dealt[:, g], bank[:].rearrange("p (u x i y w) -> p w x i y u", u=2, x=2, y=2, w=4))
             nc.vector.quantize_mx(
-                out=c_codes[:, H * h : H * (h + 1)].bitcast(FP8X4), scales=c_scales[:, H * h : H * (h + 1)], in_=c_woven[:]
+                out=c_codes[:, H * half : H * (half + 1)].bitcast(FP8X4),
+                scales=c_scales[:, H * half : H * (half + 1)],
+                in_=c_woven[:],
             )
 
         h_scales = held("h_scales", [P, S], U8)
-        h_woven = held("h_woven", [P, S, 4], BF16)
+        h_woven = held(SHARED_C, [P, S, 4], BF16)
 
         def anchor_passes(a, bank, j, picked):
             for t in range(4):
@@ -237,9 +253,8 @@ def tile_list_chromatin_loop_map_kernel(
                     stop=(a == PASSES - 1 and t == 3),
                 )
 
-        def anchor_stage(chunk, banks):
-            j0 = ANCHORS * chunk
-            picked = held("anchors1_%d" % chunk, [P, ANCHORS], U32)
+        def anchor_second_pass(j0, banks):
+            picked = held("anchors1_%d" % j0, [P, ANCHORS], U32)
             nc.vector.tensor_copy(
                 picked[:], words1[1][:].bitcast(U32).indirect(lists[:, j0 // 16 : (j0 + ANCHORS) // 16])
             )
@@ -248,12 +263,12 @@ def tile_list_chromatin_loop_map_kernel(
                 anchor_passes(1, bank, j, picked[:, P * n : P * (n + 1)])
                 nc.scalar.copy(h_woven[:, j : j + P, :], bank[:].rearrange("p (t c) -> p c t", t=4))
 
-        def loop_stage(j0, width, h):
-            sig = ring.tile([P, width, 4], F32, name="sig", align_bytes=64, bufs=8)
+        def loop_values(j0, width, half):
+            sig = ring.tile([P, width, 4], F32, name="sig", align_bytes=64, bufs=SIGMOID_BUFS)
             for j, number in zip(range(0, width, P), stream_banks(width // P)):
                 bank = take_bank(number)
                 for t in range(4):
-                    cols = slice(HALF * h + P * t, HALF * h + P * (t + 1))
+                    cols = slice(PASS * half + P * t, PASS * half + P * (t + 1))
                     nc.tensor.matmul_mx(
                         out=bank[:, P * t : P * (t + 1)],
                         lhsT=b_codes[:, cols].bitcast(FP8X4),
@@ -265,12 +280,12 @@ def tile_list_chromatin_loop_map_kernel(
                     )
                 nc.scalar.activation(sig[:, j : j + P, :], bank[:].rearrange("p (t c) -> p c t", t=4), ACT.Sigmoid)
             woven = ring.tile([P, width, 4], BF16, name="loop_woven", align_bytes=64)
-            nc.vector.tensor_tensor(woven[:], sig[:], occs[:, h : h + 1, :].to_broadcast([P, width, 4]), MULT)
+            nc.vector.tensor_tensor(woven[:], sig[:], occs[:, half : half + 1, :].to_broadcast([P, width, 4]), MULT)
             return woven
 
-        def loop_quantise(j0, width, h, woven):
-            codes = held("loop_codes%d_%d" % (j0, h), [P, width], U32)
-            scales = held("loop_scales%d_%d" % (j0, h), [P, width], U8)
+        def loop_quantise(j0, width, half, woven):
+            codes = held("loop_codes%d_%d" % (j0, half), [P, width], U32)
+            scales = held("loop_scales%d_%d" % (j0, half), [P, width], U8)
             nc.vector.quantize_mx(
                 out=codes[:].bitcast(FP8X4), scales=scales[:], in_=woven[:].rearrange("p c t -> p (c t)")
             )
@@ -278,61 +293,63 @@ def tile_list_chromatin_loop_map_kernel(
 
         def read_back(j0, width, loop):
             last = j0 + width == S
-            banks = [take_bank(number) for number in (stream_banks(2) if last else [6, 7])]
-            for h in range(2):
-                for r in range(4):
+            banks = [take_bank(number) for number in (stream_banks(2) if last else RESULT_BANKS)]
+            for half in range(2):
+                for tile in range(4):
+                    cols = slice(H * half + P * tile, H * half + P * (tile + 1))
                     nc.tensor.matmul_mx(
-                        out=banks[r // 2][:, width * (r % 2) : width * (r % 2 + 1)],
-                        lhsT=c_codes[:, H * h + P * r : H * h + P * (r + 1)].bitcast(FP8X4),
-                        lhsT_scale=c_scales[:, H * h + P * r : H * h + P * (r + 1)],
-                        rhs=loop[h][0][:].bitcast(FP8X4),
-                        rhs_scale=loop[h][1][:],
-                        start=(h == 0 and r % 2 == 0),
-                        stop=(h == 1 and r % 2 == 1),
+                        out=banks[tile // 2][:, width * (tile % 2) : width * (tile % 2 + 1)],
+                        lhsT=c_codes[:, cols].bitcast(FP8X4),
+                        lhsT_scale=c_scales[:, cols],
+                        rhs=loop[half][0][:].bitcast(FP8X4),
+                        rhs_scale=loop[half][1][:],
+                        start=(half == 0 and tile % 2 == 0),
+                        stop=(half == 1 and tile % 2 == 1),
                     )
-            for r0 in (0, 2):
-                bank = banks[r0 // 2]
-                result = ring.tile([P, 2, width], F32, name="result", align_bytes=64, bufs=6)
-                if last and r0 == 0:
+            for tile0 in (0, 2):
+                bank = banks[tile0 // 2]
+                result = ring.tile([P, 2, width], F32, name="result", align_bytes=64, bufs=RESULT_BUFS)
+                if last and tile0 == 0:
                     nc.vector.tensor_tensor(
                         result[:],
-                        bank[:, 0 : 2 * width].rearrange("p (r c) -> p r c", r=2),
-                        gains[:, r0 : r0 + 2].unsqueeze(2).to_broadcast([P, 2, width]),
+                        bank[:, 0 : 2 * width].rearrange("p (w c) -> p w c", w=2),
+                        gains[:, tile0 : tile0 + 2].unsqueeze(2).to_broadcast([P, 2, width]),
                         MULT,
                     )
                 else:
-                    for r in range(2):
+                    for n in range(2):
                         nc.scalar.activation(
-                            result[:, r, :],
-                            bank[:, width * r : width * (r + 1)],
+                            result[:, n, :],
+                            bank[:, width * n : width * (n + 1)],
                             ACT.Copy,
-                            scale=gains[:, r0 + r : r0 + r + 1],
+                            scale=gains[:, tile0 + n : tile0 + n + 1],
                         )
                 nc.sync.dma_start(
-                    out.rearrange("(q r) j -> q r j", r=4)[:, r0 : r0 + 2, j0 : j0 + width], result[:]
+                    out.rearrange("(q w) j -> q w j", w=4)[:, tile0 : tile0 + 2, j0 : j0 + width], result[:]
                 )
 
-        quantise_wb(0, "win2")
-        h_banks = [take_bank(n) for n in range(8)]
+        quantise_wb(0, "wb_codes0")
+        h_banks = [take_bank(n) for n in range(BANKS)]
         for n, bank in enumerate(h_banks):
             anchor_passes(0, bank, P * n, first_pass[:, P * n : P * (n + 1)])
-        for chunk in range(4):
-            anchor_stage(chunk, h_banks[2 * chunk : 2 * chunk + 2])
-        quantise_wb(1, "wb_codes1")
-        v2 = [[motif_gather(0, h) for h in range(2)]]
-        v2.append([motif_gather(1, h) for h in range(2)])
-        h_codes = held("wm_raw", [P, S], U32)
+        for j0 in range(0, S, ANCHORS):
+            anchor_second_pass(j0, h_banks[j0 // P : (j0 + ANCHORS) // P])
+        quantise_wb(1, SHARED_A)
+
+        motifs = [[motif_gather(a, half) for half in range(2)] for a in range(PASSES)]
+        h_codes = held(SHARED_B, [P, S], U32)
         nc.vector.quantize_mx(
             out=h_codes[:].bitcast(FP8X4), scales=h_scales[:], in_=h_woven[:].rearrange("p c t -> p (c t)")
         )
-        c_pairs = [motif_stage(h, [v2[a][h] for a in range(PASSES)]) for h in range(2)]
+        c_pairs = [motif_stage(half, [motifs[a][half] for a in range(PASSES)]) for half in range(2)]
+
         j0 = 0
-        for width in CHUNKS:
+        for width in ROUNDS:
             woven = []
-            for h in range(2):
-                woven.append(loop_stage(j0, width, h))
+            for half in range(2):
+                woven.append(loop_values(j0, width, half))
                 if j0 == 0:
-                    turn_c(h, c_pairs[h], [6, 7] if h else stream_banks(2))
-            loop = [loop_quantise(j0, width, h, woven[h]) for h in range(2)]
+                    turn_c(half, c_pairs[half], RESULT_BANKS if half == 1 else stream_banks(2))
+            loop = [loop_quantise(j0, width, half, woven[half]) for half in range(2)]
             read_back(j0, width, loop)
             j0 = j0 + width

@@ -23,7 +23,8 @@ PASS = 512
 BANKS = 8
 ANCHORS = 256
 ROUNDS = [256, 256, 256, 128, 128]
-STREAM_BANKS = 6
+SCORE_BANKS = [[[0, 1], [4, 5]], [[6, 7], [4, 5]], [[6, 7], [0, 1]], [[2], [3]], [[6], [7]]]
+ROUND_BANKS = [[4, 5], [0, 1], [4, 5], [2, 3], [6, 7]]
 RESULT_BANKS = [6, 7]
 SIGMOID_BUFS = 8
 LOOP_BUFS = 3
@@ -46,13 +47,6 @@ def tile_list_chromatin_loop_map_kernel(
 
         def take_bank(number):
             return psum.tile([P, 512], F32, name="bank%d" % number)
-
-        streamed = []
-
-        def stream_banks(count):
-            numbers = [(len(streamed) + n) % STREAM_BANKS for n in range(count)]
-            streamed.extend(numbers)
-            return numbers
 
         def held(tag, shape, dtype):
             return keep.tile(shape, dtype, name=tag, align_bytes=64)
@@ -82,8 +76,8 @@ def tile_list_chromatin_loop_map_kernel(
             return words
 
         def load_wb(tag, a, c0, width):
-            raw = held(tag, [P, 4, width], F32)
-            nc.sync.dma_start(raw[:], wb[PASS * a : PASS * (a + 1), c0 : c0 + width].rearrange("(p i) c -> p i c", i=4))
+            raw = tag[:, :, c0 : c0 + width]
+            nc.sync.dma_start(raw, wb[PASS * a : PASS * (a + 1), c0 : c0 + width].rearrange("(p i) c -> p i c", i=4))
             return a, c0, width, raw
 
         def load_scale_rows(window, scales):
@@ -97,17 +91,11 @@ def tile_list_chromatin_loop_map_kernel(
                     planes[32 * d : 32 * d + 4, :].bitcast(I32), picked[32 * d : 32 * d + 32 : 4, :].bitcast(I32)
                 )
 
-        nc.gpsimd.dma_start(dwell_rows[:], dwell.rearrange("(n c) -> n c", c=8))
-        occs = held("occs", [P, 2, 4], F32)
-        gains = held("gains", [P, 4], F32)
         make_identity(nc, ident[:])
-        nc.gpsimd.dma_start(occs[:], occ.rearrange("(h p t) -> p h t", h=2, t=4))
-        nc.gpsimd.dma_start(gains[:], gain.rearrange("(q r) -> q r", r=4))
 
         nc.sync.dma_start(lists[:], offs)
-        nc.sync.dma_start(list2[:], offs2)
+        nc.sync.dma_start(dwell_rows[:], dwell.rearrange("(n c) -> n c", c=8))
         load_scale_rows(scale_rows1, tab_scales)
-        load_scale_rows(scale_rows2, tab2_scales)
         words1 = [load_words(SHARED_C, tab_words, 0)]
         wm_raw = held(SHARED_D, [P, PASSES, 2 * H], U8)
         nc.sync.dma_start(wm_raw[:].bitcast(I32), wm_words.rearrange("a p c -> p a c").bitcast(I32))
@@ -116,13 +104,17 @@ def tile_list_chromatin_loop_map_kernel(
                 wm_scale_rows[32 * d : 32 * d + 4, :].bitcast(I32).rearrange("i (a c) -> i a c", a=PASSES),
                 wm_scales[:, 4 * d : 4 * d + 4, :].rearrange("a i c -> i a c").bitcast(I32),
             )
-        wb_raw = [load_wb("wb_raw0", 0, 0, H), load_wb("wb_raw1", 1, 0, H // 2)]
+        wb_raw = [load_wb(held("wb_raw0", [P, 4, H], F32), 0, 0, H)]
+        nc.sync.dma_start(list2[:], offs2)
+        load_scale_rows(scale_rows2, tab2_scales)
 
         gather_scales("picked1", scale_rows1, lists, planes1)
         words1.append(load_words(SHARED_A, tab_words, 1))
         first_pass = held("anchors0", [P, S], U32)
         nc.vector.tensor_copy(first_pass[:], words1[0][:].bitcast(U32).indirect(lists[:]))
-        wb_raw.append(load_wb(SHARED_C, 1, H // 2, H // 2))
+        wb_last = held(SHARED_C, [P, 4, H], F32)
+        wb_raw.append(load_wb(wb_last, 1, 0, H // 2))
+        wb_raw.append(load_wb(wb_last, 1, H // 2, H // 2))
 
         wm_codes = held("wm_codes", [P, PASSES * 2 * H], U8)
         nc.vector.tensor_copy(
@@ -145,7 +137,7 @@ def tile_list_chromatin_loop_map_kernel(
             for g in range(2):
                 nc.scalar.copy(
                     dealt[:, g, c0 // 32 : (c0 + width) // 32],
-                    raw[:].rearrange("p k (i t g n) -> p g i t k n", t=4, g=2, n=4)[:, g],
+                    raw.rearrange("p k (i t g n) -> p g i t k n", t=4, g=2, n=4)[:, g],
                 )
 
         dwells = held("dwells", [P, 8, 2, 64], F32)
@@ -232,6 +224,9 @@ def tile_list_chromatin_loop_map_kernel(
                         col = P * (2 * u + x)
                         nc.tensor.transpose(bank[:, col : col + P], pairs[:, u, 2 * g + x, :], ident[:])
                 nc.scalar.copy(dealt[:, g], bank[:].rearrange("p (u x i y w) -> p w x i y u", u=2, x=2, y=2, w=4))
+            return c_woven
+
+        def quantise_c(half, c_woven):
             nc.vector.quantize_mx(
                 out=c_codes[:, H * half : H * (half + 1)].bitcast(FP8X4),
                 scales=c_scales[:, H * half : H * (half + 1)],
@@ -264,8 +259,9 @@ def tile_list_chromatin_loop_map_kernel(
                 nc.scalar.copy(h_woven[:, j : j + P, :], bank[:].rearrange("p (t c) -> p c t", t=4))
 
         def loop_values(j0, width, half):
-            sig = ring.tile([P, width, 4], F32, name="sig", align_bytes=64, bufs=SIGMOID_BUFS)
-            for j, number in zip(range(0, width, P), stream_banks(width // P)):
+            sig = held("sig%d_%d" % (j0, half), [P, width, 4], F32)
+            numbers = SCORE_BANKS[starts.index(j0)][half]
+            for j, number in zip(range(0, width, P), numbers):
                 bank = take_bank(number)
                 for t in range(4):
                     cols = slice(PASS * half + P * t, PASS * half + P * (t + 1))
@@ -273,12 +269,15 @@ def tile_list_chromatin_loop_map_kernel(
                         out=bank[:, P * t : P * (t + 1)],
                         lhsT=b_codes[:, cols].bitcast(FP8X4),
                         lhsT_scale=b_scales[:, cols],
-                        rhs=h_codes[:, j0 + j : j0 + j + P].bitcast(FP8X4),
+                        rhs=h_codes[j0 + j].bitcast(FP8X4),
                         rhs_scale=h_scales[:, j0 + j : j0 + j + P],
                         start=True,
                         stop=True,
                     )
                 nc.scalar.activation(sig[:, j : j + P, :], bank[:].rearrange("p (t c) -> p c t", t=4), ACT.Sigmoid)
+            return sig
+
+        def occ_product(width, half, sig):
             woven = ring.tile([P, width, 4], BF16, name="loop_woven", align_bytes=64)
             nc.vector.tensor_tensor(woven[:], sig[:], occs[:, half : half + 1, :].to_broadcast([P, width, 4]), MULT)
             return woven
@@ -292,9 +291,9 @@ def tile_list_chromatin_loop_map_kernel(
             return codes, scales
 
         def read_back(j0, width, loop):
-            last = j0 + width == S
-            banks = [take_bank(number) for number in (stream_banks(2) if last else RESULT_BANKS)]
-            for half in range(2):
+            banks = [take_bank(number) for number in ROUND_BANKS[starts.index(j0)]]
+            first, second = loop
+            for half in loop:
                 for tile in range(4):
                     cols = slice(H * half + P * tile, H * half + P * (tile + 1))
                     nc.tensor.matmul_mx(
@@ -303,13 +302,17 @@ def tile_list_chromatin_loop_map_kernel(
                         lhsT_scale=c_scales[:, cols],
                         rhs=loop[half][0][:].bitcast(FP8X4),
                         rhs_scale=loop[half][1][:],
-                        start=(half == 0 and tile % 2 == 0),
-                        stop=(half == 1 and tile % 2 == 1),
+                        start=(half == first and tile % 2 == 0),
+                        stop=(half == second and tile % 2 == 1),
                     )
-            for tile0 in (0, 2):
+            return banks
+
+        def copy_out(j0, width, banks, tiles, on_vector):
+            for tile0 in tiles:
                 bank = banks[tile0 // 2]
-                result = ring.tile([P, 2, width], F32, name="result", align_bytes=64, bufs=RESULT_BUFS)
-                if last and tile0 == 0:
+                tag = "sig%d_1" % (j0 + width) if on_vector else "result%d_%d" % (j0, tile0)
+                result = held(tag, [P, 2, width], F32)
+                if on_vector:
                     nc.vector.tensor_tensor(
                         result[:],
                         bank[:, 0 : 2 * width].rearrange("p (w c) -> p w c", w=2),
@@ -335,21 +338,53 @@ def tile_list_chromatin_loop_map_kernel(
         for j0 in range(0, S, ANCHORS):
             anchor_second_pass(j0, h_banks[j0 // P : (j0 + ANCHORS) // P])
         quantise_wb(1, SHARED_A)
+        spare = take_bank(0)
+        for t in range(4):
+            nc.tensor.matmul_mx(
+                out=spare[:],
+                lhsT=wm_codes[:, 2 * P * t : 2 * P * (t + 1)].bitcast(FP4X4),
+                lhsT_scale=wm_planes[:, P * t : P * (t + 1)],
+                rhs=first_pass[:, 0:PASS].bitcast(FP8X4),
+                rhs_scale=planes1[:, 0:PASS],
+                start=True,
+                stop=True,
+            )
 
         motifs = [[motif_gather(a, half) for half in range(2)] for a in range(PASSES)]
-        h_codes = held(SHARED_B, [P, S], U32)
-        nc.vector.quantize_mx(
-            out=h_codes[:].bitcast(FP8X4), scales=h_scales[:], in_=h_woven[:].rearrange("p c t -> p (c t)")
-        )
-        c_pairs = [motif_stage(half, [motifs[a][half] for a in range(PASSES)]) for half in range(2)]
+        h_codes = {}
 
-        j0 = 0
-        for width in ROUNDS:
-            woven = []
-            for half in range(2):
-                woven.append(loop_values(j0, width, half))
-                if j0 == 0:
-                    turn_c(half, c_pairs[half], RESULT_BANKS if half == 1 else stream_banks(2))
-            loop = [loop_quantise(j0, width, half, woven[half]) for half in range(2)]
-            read_back(j0, width, loop)
-            j0 = j0 + width
+        def quantise_h(codes, j0):
+            width = codes.shape[1]
+            nc.vector.quantize_mx(
+                out=codes.bitcast(FP8X4),
+                scales=h_scales[:, j0 : j0 + width],
+                in_=h_woven[:, j0 : j0 + width, :].rearrange("p c t -> p (c t)"),
+            )
+            for j in range(0, width, P):
+                h_codes[j0 + j] = codes[:, j : j + P]
+
+        quantise_h(held(SHARED_B, [P, S // 2], U32)[:], 0)
+        c_pairs = [motif_stage(half, [motifs[a][half] for a in range(PASSES)]) for half in range(2)]
+        quantise_h(held("b_woven1", [P, S // 2], U32)[:], S // 2)
+
+        occs = held(SHARED_D, [P, 2, 4], F32)
+        nc.sync.dma_start(occs[:], occ.rearrange("(h p t) -> p h t", h=2, t=4))
+        gains = held("motifs0_0", [P, 4], F32)
+        nc.sync.dma_start(gains[:], gain.rearrange("(q r) -> q r", r=4))
+        starts = [sum(ROUNDS[:r]) for r in range(len(ROUNDS))]
+        sigs = [[loop_values(0, ROUNDS[0], 0)]]
+        quantise_c(0, turn_c(0, c_pairs[0], [2, 3]))
+        sigs[0].append(loop_values(0, ROUNDS[0], 1))
+        sigs.append([loop_values(starts[1], ROUNDS[1], 0)])
+        c_woven = turn_c(1, c_pairs[1], [0, 1])
+        sigs[1].append(loop_values(starts[1], ROUNDS[1], 1))
+        for r in range(2, len(ROUNDS)):
+            sigs.append([loop_values(starts[r], ROUNDS[r], half) for half in range(2)])
+        for r, (j0, width) in enumerate(zip(starts, ROUNDS)):
+            woven = [occ_product(width, half, sigs[r][half]) for half in range(2)]
+            if r == 0:
+                quantise_c(1, c_woven)
+            loop = {half: loop_quantise(j0, width, half, woven[half]) for half in range(2)}
+            banks = read_back(j0, width, loop)
+            copy_out(j0, width, banks, [0], j0 + width == S)
+            copy_out(j0, width, banks, [2], False)

@@ -76,8 +76,8 @@ def tile_list_chromatin_loop_map_kernel(
             return words
 
         def load_wb(tag, a, c0, width):
-            raw = tag[:, :, c0 : c0 + width]
-            nc.sync.dma_start(raw, wb[PASS * a : PASS * (a + 1), c0 : c0 + width].rearrange("(p i) c -> p i c", i=4))
+            raw = held(tag, [P, 4, width], F32)
+            nc.sync.dma_start(raw[:], wb[PASS * a : PASS * (a + 1), c0 : c0 + width].rearrange("(p i) c -> p i c", i=4))
             return a, c0, width, raw
 
         def load_scale_rows(window, scales):
@@ -91,11 +91,17 @@ def tile_list_chromatin_loop_map_kernel(
                     planes[32 * d : 32 * d + 4, :].bitcast(I32), picked[32 * d : 32 * d + 32 : 4, :].bitcast(I32)
                 )
 
+        nc.gpsimd.dma_start(dwell_rows[:], dwell.rearrange("(n c) -> n c", c=8))
+        occs = held("occs", [P, 2, 4], F32)
+        gains = held("gains", [P, 4], F32)
         make_identity(nc, ident[:])
+        nc.gpsimd.dma_start(occs[:], occ.rearrange("(h p t) -> p h t", h=2, t=4))
+        nc.gpsimd.dma_start(gains[:], gain.rearrange("(q r) -> q r", r=4))
 
         nc.sync.dma_start(lists[:], offs)
-        nc.sync.dma_start(dwell_rows[:], dwell.rearrange("(n c) -> n c", c=8))
+        nc.sync.dma_start(list2[:], offs2)
         load_scale_rows(scale_rows1, tab_scales)
+        load_scale_rows(scale_rows2, tab2_scales)
         words1 = [load_words(SHARED_C, tab_words, 0)]
         wm_raw = held(SHARED_D, [P, PASSES, 2 * H], U8)
         nc.sync.dma_start(wm_raw[:].bitcast(I32), wm_words.rearrange("a p c -> p a c").bitcast(I32))
@@ -104,17 +110,13 @@ def tile_list_chromatin_loop_map_kernel(
                 wm_scale_rows[32 * d : 32 * d + 4, :].bitcast(I32).rearrange("i (a c) -> i a c", a=PASSES),
                 wm_scales[:, 4 * d : 4 * d + 4, :].rearrange("a i c -> i a c").bitcast(I32),
             )
-        wb_raw = [load_wb(held("wb_raw0", [P, 4, H], F32), 0, 0, H)]
-        nc.sync.dma_start(list2[:], offs2)
-        load_scale_rows(scale_rows2, tab2_scales)
+        wb_raw = [load_wb("wb_raw0", 0, 0, H), load_wb("wb_raw1", 1, 0, H // 2)]
 
         gather_scales("picked1", scale_rows1, lists, planes1)
         words1.append(load_words(SHARED_A, tab_words, 1))
         first_pass = held("anchors0", [P, S], U32)
         nc.vector.tensor_copy(first_pass[:], words1[0][:].bitcast(U32).indirect(lists[:]))
-        wb_last = held(SHARED_C, [P, 4, H], F32)
-        wb_raw.append(load_wb(wb_last, 1, 0, H // 2))
-        wb_raw.append(load_wb(wb_last, 1, H // 2, H // 2))
+        wb_raw.append(load_wb(SHARED_C, 1, H // 2, H // 2))
 
         wm_codes = held("wm_codes", [P, PASSES * 2 * H], U8)
         nc.vector.tensor_copy(
@@ -137,7 +139,7 @@ def tile_list_chromatin_loop_map_kernel(
             for g in range(2):
                 nc.scalar.copy(
                     dealt[:, g, c0 // 32 : (c0 + width) // 32],
-                    raw.rearrange("p k (i t g n) -> p g i t k n", t=4, g=2, n=4)[:, g],
+                    raw[:].rearrange("p k (i t g n) -> p g i t k n", t=4, g=2, n=4)[:, g],
                 )
 
         dwells = held("dwells", [P, 8, 2, 64], F32)
@@ -367,10 +369,6 @@ def tile_list_chromatin_loop_map_kernel(
         c_pairs = [motif_stage(half, [motifs[a][half] for a in range(PASSES)]) for half in range(2)]
         quantise_h(held("b_woven1", [P, S // 2], U32)[:], S // 2)
 
-        occs = held(SHARED_D, [P, 2, 4], F32)
-        nc.sync.dma_start(occs[:], occ.rearrange("(h p t) -> p h t", h=2, t=4))
-        gains = held("motifs0_0", [P, 4], F32)
-        nc.sync.dma_start(gains[:], gain.rearrange("(q r) -> q r", r=4))
         starts = [sum(ROUNDS[:r]) for r in range(len(ROUNDS))]
         sigs = [[loop_values(0, ROUNDS[0], 0)]]
         quantise_c(0, turn_c(0, c_pairs[0], [2, 3]))

@@ -24,16 +24,16 @@ BANKS = 8
 ANCHORS = 256
 ROUNDS = [256, 256, 256, 128, 128]
 SCORE_BANKS = [[[0, 1], [4, 5]], [[6, 7], [4, 5]], [[6, 7], [0, 1]], [[2], [3]], [[6], [7]]]
-ROUND_BANKS = [[4, 5], [0, 1], [4, 5], [2, 3], [6, 7]]
-RESULT_BANKS = [6, 7]
-SIGMOID_BUFS = 8
+RESULT_BANKS = [[4, 5], [0, 1], [4, 5], [2, 3], [6, 7]]
+TURN_BANKS = [[2, 3], [0, 1]]
+DWELL_BANKS = [6, 7]
 LOOP_BUFS = 3
-RESULT_BUFS = 6
 
 SHARED_A = "shared_a"
 SHARED_B = "shared_b"
 SHARED_C = "shared_c"
 SHARED_D = "shared_d"
+SHARED_E = "shared_e"
 
 
 def tile_list_chromatin_loop_map_kernel(
@@ -144,7 +144,7 @@ def tile_list_chromatin_loop_map_kernel(
 
         dwells = held("dwells", [P, 8, 2, 64], F32)
         for u in range(2):
-            bank = take_bank(RESULT_BANKS[u])
+            bank = take_bank(DWELL_BANKS[u])
             for g in range(2):
                 for e in range(2):
                     c = 4 * g + 2 * u + e
@@ -176,7 +176,7 @@ def tile_list_chromatin_loop_map_kernel(
         c_scales = held("c_scales", [P, 2 * H], U8)
 
         def motif_stage(half, picked):
-            b_woven = held("b_woven%d" % half, [P, 4, P, 4], BF16)
+            b_woven = held(SHARED_E if half == 1 else "b_woven0", [P, 4, P, 4], BF16)
             c_pairs = held("c_pairs%d" % half, [P, 2, 4, 256], BF16)
             banks = [take_bank(4 * half + n) for n in range(4)]
 
@@ -215,11 +215,11 @@ def tile_list_chromatin_loop_map_kernel(
                 )
             return c_pairs
 
-        def turn_c(half, c_pairs, bank_numbers):
+        def turn_c(half, c_pairs):
             c_woven = held("c_woven%d" % half, [P, H * 4], BF16)
             pairs = c_pairs[:].bitcast(F32)
             dealt = c_woven[:].bitcast(F32).rearrange("p (w i g x y u) -> p g w x i y u", w=4, g=2, x=2, y=2, u=2)
-            for g, number in enumerate(bank_numbers):
+            for g, number in enumerate(TURN_BANKS[half]):
                 bank = take_bank(number)
                 for u in range(2):
                     for x in range(2):
@@ -260,10 +260,12 @@ def tile_list_chromatin_loop_map_kernel(
                 anchor_passes(1, bank, j, picked[:, P * n : P * (n + 1)])
                 nc.scalar.copy(h_woven[:, j : j + P, :], bank[:].rearrange("p (t c) -> p c t", t=4))
 
-        def loop_values(j0, width, half):
-            sig = held("sig%d_%d" % (j0, half), [P, width, 4], F32)
-            numbers = SCORE_BANKS[starts.index(j0)][half]
-            for j, number in zip(range(0, width, P), numbers):
+        starts = [sum(ROUNDS[:r]) for r in range(len(ROUNDS))]
+
+        def sigmoids(r, half):
+            j0, width = starts[r], ROUNDS[r]
+            sig = held("sig%d_%d" % (r, half), [P, width, 4], F32)
+            for j, number in zip(range(0, width, P), SCORE_BANKS[r][half]):
                 bank = take_bank(number)
                 for t in range(4):
                     cols = slice(PASS * half + P * t, PASS * half + P * (t + 1))
@@ -292,10 +294,10 @@ def tile_list_chromatin_loop_map_kernel(
             )
             return codes, scales
 
-        def read_back(j0, width, loop):
-            banks = [take_bank(number) for number in ROUND_BANKS[starts.index(j0)]]
-            first, second = loop
-            for half in loop:
+        def read_back(r, loop):
+            j0, width = starts[r], ROUNDS[r]
+            banks = [take_bank(number) for number in RESULT_BANKS[r]]
+            for half in range(2):
                 for tile in range(4):
                     cols = slice(H * half + P * tile, H * half + P * (tile + 1))
                     nc.tensor.matmul_mx(
@@ -304,17 +306,13 @@ def tile_list_chromatin_loop_map_kernel(
                         lhsT_scale=c_scales[:, cols],
                         rhs=loop[half][0][:].bitcast(FP8X4),
                         rhs_scale=loop[half][1][:],
-                        start=(half == first and tile % 2 == 0),
-                        stop=(half == second and tile % 2 == 1),
+                        start=(half == 0 and tile % 2 == 0),
+                        stop=(half == 1 and tile % 2 == 1),
                     )
-            return banks
-
-        def copy_out(j0, width, banks, tiles, on_vector):
-            for tile0 in tiles:
+            for tile0 in (0, 2):
                 bank = banks[tile0 // 2]
-                tag = "sig%d_1" % (j0 + width) if on_vector else "result%d_%d" % (j0, tile0)
-                result = held(tag, [P, 2, width], F32)
-                if on_vector:
+                result = held("result%d_%d" % (r, tile0), [P, 2, width], F32)
+                if j0 + width == S and tile0 == 0:
                     nc.vector.tensor_tensor(
                         result[:],
                         bank[:, 0 : 2 * width].rearrange("p (w c) -> p w c", w=2),
@@ -340,17 +338,6 @@ def tile_list_chromatin_loop_map_kernel(
         for j0 in range(0, S, ANCHORS):
             anchor_second_pass(j0, h_banks[j0 // P : (j0 + ANCHORS) // P])
         quantise_wb(1, SHARED_A)
-        spare = take_bank(0)
-        for t in range(4):
-            nc.tensor.matmul_mx(
-                out=spare[:],
-                lhsT=wm_codes[:, 2 * P * t : 2 * P * (t + 1)].bitcast(FP4X4),
-                lhsT_scale=wm_planes[:, P * t : P * (t + 1)],
-                rhs=first_pass[:, 0:PASS].bitcast(FP8X4),
-                rhs_scale=planes1[:, 0:PASS],
-                start=True,
-                stop=True,
-            )
 
         motifs = [[motif_gather(a, half) for half in range(2)] for a in range(PASSES)]
         h_codes = {}
@@ -367,22 +354,18 @@ def tile_list_chromatin_loop_map_kernel(
 
         quantise_h(held(SHARED_B, [P, S // 2], U32)[:], 0)
         c_pairs = [motif_stage(half, [motifs[a][half] for a in range(PASSES)]) for half in range(2)]
-        quantise_h(held("b_woven1", [P, S // 2], U32)[:], S // 2)
+        quantise_h(held(SHARED_E, [P, S // 2], U32)[:], S // 2)
 
-        starts = [sum(ROUNDS[:r]) for r in range(len(ROUNDS))]
-        sigs = [[loop_values(0, ROUNDS[0], 0)]]
-        quantise_c(0, turn_c(0, c_pairs[0], [2, 3]))
-        sigs[0].append(loop_values(0, ROUNDS[0], 1))
-        sigs.append([loop_values(starts[1], ROUNDS[1], 0)])
-        c_woven = turn_c(1, c_pairs[1], [0, 1])
-        sigs[1].append(loop_values(starts[1], ROUNDS[1], 1))
+        sigs = [[sigmoids(0, 0)]]
+        quantise_c(0, turn_c(0, c_pairs[0]))
+        sigs[0].append(sigmoids(0, 1))
+        sigs.append([sigmoids(1, 0)])
+        c_woven = turn_c(1, c_pairs[1])
+        sigs[1].append(sigmoids(1, 1))
         for r in range(2, len(ROUNDS)):
-            sigs.append([loop_values(starts[r], ROUNDS[r], half) for half in range(2)])
-        for r, (j0, width) in enumerate(zip(starts, ROUNDS)):
+            sigs.append([sigmoids(r, half) for half in range(2)])
+        for r, width in enumerate(ROUNDS):
             woven = [occ_product(width, half, sigs[r][half]) for half in range(2)]
             if r == 0:
                 quantise_c(1, c_woven)
-            loop = {half: loop_quantise(j0, width, half, woven[half]) for half in range(2)}
-            banks = read_back(j0, width, loop)
-            copy_out(j0, width, banks, [0], j0 + width == S)
-            copy_out(j0, width, banks, [2], False)
+            read_back(r, [loop_quantise(starts[r], width, half, woven[half]) for half in range(2)])

@@ -29,6 +29,22 @@ TURN_BANKS = [[2, 3], [0, 1]]
 DWELL_BANKS = [6, 7]
 LOOP_BUFS = 3
 
+KIB = 1024
+PLACES = {
+    "scale_rows1": 7 * KIB,
+    "tab_second": 0,
+    "wb_codes1": 0,
+    "wb_middle": 8 * KIB,
+    "h_woven0": 8 * KIB,
+    "tab_first": 12 * KIB,
+    "tab2_first": 12 * KIB,
+    "h_codes0": 24 * KIB,
+    "wb_first": 20 * KIB,
+    "wb_last": 20 * KIB,
+    "h_woven1": 20 * KIB,
+    "tab2_second": 24 * KIB,
+}
+
 SHARED_A = "shared_a"
 SHARED_B = "shared_b"
 SHARED_C = "shared_c"
@@ -49,12 +65,19 @@ def tile_list_chromatin_loop_map_kernel(
             return psum.tile([P, 512], F32, name="bank%d" % number)
 
         def held(tag, shape, dtype):
+            if tag in PLACES:
+                return placed(tag, shape, dtype)
             return keep.tile(shape, dtype, name=tag, align_bytes=64)
+
+        arena = ctx.enter_context(tc.tile_pool(name="arena", bufs=1))
+
+        def placed(name, shape, dtype):
+            return arena.tile(shape, dtype, name=name, align_bytes=64, offset=PLACES[name])
 
         lists = held("lists", [P, S // 16], U16)
         list2 = held("list2", [P, S // 16], U16)
-        scale_rows1 = held(SHARED_A, [P, T], U8)
-        scale_rows2 = held(SHARED_B, [P, T], U8)
+        scale_rows1 = placed("scale_rows1", [P, T], U8)
+        scale_rows2 = held("scale_rows2", [P, T], U8)
         planes1 = held("planes1", [P, PASSES * S], U8)
         planes2 = held("planes2", [P, PASSES * S], U8)
         wm_scale_rows = held("wm_scale_rows", [P, PASSES * H], U8)
@@ -101,46 +124,53 @@ def tile_list_chromatin_loop_map_kernel(
         nc.sync.dma_start(lists[:], offs)
         nc.sync.dma_start(list2[:], offs2)
         load_scale_rows(scale_rows1, tab_scales)
+        words1 = [load_words("tab_first", tab_words, 0)]
         load_scale_rows(scale_rows2, tab2_scales)
-        words1 = [load_words(SHARED_C, tab_words, 0)]
-        wm_raw = held(SHARED_D, [P, PASSES, 2 * H], U8)
+        wm_raw = held("wm_raw", [P, PASSES, 2 * H], U8)
         nc.sync.dma_start(wm_raw[:].bitcast(I32), wm_words.rearrange("a p c -> p a c").bitcast(I32))
         for d in range(4):
             nc.sync.dma_start(
                 wm_scale_rows[32 * d : 32 * d + 4, :].bitcast(I32).rearrange("i (a c) -> i a c", a=PASSES),
                 wm_scales[:, 4 * d : 4 * d + 4, :].rearrange("a i c -> i a c").bitcast(I32),
             )
-        wb_raw = [load_wb("wb_raw0", 0, 0, H), load_wb("wb_raw1", 1, 0, H // 2)]
+        wb_raw = [load_wb("wb_first", 0, 0, H)]
 
         gather_scales("picked1", scale_rows1, lists, planes1)
-        words1.append(load_words(SHARED_A, tab_words, 1))
+        words1.append(load_words("tab_second", tab_words, 1))
+        wb_raw.append(load_wb("wb_middle", 1, 0, H // 2))
         first_pass = held("anchors0", [P, S], U32)
         nc.vector.tensor_copy(first_pass[:], words1[0][:].bitcast(U32).indirect(lists[:]))
-        wb_raw.append(load_wb(SHARED_C, 1, H // 2, H // 2))
+
+        words2 = [load_words("tab2_first", tab2_words, 0)]
 
         wm_codes = held("wm_codes", [P, PASSES * 2 * H], U8)
-        nc.vector.tensor_copy(
-            wm_codes[:].bitcast(I32).rearrange("p (a t i w) -> p a t i w", a=PASSES, t=4, w=4),
-            wm_raw[:].bitcast(I32).rearrange("p a (i t w) -> p a t i w", t=4, w=4),
+        nc.scalar.copy(
+            wm_codes[:].bitcast(U32).rearrange("p (a t i w) -> p a t i w", a=PASSES, t=4, w=4),
+            wm_raw[:].bitcast(U32).rearrange("p a (i t w) -> p a t i w", t=4, w=4),
         )
-        words2 = [load_words(SHARED_D, tab2_words, 0)]
         wm_planes = held("wm_planes", [P, PASSES * H], U8)
-        nc.vector.tensor_copy(
-            wm_planes[:].bitcast(I32).rearrange("p (a t i w) -> p a t i w", a=PASSES, t=4, w=2),
-            wm_scale_rows[:].bitcast(I32).rearrange("p (a i t w) -> p a t i w", a=PASSES, t=4, w=2),
+        nc.scalar.copy(
+            wm_planes[:].bitcast(U32).rearrange("p (a t i w) -> p a t i w", a=PASSES, t=4, w=2),
+            wm_scale_rows[:].bitcast(U32).rearrange("p (a i t w) -> p a t i w", a=PASSES, t=4, w=2),
         )
 
         gather_scales("picked2", scale_rows2, list2, planes2)
-        words2.append(load_words(SHARED_B, tab2_words, 1))
 
         wb_woven = [held("wb_woven%d" % a, [P, H * 4], BF16) for a in range(PASSES)]
-        for a, c0, width, raw in wb_raw:
+
+        def weave_wb(a, c0, width, raw):
             dealt = wb_woven[a][:].rearrange("p (t i g n k) -> p g i t k n", t=4, g=2, n=4, k=4)
             for g in range(2):
                 nc.scalar.copy(
                     dealt[:, g, c0 // 32 : (c0 + width) // 32],
                     raw[:].rearrange("p k (i t g n) -> p g i t k n", t=4, g=2, n=4)[:, g],
                 )
+
+        weave_wb(*wb_raw[0])
+        weave_wb(*wb_raw[1])
+        wb_raw.append(load_wb("wb_last", 1, H // 2, H // 2))
+        words2.append(load_words("tab2_second", tab2_words, 1))
+        weave_wb(*wb_raw[2])
 
         dwells = held("dwells", [P, 8, 2, 64], F32)
         for u in range(2):
@@ -164,11 +194,11 @@ def tile_list_chromatin_loop_map_kernel(
                 out=wb_codes[a][:].bitcast(FP8X4), scales=wb_scales[:, H * a : H * (a + 1)], in_=wb_woven[a][:]
             )
 
-        def motif_gather(a, half):
-            picked = held("motifs%d_%d" % (a, half), [P, PASS], U32)
-            offsets = list2[:, PASS * half // 16 : PASS * (half + 1) // 16]
+        def motif_gather(a, m0, width):
+            picked = held("motifs%d_%d" % (a, m0), [P, width], U32)
+            offsets = list2[:, m0 // 16 : (m0 + width) // 16]
             nc.vector.tensor_copy(picked[:], words2[a][:].bitcast(U32).indirect(offsets))
-            return picked
+            return [picked[:, j : j + P] for j in range(0, width, P)]
 
         b_codes = held("b_codes", [P, S], U32)
         b_scales = held("b_scales", [P, S], U8)
@@ -187,7 +217,7 @@ def tile_list_chromatin_loop_map_kernel(
                         out=banks[n][:, P * t : P * (t + 1)],
                         lhsT=wb_codes[a][:, P * t : P * (t + 1)].bitcast(FP8X4),
                         lhsT_scale=wb_scales[:, H * a + P * t : H * a + P * (t + 1)],
-                        rhs=picked[a][:, P * n : P * (n + 1)].bitcast(FP8X4),
+                        rhs=picked[a][4 * half + n].bitcast(FP8X4),
                         rhs_scale=planes2[:, S * a + m0 : S * a + m0 + P],
                         start=(a == 0 and t == 0),
                         stop=(a == PASSES - 1 and t == 3),
@@ -236,7 +266,7 @@ def tile_list_chromatin_loop_map_kernel(
             )
 
         h_scales = held("h_scales", [P, S], U8)
-        h_woven = held(SHARED_C, [P, S, 4], BF16)
+        h_woven = [held("h_woven%d" % half, [P, S // 2, 4], BF16) for half in range(2)]
 
         def anchor_passes(a, bank, j, picked):
             for t in range(4):
@@ -258,7 +288,7 @@ def tile_list_chromatin_loop_map_kernel(
             for n, bank in enumerate(banks):
                 j = j0 + P * n
                 anchor_passes(1, bank, j, picked[:, P * n : P * (n + 1)])
-                nc.scalar.copy(h_woven[:, j : j + P, :], bank[:].rearrange("p (t c) -> p c t", t=4))
+                nc.scalar.copy(h_woven[j // PASS][:, j % PASS : j % PASS + P, :], bank[:].rearrange("p (t c) -> p c t", t=4))
 
         starts = [sum(ROUNDS[:r]) for r in range(len(ROUNDS))]
 
@@ -337,9 +367,9 @@ def tile_list_chromatin_loop_map_kernel(
             anchor_passes(0, bank, P * n, first_pass[:, P * n : P * (n + 1)])
         for j0 in range(0, S, ANCHORS):
             anchor_second_pass(j0, h_banks[j0 // P : (j0 + ANCHORS) // P])
-        quantise_wb(1, SHARED_A)
+        first_motifs = motif_gather(0, 0, PASS) + motif_gather(0, PASS, PASS)
+        quantise_wb(1, "wb_codes1")
 
-        motifs = [[motif_gather(a, half) for half in range(2)] for a in range(PASSES)]
         h_codes = {}
 
         def quantise_h(codes, j0):
@@ -347,13 +377,14 @@ def tile_list_chromatin_loop_map_kernel(
             nc.vector.quantize_mx(
                 out=codes.bitcast(FP8X4),
                 scales=h_scales[:, j0 : j0 + width],
-                in_=h_woven[:, j0 : j0 + width, :].rearrange("p c t -> p (c t)"),
+                in_=h_woven[j0 // PASS][:].rearrange("p c t -> p (c t)"),
             )
             for j in range(0, width, P):
                 h_codes[j0 + j] = codes[:, j : j + P]
 
-        quantise_h(held(SHARED_B, [P, S // 2], U32)[:], 0)
-        c_pairs = [motif_stage(half, [motifs[a][half] for a in range(PASSES)]) for half in range(2)]
+        motifs = [first_motifs, motif_gather(1, 0, 256) + motif_gather(1, 256, 256) + motif_gather(1, PASS, PASS)]
+        quantise_h(held("h_codes0", [P, S // 2], U32)[:], 0)
+        c_pairs = [motif_stage(half, motifs) for half in range(2)]
         quantise_h(held(SHARED_E, [P, S // 2], U32)[:], S // 2)
 
         sigs = [[sigmoids(0, 0)]]

@@ -38,11 +38,13 @@ PLACES = {
     "h_woven0": 8 * KIB,
     "tab_first": 12 * KIB,
     "tab2_first": 12 * KIB,
-    "h_codes0": 24 * KIB,
+    "h_codes0": 12 * KIB,
     "wb_first": 20 * KIB,
     "wb_last": 20 * KIB,
     "h_woven1": 20 * KIB,
     "tab2_second": 24 * KIB,
+    "occs": 28 * KIB,
+    "gains": 29 * KIB,
 }
 
 SHARED_A = "shared_a"
@@ -85,7 +87,7 @@ def tile_list_chromatin_loop_map_kernel(
         dwell_rows = held("dwell_rows", [P, 8], F32)
 
         warm = held("warm", [P, 2], F32)
-        nc.gpsimd.memset(scale_rows1[:].bitcast(I32), 0)
+        nc.vector.memset(scale_rows1[:].bitcast(I32), 0)
         nc.vector.memset(warm[:, 0:1], 0.0)
         nc.vector.memset(scale_rows2[:].bitcast(I32), 0)
         nc.vector.memset(wm_scale_rows[:].bitcast(I32), 0)
@@ -115,19 +117,15 @@ def tile_list_chromatin_loop_map_kernel(
                 )
 
         nc.gpsimd.dma_start(dwell_rows[:], dwell.rearrange("(n c) -> n c", c=8))
-        occs = held("occs", [P, 2, 4], F32)
-        gains = held("gains", [P, 4], F32)
         make_identity(nc, ident[:])
-        nc.gpsimd.dma_start(occs[:], occ.rearrange("(h p t) -> p h t", h=2, t=4))
-        nc.gpsimd.dma_start(gains[:], gain.rearrange("(q r) -> q r", r=4))
 
         nc.sync.dma_start(lists[:], offs)
         nc.sync.dma_start(list2[:], offs2)
+        wm_raw = held("wm_raw", [P, PASSES, 2 * H], U8)
+        nc.sync.dma_start(wm_raw[:].bitcast(I32), wm_words.rearrange("a p c -> p a c").bitcast(I32))
         load_scale_rows(scale_rows1, tab_scales)
         words1 = [load_words("tab_first", tab_words, 0)]
         load_scale_rows(scale_rows2, tab2_scales)
-        wm_raw = held("wm_raw", [P, PASSES, 2 * H], U8)
-        nc.sync.dma_start(wm_raw[:].bitcast(I32), wm_words.rearrange("a p c -> p a c").bitcast(I32))
         for d in range(4):
             nc.sync.dma_start(
                 wm_scale_rows[32 * d : 32 * d + 4, :].bitcast(I32).rearrange("i (a c) -> i a c", a=PASSES),
@@ -368,7 +366,6 @@ def tile_list_chromatin_loop_map_kernel(
         for j0 in range(0, S, ANCHORS):
             anchor_second_pass(j0, h_banks[j0 // P : (j0 + ANCHORS) // P])
         first_motifs = motif_gather(0, 0, PASS) + motif_gather(0, PASS, PASS)
-        quantise_wb(1, "wb_codes1")
 
         h_codes = {}
 
@@ -382,8 +379,13 @@ def tile_list_chromatin_loop_map_kernel(
             for j in range(0, width, P):
                 h_codes[j0 + j] = codes[:, j : j + P]
 
-        motifs = [first_motifs, motif_gather(1, 0, 256) + motif_gather(1, 256, 256) + motif_gather(1, PASS, PASS)]
         quantise_h(held("h_codes0", [P, S // 2], U32)[:], 0)
+        quantise_wb(1, "wb_codes1")
+        motifs = [first_motifs, motif_gather(1, 0, 256) + motif_gather(1, 256, 256) + motif_gather(1, PASS, PASS)]
+        occs = held("occs", [P, 2, 4], F32)
+        gains = held("gains", [P, 4], F32)
+        nc.sync.dma_start(occs[:], occ.rearrange("(h p t) -> p h t", h=2, t=4))
+        nc.sync.dma_start(gains[:], gain.rearrange("(q r) -> q r", r=4))
         c_pairs = [motif_stage(half, motifs) for half in range(2)]
         quantise_h(held(SHARED_E, [P, S // 2], U32)[:], S // 2)
 

@@ -38,7 +38,6 @@ PLACES = {
     "h_woven0": 8 * KIB,
     "tab_first": 12 * KIB,
     "tab2_first": 12 * KIB,
-    "h_codes0": 12 * KIB,
     "wb_first": 20 * KIB,
     "wb_last": 20 * KIB,
     "h_woven1": 20 * KIB,

@@ -22,11 +22,13 @@ PASSES = 2
 PASS = 512
 BANKS = 8
 ANCHORS = 256
+MOTIF_GATHERS = [[512, 512], [256, 256, 512]]
 ROUNDS = [256, 256, 256, 128, 128]
 SCORE_BANKS = [[[0, 1], [4, 5]], [[6, 7], [4, 5]], [[6, 7], [0, 1]], [[2], [3]], [[6], [7]]]
 RESULT_BANKS = [[4, 5], [0, 1], [4, 5], [2, 3], [6, 7]]
 TURN_BANKS = [[2, 3], [0, 1]]
 DWELL_BANKS = [6, 7]
+EARLY_BANKS = 6
 LOOP_BUFS = 3
 
 KIB = 1024
@@ -45,12 +47,7 @@ PLACES = {
     "occs": 28 * KIB,
     "gains": 29 * KIB,
 }
-
-SHARED_A = "shared_a"
-SHARED_B = "shared_b"
-SHARED_C = "shared_c"
-SHARED_D = "shared_d"
-SHARED_E = "shared_e"
+SHARED = "shared_e"
 
 
 def tile_list_chromatin_loop_map_kernel(
@@ -65,19 +62,16 @@ def tile_list_chromatin_loop_map_kernel(
         def take_bank(number):
             return psum.tile([P, 512], F32, name="bank%d" % number)
 
+        reused = ctx.enter_context(tc.tile_pool(name="reused", bufs=1))
+
         def held(tag, shape, dtype):
             if tag in PLACES:
-                return placed(tag, shape, dtype)
+                return reused.tile(shape, dtype, name=tag, align_bytes=64, offset=PLACES[tag])
             return keep.tile(shape, dtype, name=tag, align_bytes=64)
-
-        arena = ctx.enter_context(tc.tile_pool(name="arena", bufs=1))
-
-        def placed(name, shape, dtype):
-            return arena.tile(shape, dtype, name=name, align_bytes=64, offset=PLACES[name])
 
         lists = held("lists", [P, S // 16], U16)
         list2 = held("list2", [P, S // 16], U16)
-        scale_rows1 = placed("scale_rows1", [P, T], U8)
+        scale_rows1 = held("scale_rows1", [P, T], U8)
         scale_rows2 = held("scale_rows2", [P, T], U8)
         planes1 = held("planes1", [P, PASSES * S], U8)
         planes2 = held("planes2", [P, PASSES * S], U8)
@@ -191,11 +185,15 @@ def tile_list_chromatin_loop_map_kernel(
                 out=wb_codes[a][:].bitcast(FP8X4), scales=wb_scales[:, H * a : H * (a + 1)], in_=wb_woven[a][:]
             )
 
-        def motif_gather(a, m0, width):
-            picked = held("motifs%d_%d" % (a, m0), [P, width], U32)
-            offsets = list2[:, m0 // 16 : (m0 + width) // 16]
-            nc.vector.tensor_copy(picked[:], words2[a][:].bitcast(U32).indirect(offsets))
-            return [picked[:, j : j + P] for j in range(0, width, P)]
+        def motif_gathers(a):
+            slices = []
+            for width in MOTIF_GATHERS[a]:
+                m0 = P * len(slices)
+                picked = held("motifs%d_%d" % (a, m0), [P, width], U32)
+                offsets = list2[:, m0 // 16 : (m0 + width) // 16]
+                nc.vector.tensor_copy(picked[:], words2[a][:].bitcast(U32).indirect(offsets))
+                slices.extend([picked[:, j : j + P] for j in range(0, width, P)])
+            return slices
 
         b_codes = held("b_codes", [P, S], U32)
         b_scales = held("b_scales", [P, S], U8)
@@ -203,11 +201,11 @@ def tile_list_chromatin_loop_map_kernel(
         c_scales = held("c_scales", [P, 2 * H], U8)
 
         def motif_stage(half, picked):
-            b_woven = held(SHARED_E if half == 1 else "b_woven0", [P, 4, P, 4], BF16)
+            b_woven = held(SHARED if half == 1 else "b_woven0", [P, 4, P, 4], BF16)
             c_pairs = held("c_pairs%d" % half, [P, 2, 4, 256], BF16)
             banks = [take_bank(4 * half + n) for n in range(4)]
 
-            def passes(a, n):
+            def passes(a, n, first):
                 m0 = PASS * half + P * n
                 for t in range(4):
                     nc.tensor.matmul_mx(
@@ -216,14 +214,17 @@ def tile_list_chromatin_loop_map_kernel(
                         lhsT_scale=wb_scales[:, H * a + P * t : H * a + P * (t + 1)],
                         rhs=picked[a][4 * half + n].bitcast(FP8X4),
                         rhs_scale=planes2[:, S * a + m0 : S * a + m0 + P],
-                        start=(a == 0 and t == 0),
-                        stop=(a == PASSES - 1 and t == 3),
+                        start=(first and t == 0),
+                        stop=(not first and t == 3),
                     )
 
+            early = [n for n in range(4) if 4 * half + n < EARLY_BANKS]
+            for n in early:
+                passes(0, n, True)
             for n in range(4):
-                passes(0, n)
-            for n in range(4):
-                passes(1, n)
+                passes(1, n, n not in early)
+                if n not in early:
+                    passes(0, n, False)
                 nc.scalar.copy(
                     b_woven[:, :, 32 * n : 32 * (n + 1), :], banks[n][:].rearrange("p (t q v) -> p v q t", t=4, v=4)
                 )
@@ -285,7 +286,9 @@ def tile_list_chromatin_loop_map_kernel(
             for n, bank in enumerate(banks):
                 j = j0 + P * n
                 anchor_passes(1, bank, j, picked[:, P * n : P * (n + 1)])
-                nc.scalar.copy(h_woven[j // PASS][:, j % PASS : j % PASS + P, :], bank[:].rearrange("p (t c) -> p c t", t=4))
+                nc.scalar.copy(
+                    h_woven[j // PASS][:, j % PASS : j % PASS + P, :], bank[:].rearrange("p (t c) -> p c t", t=4)
+                )
 
         starts = [sum(ROUNDS[:r]) for r in range(len(ROUNDS))]
 
@@ -364,7 +367,7 @@ def tile_list_chromatin_loop_map_kernel(
             anchor_passes(0, bank, P * n, first_pass[:, P * n : P * (n + 1)])
         for j0 in range(0, S, ANCHORS):
             anchor_second_pass(j0, h_banks[j0 // P : (j0 + ANCHORS) // P])
-        first_motifs = motif_gather(0, 0, PASS) + motif_gather(0, PASS, PASS)
+        motifs = [motif_gathers(0)]
 
         h_codes = {}
 
@@ -380,13 +383,13 @@ def tile_list_chromatin_loop_map_kernel(
 
         quantise_h(held("h_codes0", [P, S // 2], U32)[:], 0)
         quantise_wb(1, "wb_codes1")
-        motifs = [first_motifs, motif_gather(1, 0, 256) + motif_gather(1, 256, 256) + motif_gather(1, PASS, PASS)]
+        motifs.append(motif_gathers(1))
         occs = held("occs", [P, 2, 4], F32)
         gains = held("gains", [P, 4], F32)
         nc.sync.dma_start(occs[:], occ.rearrange("(h p t) -> p h t", h=2, t=4))
         nc.sync.dma_start(gains[:], gain.rearrange("(q r) -> q r", r=4))
         c_pairs = [motif_stage(half, motifs) for half in range(2)]
-        quantise_h(held(SHARED_E, [P, S // 2], U32)[:], S // 2)
+        quantise_h(held(SHARED, [P, S // 2], U32)[:], S // 2)
 
         sigs = [[sigmoids(0, 0)]]
         quantise_c(0, turn_c(0, c_pairs[0]))

@@ -22,7 +22,7 @@ PASSES = 2
 PASS = 512
 BANKS = 8
 ANCHORS = 256
-MOTIF_GATHERS = [[512, 512], [256, 256, 512]]
+MOTIF_GATHERS = [[1024], [256, 256, 512]]
 ROUNDS = [256, 256, 256, 128, 128]
 SCORE_BANKS = [[[0, 1], [4, 5]], [[6, 7], [4, 5]], [[6, 7], [0, 1]], [[2], [3]], [[6], [7]]]
 RESULT_BANKS = [[4, 5], [0, 1], [4, 5], [2, 3], [6, 7]]
@@ -35,19 +35,15 @@ KIB = 1024
 PLACES = {
     "scale_rows1": 7 * KIB,
     "tab_second": 0,
-    "wb_codes1": 0,
-    "wb_middle": 8 * KIB,
-    "h_woven0": 8 * KIB,
-    "tab_first": 12 * KIB,
-    "tab2_first": 12 * KIB,
-    "wb_first": 20 * KIB,
-    "wb_last": 20 * KIB,
-    "h_woven1": 20 * KIB,
-    "tab2_second": 24 * KIB,
-    "occs": 28 * KIB,
-    "gains": 29 * KIB,
+    "tab2_first": 8 * KIB,
+    "wb_first": 16 * KIB,
+    "wb_last": 16 * KIB,
+    "h_woven1": 16 * KIB,
+    "tab2_second": 20 * KIB,
+    "occs": 24 * KIB,
+    "gains": 25 * KIB,
 }
-SHARED = "shared_e"
+MOTIF_PLANE = 8
 
 
 def tile_list_chromatin_loop_map_kernel(
@@ -98,17 +94,6 @@ def tile_list_chromatin_loop_map_kernel(
             nc.sync.dma_start(raw[:], wb[PASS * a : PASS * (a + 1), c0 : c0 + width].rearrange("(p i) c -> p i c", i=4))
             return a, c0, width, raw
 
-        def load_scale_rows(window, scales):
-            nc.sync.dma_start(window[0:P:4, :].bitcast(I32), scales.rearrange("a q t -> q a t").bitcast(I32))
-
-        def gather_scales(tag, window, offsets, planes):
-            picked = held(tag, [P, S], U8)
-            nc.vector.tensor_copy(picked[:], window[:].indirect(offsets[:]))
-            for d in range(4):
-                nc.sync.dma_start(
-                    planes[32 * d : 32 * d + 4, :].bitcast(I32), picked[32 * d : 32 * d + 32 : 4, :].bitcast(I32)
-                )
-
         nc.gpsimd.dma_start(dwell_rows[:], dwell.rearrange("(n c) -> n c", c=8))
         make_identity(nc, ident[:])
 
@@ -116,23 +101,35 @@ def tile_list_chromatin_loop_map_kernel(
         nc.sync.dma_start(list2[:], offs2)
         wm_raw = held("wm_raw", [P, PASSES, 2 * H], U8)
         nc.sync.dma_start(wm_raw[:].bitcast(I32), wm_words.rearrange("a p c -> p a c").bitcast(I32))
-        load_scale_rows(scale_rows1, tab_scales)
+        nc.sync.dma_start(scale_rows1[0:P:4, :].bitcast(I32), tab_scales.rearrange("a q t -> q a t").bitcast(I32))
         words1 = [load_words("tab_first", tab_words, 0)]
-        load_scale_rows(scale_rows2, tab2_scales)
+        nc.sync.dma_start(scale_rows2[0:P:4, :].bitcast(I32), tab2_scales.rearrange("a q t -> q a t").bitcast(I32))
         for d in range(4):
             nc.sync.dma_start(
                 wm_scale_rows[32 * d : 32 * d + 4, :].bitcast(I32).rearrange("i (a c) -> i a c", a=PASSES),
                 wm_scales[:, 4 * d : 4 * d + 4, :].rearrange("a i c -> i a c").bitcast(I32),
             )
         wb_raw = [load_wb("wb_first", 0, 0, H)]
-
-        gather_scales("picked1", scale_rows1, lists, planes1)
-        words1.append(load_words("tab_second", tab_words, 1))
         wb_raw.append(load_wb("wb_middle", 1, 0, H // 2))
+
+        picked1 = held("picked1", [P, S], U8)
+        nc.vector.tensor_copy(picked1[:], scale_rows1[:].indirect(lists[:]))
+        for d in range(4):
+            nc.sync.dma_start(
+                planes1[32 * d : 32 * d + 4, :].bitcast(I32), picked1[32 * d : 32 * d + 32 : 4, :].bitcast(I32)
+            )
         first_pass = held("anchors0", [P, S], U32)
         nc.vector.tensor_copy(first_pass[:], words1[0][:].bitcast(U32).indirect(lists[:]))
 
+        words1.append(load_words("tab_second", tab_words, 1))
         words2 = [load_words("tab2_first", tab2_words, 0)]
+        picked2 = held("picked2", [P, S], U8)
+        nc.vector.tensor_copy(picked2[:], scale_rows2[:].indirect(list2[:]))
+        for d in range(4):
+            row = 32 * d + MOTIF_PLANE
+            nc.sync.dma_start(
+                planes2[row : row + 4, :].bitcast(I32), picked2[32 * d : 32 * d + 32 : 4, :].bitcast(I32)
+            )
 
         wm_codes = held("wm_codes", [P, PASSES * 2 * H], U8)
         nc.scalar.copy(
@@ -144,24 +141,21 @@ def tile_list_chromatin_loop_map_kernel(
             wm_planes[:].bitcast(U32).rearrange("p (a t i w) -> p a t i w", a=PASSES, t=4, w=2),
             wm_scale_rows[:].bitcast(U32).rearrange("p (a i t w) -> p a t i w", a=PASSES, t=4, w=2),
         )
-
-        gather_scales("picked2", scale_rows2, list2, planes2)
+        wb_raw.append(load_wb("wb_last", 1, H // 2, H // 2))
+        words2.append(load_words("tab2_second", tab2_words, 1))
 
         wb_woven = [held("wb_woven%d" % a, [P, H * 4], BF16) for a in range(PASSES)]
 
-        def weave_wb(a, c0, width, raw):
+        def weave_wb(copy, a, c0, width, raw):
             dealt = wb_woven[a][:].rearrange("p (t i g n k) -> p g i t k n", t=4, g=2, n=4, k=4)
             for g in range(2):
-                nc.scalar.copy(
+                copy(
                     dealt[:, g, c0 // 32 : (c0 + width) // 32],
                     raw[:].rearrange("p k (i t g n) -> p g i t k n", t=4, g=2, n=4)[:, g],
                 )
 
-        weave_wb(*wb_raw[0])
-        weave_wb(*wb_raw[1])
-        wb_raw.append(load_wb("wb_last", 1, H // 2, H // 2))
-        words2.append(load_words("tab2_second", tab2_words, 1))
-        weave_wb(*wb_raw[2])
+        for raw in wb_raw:
+            weave_wb(nc.scalar.copy, *raw)
 
         dwells = held("dwells", [P, 8, 2, 64], F32)
         for u in range(2):
@@ -201,7 +195,7 @@ def tile_list_chromatin_loop_map_kernel(
         c_scales = held("c_scales", [P, 2 * H], U8)
 
         def motif_stage(half, picked):
-            b_woven = held(SHARED if half == 1 else "b_woven0", [P, 4, P, 4], BF16)
+            b_woven = held("b_woven%d" % half, [P, 4, P, 4], BF16)
             c_pairs = held("c_pairs%d" % half, [P, 2, 4, 256], BF16)
             banks = [take_bank(4 * half + n) for n in range(4)]
 
@@ -213,7 +207,7 @@ def tile_list_chromatin_loop_map_kernel(
                         lhsT=wb_codes[a][:, P * t : P * (t + 1)].bitcast(FP8X4),
                         lhsT_scale=wb_scales[:, H * a + P * t : H * a + P * (t + 1)],
                         rhs=picked[a][4 * half + n].bitcast(FP8X4),
-                        rhs_scale=planes2[:, S * a + m0 : S * a + m0 + P],
+                        rhs_scale=planes2[MOTIF_PLANE:P, S * a + m0 : S * a + m0 + P],
                         start=(first and t == 0),
                         stop=(not first and t == 3),
                     )
@@ -361,8 +355,8 @@ def tile_list_chromatin_loop_map_kernel(
                     out.rearrange("(q w) j -> q w j", w=4)[:, tile0 : tile0 + 2, j0 : j0 + width], result[:]
                 )
 
-        quantise_wb(0, "wb_codes0")
         h_banks = [take_bank(n) for n in range(BANKS)]
+        quantise_wb(0, "wb_codes0")
         for n, bank in enumerate(h_banks):
             anchor_passes(0, bank, P * n, first_pass[:, P * n : P * (n + 1)])
         for j0 in range(0, S, ANCHORS):
@@ -384,12 +378,12 @@ def tile_list_chromatin_loop_map_kernel(
         quantise_h(held("h_codes0", [P, S // 2], U32)[:], 0)
         quantise_wb(1, "wb_codes1")
         motifs.append(motif_gathers(1))
+        quantise_h(held("h_codes1", [P, S // 2], U32)[:], S // 2)
         occs = held("occs", [P, 2, 4], F32)
         gains = held("gains", [P, 4], F32)
         nc.sync.dma_start(occs[:], occ.rearrange("(h p t) -> p h t", h=2, t=4))
         nc.sync.dma_start(gains[:], gain.rearrange("(q r) -> q r", r=4))
         c_pairs = [motif_stage(half, motifs) for half in range(2)]
-        quantise_h(held(SHARED, [P, S // 2], U32)[:], S // 2)
 
         sigs = [[sigmoids(0, 0)]]
         quantise_c(0, turn_c(0, c_pairs[0]))

@@ -22,7 +22,7 @@ PASSES = 2
 PASS = 512
 BANKS = 8
 ANCHORS = 256
-MOTIF_GATHERS = [[1024], [256, 256, 512]]
+MOTIF_GATHERS = [[512, 512], [256, 256, 512]]
 ROUNDS = [256, 256, 256, 128, 128]
 SCORE_BANKS = [[[0, 1], [4, 5]], [[6, 7], [4, 5]], [[6, 7], [0, 1]], [[2], [3]], [[6], [7]]]
 RESULT_BANKS = [[4, 5], [0, 1], [4, 5], [2, 3], [6, 7]]
@@ -43,6 +43,7 @@ PLACES = {
     "occs": 24 * KIB,
     "gains": 25 * KIB,
 }
+SHARED = "shared_e"
 MOTIF_PLANE = 8
 
 
@@ -195,7 +196,7 @@ def tile_list_chromatin_loop_map_kernel(
         c_scales = held("c_scales", [P, 2 * H], U8)
 
         def motif_stage(half, picked):
-            b_woven = held("b_woven%d" % half, [P, 4, P, 4], BF16)
+            b_woven = held(SHARED if half == 1 else "b_woven0", [P, 4, P, 4], BF16)
             c_pairs = held("c_pairs%d" % half, [P, 2, 4, 256], BF16)
             banks = [take_bank(4 * half + n) for n in range(4)]
 
@@ -378,12 +379,12 @@ def tile_list_chromatin_loop_map_kernel(
         quantise_h(held("h_codes0", [P, S // 2], U32)[:], 0)
         quantise_wb(1, "wb_codes1")
         motifs.append(motif_gathers(1))
-        quantise_h(held("h_codes1", [P, S // 2], U32)[:], S // 2)
         occs = held("occs", [P, 2, 4], F32)
         gains = held("gains", [P, 4], F32)
         nc.sync.dma_start(occs[:], occ.rearrange("(h p t) -> p h t", h=2, t=4))
         nc.sync.dma_start(gains[:], gain.rearrange("(q r) -> q r", r=4))
         c_pairs = [motif_stage(half, motifs) for half in range(2)]
+        quantise_h(held(SHARED, [P, S // 2], U32)[:], S // 2)
 
         sigs = [[sigmoids(0, 0)]]
         quantise_c(0, turn_c(0, c_pairs[0]))

@@ -24,12 +24,11 @@ BANKS = 8
 ANCHORS = 256
 MOTIF_GATHERS = [[512, 512], [256, 256, 512]]
 ROUNDS = [256, 256, 256, 128, 128]
-SCORE_BANKS = [[[0, 1], [4, 5]], [[6, 7], [4, 5]], [[6, 7], [0, 1]], [[2], [3]], [[6], [7]]]
-RESULT_BANKS = [[4, 5], [0, 1], [4, 5], [2, 3], [6, 7]]
-TURN_BANKS = [[2, 3], [0, 1]]
+SCORE_BANKS = [[[0, 1], [4, 5]], [[0, 1], [0, 1]], [[2, 3], [4, 5]], [[0], [1]], [[6], [7]]]
+RESULT_BANKS = [[2, 3], [4, 5], [0, 1], [6, 7], [2, 3, 4, 5]]
+TURN_BANKS = [[2, 3], [6, 7]]
 DWELL_BANKS = [6, 7]
 EARLY_BANKS = 6
-LOOP_BUFS = 3
 
 KIB = 1024
 PLACES = {
@@ -40,10 +39,10 @@ PLACES = {
     "wb_last": 16 * KIB,
     "h_woven1": 16 * KIB,
     "tab2_second": 20 * KIB,
-    "occs": 24 * KIB,
-    "gains": 25 * KIB,
+    "occs": 0,
+    "gains": 1 * KIB,
 }
-SHARED = "shared_e"
+SHARED = "shared"
 MOTIF_PLANE = 8
 
 
@@ -53,7 +52,6 @@ def tile_list_chromatin_loop_map_kernel(
     nc = tc.nc
     with ExitStack() as ctx:
         keep = ctx.enter_context(tc.tile_pool(name="keep", bufs=1))
-        ring = ctx.enter_context(tc.tile_pool(name="ring", bufs=LOOP_BUFS))
         psum = ctx.enter_context(tc.psum_pool(name="psum", bufs=1))
 
         def take_bank(number):
@@ -195,52 +193,58 @@ def tile_list_chromatin_loop_map_kernel(
         c_codes = held("c_codes", [P, 2 * H], U32)
         c_scales = held("c_scales", [P, 2 * H], U8)
 
-        def motif_stage(half, picked):
-            b_woven = held(SHARED if half == 1 else "b_woven0", [P, 4, P, 4], BF16)
-            c_pairs = held("c_pairs%d" % half, [P, 2, 4, 256], BF16)
-            banks = [take_bank(4 * half + n) for n in range(4)]
+        b_woven = [held(tag, [P, 4, P, 4], BF16) for tag in ("b_woven0", SHARED)]
+        c_pairs = [held("c_pairs%d" % half, [P, 2, 4, 256], BF16) for half in range(2)]
+        b_banks = {}
 
-            def passes(a, n, first):
-                m0 = PASS * half + P * n
-                for t in range(4):
-                    nc.tensor.matmul_mx(
-                        out=banks[n][:, P * t : P * (t + 1)],
-                        lhsT=wb_codes[a][:, P * t : P * (t + 1)].bitcast(FP8X4),
-                        lhsT_scale=wb_scales[:, H * a + P * t : H * a + P * (t + 1)],
-                        rhs=picked[a][4 * half + n].bitcast(FP8X4),
-                        rhs_scale=planes2[MOTIF_PLANE:P, S * a + m0 : S * a + m0 + P],
-                        start=(first and t == 0),
-                        stop=(not first and t == 3),
-                    )
-
-            early = [n for n in range(4) if 4 * half + n < EARLY_BANKS]
-            for n in early:
-                passes(0, n, True)
-            for n in range(4):
-                passes(1, n, n not in early)
-                if n not in early:
-                    passes(0, n, False)
-                nc.scalar.copy(
-                    b_woven[:, :, 32 * n : 32 * (n + 1), :], banks[n][:].rearrange("p (t q v) -> p v q t", t=4, v=4)
+        def motif_passes(a, number, first):
+            if first:
+                b_banks[number] = take_bank(number)
+            m0 = P * number
+            for t in range(4):
+                nc.tensor.matmul_mx(
+                    out=b_banks[number][:, P * t : P * (t + 1)],
+                    lhsT=wb_codes[a][:, P * t : P * (t + 1)].bitcast(FP8X4),
+                    lhsT_scale=wb_scales[:, H * a + P * t : H * a + P * (t + 1)],
+                    rhs=motifs[a][number].bitcast(FP8X4),
+                    rhs_scale=planes2[MOTIF_PLANE:P, S * a + m0 : S * a + m0 + P],
+                    start=(first and t == 0),
+                    stop=(not first and t == 3),
                 )
+
+        def finish_b(number):
+            late = number >= EARLY_BANKS
+            motif_passes(1, number, late)
+            if late:
+                motif_passes(0, number, False)
+
+        def weave_b(number):
+            half, n = divmod(number, 4)
+            nc.scalar.copy(
+                b_woven[half][:, :, 32 * n : 32 * (n + 1), :],
+                b_banks[number][:].rearrange("p (t q v) -> p v q t", t=4, v=4),
+            )
+
+        def quantise_b(half):
             nc.vector.quantize_mx(
                 out=b_codes[:, PASS * half : PASS * (half + 1)].bitcast(FP8X4),
                 scales=b_scales[:, PASS * half : PASS * (half + 1)],
-                in_=b_woven[:].rearrange("p v q t -> p (v q t)"),
+                in_=b_woven[half][:].rearrange("p v q t -> p (v q t)"),
             )
-            for n in range(4):
-                factors = dwells[:, 4 * half + n, :, :].unsqueeze(2).to_broadcast([P, 2, 4, 64])
-                nc.vector.tensor_tensor(
-                    c_pairs[:, :, :, 64 * n : 64 * (n + 1)].rearrange("p u t (q e) -> p u t q e", e=2),
-                    banks[n][:].rearrange("p (t q u e) -> p u t q e", t=4, u=2, e=2),
-                    factors.rearrange("p u t (q e) -> p u t q e", e=2),
-                    MULT,
-                )
-            return c_pairs
 
-        def turn_c(half, c_pairs):
+        def dwell_product(number):
+            half, n = divmod(number, 4)
+            factors = dwells[:, number, :, :].unsqueeze(2).to_broadcast([P, 2, 4, 64])
+            nc.vector.tensor_tensor(
+                c_pairs[half][:, :, :, 64 * n : 64 * (n + 1)].rearrange("p u t (q e) -> p u t q e", e=2),
+                b_banks[number][:].rearrange("p (t q u e) -> p u t q e", t=4, u=2, e=2),
+                factors.rearrange("p u t (q e) -> p u t q e", e=2),
+                MULT,
+            )
+
+        def turn_c(half, copies):
             c_woven = held("c_woven%d" % half, [P, H * 4], BF16)
-            pairs = c_pairs[:].bitcast(F32)
+            pairs = c_pairs[half][:].bitcast(F32)
             dealt = c_woven[:].bitcast(F32).rearrange("p (w i g x y u) -> p g w x i y u", w=4, g=2, x=2, y=2, u=2)
             for g, number in enumerate(TURN_BANKS[half]):
                 bank = take_bank(number)
@@ -248,7 +252,7 @@ def tile_list_chromatin_loop_map_kernel(
                     for x in range(2):
                         col = P * (2 * u + x)
                         nc.tensor.transpose(bank[:, col : col + P], pairs[:, u, 2 * g + x, :], ident[:])
-                nc.scalar.copy(dealt[:, g], bank[:].rearrange("p (u x i y w) -> p w x i y u", u=2, x=2, y=2, w=4))
+                copies[g](dealt[:, g], bank[:].rearrange("p (u x i y w) -> p w x i y u", u=2, x=2, y=2, w=4))
             return c_woven
 
         def quantise_c(half, c_woven):
@@ -304,54 +308,52 @@ def tile_list_chromatin_loop_map_kernel(
                         stop=True,
                     )
                 nc.scalar.activation(sig[:, j : j + P, :], bank[:].rearrange("p (t c) -> p c t", t=4), ACT.Sigmoid)
-            return sig
+            sigs[r, half] = sig
 
-        def occ_product(width, half, sig):
-            woven = ring.tile([P, width, 4], BF16, name="loop_woven", align_bytes=64)
-            nc.vector.tensor_tensor(woven[:], sig[:], occs[:, half : half + 1, :].to_broadcast([P, width, 4]), MULT)
-            return woven
-
-        def loop_quantise(j0, width, half, woven):
-            codes = held("loop_codes%d_%d" % (j0, half), [P, width], U32)
-            scales = held("loop_scales%d_%d" % (j0, half), [P, width], U8)
-            nc.vector.quantize_mx(
-                out=codes[:].bitcast(FP8X4), scales=scales[:], in_=woven[:].rearrange("p c t -> p (c t)")
+        def occ_product(r, half):
+            width = ROUNDS[r]
+            woven = held("loop_woven%d_%d" % (r, half), [P, width, 4], BF16)
+            nc.vector.tensor_tensor(
+                woven[:], sigs[r, half][:], occs[:, half : half + 1, :].to_broadcast([P, width, 4]), MULT
             )
-            return codes, scales
+            loop_woven[r, half] = woven
 
-        def read_back(r, loop):
+        def loop_quantise(r, half):
+            width = ROUNDS[r]
+            codes = held("loop_codes%d_%d" % (r, half), [P, width], U32)
+            scales = held("loop_scales%d_%d" % (r, half), [P, width], U8)
+            nc.vector.quantize_mx(
+                out=codes[:].bitcast(FP8X4), scales=scales[:], in_=loop_woven[r, half][:].rearrange("p c t -> p (c t)")
+            )
+            loop_mx[r, half] = codes, scales
+
+        def read_back(r):
             j0, width = starts[r], ROUNDS[r]
+            loop = [loop_mx[r, half] for half in range(2)]
             banks = [take_bank(number) for number in RESULT_BANKS[r]]
+            shared = 4 // len(banks)
             for half in range(2):
                 for tile in range(4):
                     cols = slice(H * half + P * tile, H * half + P * (tile + 1))
+                    n = tile % shared
                     nc.tensor.matmul_mx(
-                        out=banks[tile // 2][:, width * (tile % 2) : width * (tile % 2 + 1)],
+                        out=banks[tile // shared][:, width * n : width * (n + 1)],
                         lhsT=c_codes[:, cols].bitcast(FP8X4),
                         lhsT_scale=c_scales[:, cols],
                         rhs=loop[half][0][:].bitcast(FP8X4),
                         rhs_scale=loop[half][1][:],
-                        start=(half == 0 and tile % 2 == 0),
-                        stop=(half == 1 and tile % 2 == 1),
+                        start=(half == 0 and n == 0),
+                        stop=(half == 1 and n == shared - 1),
                     )
             for tile0 in (0, 2):
-                bank = banks[tile0 // 2]
                 result = held("result%d_%d" % (r, tile0), [P, 2, width], F32)
-                if j0 + width == S and tile0 == 0:
-                    nc.vector.tensor_tensor(
-                        result[:],
-                        bank[:, 0 : 2 * width].rearrange("p (w c) -> p w c", w=2),
-                        gains[:, tile0 : tile0 + 2].unsqueeze(2).to_broadcast([P, 2, width]),
-                        MULT,
-                    )
-                else:
-                    for n in range(2):
-                        nc.scalar.activation(
-                            result[:, n, :],
-                            bank[:, width * n : width * (n + 1)],
-                            ACT.Copy,
-                            scale=gains[:, tile0 + n : tile0 + n + 1],
-                        )
+                for n in range(2):
+                    tile = tile0 + n
+                    sums = banks[tile // shared][:, width * (tile % shared) : width * (tile % shared + 1)]
+                    if j0 + width == S and n == 1:
+                        nc.vector.tensor_scalar(result[:, n, :], sums, gains[:, tile : tile + 1], None, MULT)
+                    else:
+                        nc.scalar.activation(result[:, n, :], sums, ACT.Copy, scale=gains[:, tile : tile + 1])
                 nc.sync.dma_start(
                     out.rearrange("(q w) j -> q w j", w=4)[:, tile0 : tile0 + 2, j0 : j0 + width], result[:]
                 )
@@ -382,20 +384,63 @@ def tile_list_chromatin_loop_map_kernel(
         occs = held("occs", [P, 2, 4], F32)
         gains = held("gains", [P, 4], F32)
         nc.sync.dma_start(occs[:], occ.rearrange("(h p t) -> p h t", h=2, t=4))
+        occ_run = held("occ_run", [P, 64, 4], F32)
+        nc.scalar.copy(occ_run[:], occs[:, 0:1, :].to_broadcast([P, 64, 4]))
         nc.sync.dma_start(gains[:], gain.rearrange("(q r) -> q r", r=4))
-        c_pairs = [motif_stage(half, motifs) for half in range(2)]
-        quantise_h(held(SHARED, [P, S // 2], U32)[:], S // 2)
+        sigs, loop_woven, loop_mx = {}, {}, {}
 
-        sigs = [[sigmoids(0, 0)]]
-        quantise_c(0, turn_c(0, c_pairs[0]))
-        sigs[0].append(sigmoids(0, 1))
-        sigs.append([sigmoids(1, 0)])
-        c_woven = turn_c(1, c_pairs[1])
-        sigs[1].append(sigmoids(1, 1))
-        for r in range(2, len(ROUNDS)):
-            sigs.append([sigmoids(r, half) for half in range(2)])
-        for r, width in enumerate(ROUNDS):
-            woven = [occ_product(width, half, sigs[r][half]) for half in range(2)]
-            if r == 0:
-                quantise_c(1, c_woven)
-            read_back(r, [loop_quantise(starts[r], width, half, woven[half]) for half in range(2)])
+        for number in range(EARLY_BANKS):
+            motif_passes(0, number, True)
+        for number in range(4):
+            finish_b(number)
+            weave_b(number)
+        quantise_b(0)
+        for number in range(4):
+            dwell_product(number)
+        for number in range(4, 8):
+            finish_b(number)
+        weave_b(4)
+        weave_b(5)
+        sigmoids(0, 0)
+        weave_b(6)
+        weave_b(7)
+        for number in range(4, 8):
+            dwell_product(number)
+
+        first_woven = held("loop_woven0_0", [P, ROUNDS[0], 4], BF16)
+        nc.gpsimd.tensor_tensor(
+            first_woven[:, 0:P, :].rearrange("p (n c) t -> p n (c t)", c=64),
+            sigs[0, 0][:, 0:P, :].rearrange("p (n c) t -> p n (c t)", c=64),
+            occ_run[:].rearrange("p c t -> p (c t)").unsqueeze(1).to_broadcast([P, P // 64, 256]),
+            MULT,
+        )
+        loop_woven[0, 0] = first_woven
+
+        quantise_b(1)
+        nc.vector.tensor_tensor(
+            first_woven[:, P:, :], sigs[0, 0][:, P:, :], occs[:, 0:1, :].to_broadcast([P, P, 4]), MULT
+        )
+        quantise_h(held(SHARED, [P, S // 2], U32)[:], S // 2)
+        sigmoids(1, 0)
+        c_woven = [turn_c(0, [nc.scalar.copy, nc.scalar.copy])]
+        sigmoids(0, 1)
+        sigmoids(1, 1)
+        c_woven.append(turn_c(1, [nc.scalar.copy, nc.scalar.copy]))
+        sigmoids(2, 0)
+        sigmoids(2, 1)
+        for r in (3, 4):
+            sigmoids(r, 0)
+            sigmoids(r, 1)
+
+        units = [(1, 0), (0, 1), (1, 1), (2, 0), (2, 1), (3, 0), (3, 1), (4, 0), (4, 1)]
+        occ_product(*units[0])
+        quantise_c(0, c_woven[0])
+        loop_quantise(0, 0)
+        for n, (r, half) in enumerate(units):
+            if n + 1 < len(units):
+                occ_product(*units[n + 1])
+            loop_quantise(r, half)
+            if (r, half) == (0, 1):
+                quantise_c(1, c_woven[1])
+            if half == 1:
+                read_back(r)

@@ -24,9 +24,10 @@ BANKS = 8
 ANCHORS = 256
 MOTIF_GATHERS = [[512, 512], [256, 256, 512]]
 ROUNDS = [256, 256, 256, 128, 128]
-SCORE_BANKS = [[[0, 1], [4, 5]], [[0, 1], [0, 1]], [[2, 3], [4, 5]], [[0], [1]], [[6], [7]]]
-RESULT_BANKS = [[2, 3], [4, 5], [0, 1], [6, 7], [2, 3, 4, 5]]
-TURN_BANKS = [[2, 3], [6, 7]]
+SCORE_BANKS = [[[0, 1], [0, 1]], [[2, 3], [2, 3]], [[7, 2], [3, 4]], [[5], [0]], [[1], [7]]]
+RESULT_BANKS = [[1, 7], [2, 3], [4, 5], [1, 7], [0, 6, 2, 3]]
+OCC_BANK = 6
+TURN_BANKS = [[4, 5], [0, 1]]
 DWELL_BANKS = [6, 7]
 EARLY_BANKS = 6
 
@@ -38,6 +39,9 @@ PLACES = {
     "wb_first": 16 * KIB,
     "wb_last": 16 * KIB,
     "h_woven1": 16 * KIB,
+    "sig1_0": 35 * KIB,
+    "c_codes": 32 * KIB,
+    "loop_codes0": 36 * KIB,
     "tab2_second": 20 * KIB,
     "occs": 0,
     "gains": 1 * KIB,
@@ -242,24 +246,26 @@ def tile_list_chromatin_loop_map_kernel(
                 MULT,
             )
 
-        def turn_c(half, copies):
-            c_woven = held("c_woven%d" % half, [P, H * 4], BF16)
-            pairs = c_pairs[half][:].bitcast(F32)
-            dealt = c_woven[:].bitcast(F32).rearrange("p (w i g x y u) -> p g w x i y u", w=4, g=2, x=2, y=2, u=2)
-            for g, number in enumerate(TURN_BANKS[half]):
-                bank = take_bank(number)
-                for u in range(2):
-                    for x in range(2):
-                        col = P * (2 * u + x)
-                        nc.tensor.transpose(bank[:, col : col + P], pairs[:, u, 2 * g + x, :], ident[:])
-                copies[g](dealt[:, g], bank[:].rearrange("p (u x i y w) -> p w x i y u", u=2, x=2, y=2, w=4))
-            return c_woven
+        c_woven = [held("c_woven%d" % half, [P, H * 4], BF16) for half in range(2)]
 
-        def quantise_c(half, c_woven):
+        def turn_c(half, g):
+            pairs = c_pairs[half][:].bitcast(F32)
+            bank = take_bank(TURN_BANKS[half][g])
+            for u in range(2):
+                for x in range(2):
+                    col = P * (2 * u + x)
+                    nc.tensor.transpose(bank[:, col : col + P], pairs[:, u, 2 * g + x, :], ident[:])
+            return bank
+
+        def weave_c(copy, half, g, bank):
+            dealt = c_woven[half][:].bitcast(F32).rearrange("p (w i g x y u) -> p g w x i y u", w=4, g=2, x=2, y=2, u=2)
+            copy(dealt[:, g], bank[:].rearrange("p (u x i y w) -> p w x i y u", u=2, x=2, y=2, w=4))
+
+        def quantise_c(half):
             nc.vector.quantize_mx(
                 out=c_codes[:, H * half : H * (half + 1)].bitcast(FP8X4),
                 scales=c_scales[:, H * half : H * (half + 1)],
-                in_=c_woven[:],
+                in_=c_woven[half][:],
             )
 
         h_scales = held("h_scales", [P, S], U8)
@@ -310,26 +316,32 @@ def tile_list_chromatin_loop_map_kernel(
                 nc.scalar.activation(sig[:, j : j + P, :], bank[:].rearrange("p (t c) -> p c t", t=4), ACT.Sigmoid)
             sigs[r, half] = sig
 
-        def occ_product(r, half):
-            width = ROUNDS[r]
-            woven = held("loop_woven%d_%d" % (r, half), [P, width, 4], BF16)
-            nc.vector.tensor_tensor(
-                woven[:], sigs[r, half][:], occs[:, half : half + 1, :].to_broadcast([P, width, 4]), MULT
-            )
-            loop_woven[r, half] = woven
+        loop_codes = [held("loop_codes%d" % r, [P, 2 * width], U32) for r, width in enumerate(ROUNDS)]
+        loop_scales = [held("loop_scales%d" % r, [P, 2 * width], U8) for r, width in enumerate(ROUNDS)]
 
-        def loop_quantise(r, half):
-            width = ROUNDS[r]
-            codes = held("loop_codes%d_%d" % (r, half), [P, width], U32)
-            scales = held("loop_scales%d_%d" % (r, half), [P, width], U8)
-            nc.vector.quantize_mx(
-                out=codes[:].bitcast(FP8X4), scales=scales[:], in_=loop_woven[r, half][:].rearrange("p c t -> p (c t)")
+        def occ_product(woven, sig, half):
+            factors = occ_bank[0][:].rearrange("p (t x) -> p x t", t=4)[:, half : half + 1, :]
+            nc.vector.tensor_tensor(woven, sig, factors.to_broadcast(list(sig.shape)), MULT)
+
+        def side_product(woven, sig):
+            width = sig.shape[1]
+            nc.gpsimd.tensor_tensor(
+                woven.rearrange("p (n c) t -> p n (c t)", c=16),
+                sig.rearrange("p (n c) t -> p n (c t)", c=16),
+                occ_run[:].rearrange("p c t -> p (c t)").unsqueeze(1).to_broadcast([P, width // 16, 64]),
+                MULT,
             )
-            loop_mx[r, half] = codes, scales
+
+        def loop_quantise(r, first, woven):
+            cols = slice(first, first + woven.shape[1])
+            nc.vector.quantize_mx(
+                out=loop_codes[r][:, cols].bitcast(FP8X4),
+                scales=loop_scales[r][:, cols],
+                in_=woven[:].rearrange("p c t -> p (c t)"),
+            )
 
         def read_back(r):
             j0, width = starts[r], ROUNDS[r]
-            loop = [loop_mx[r, half] for half in range(2)]
             banks = [take_bank(number) for number in RESULT_BANKS[r]]
             shared = 4 // len(banks)
             for half in range(2):
@@ -340,23 +352,36 @@ def tile_list_chromatin_loop_map_kernel(
                         out=banks[tile // shared][:, width * n : width * (n + 1)],
                         lhsT=c_codes[:, cols].bitcast(FP8X4),
                         lhsT_scale=c_scales[:, cols],
-                        rhs=loop[half][0][:].bitcast(FP8X4),
-                        rhs_scale=loop[half][1][:],
+                        rhs=loop_codes[r][:, width * half : width * (half + 1)].bitcast(FP8X4),
+                        rhs_scale=loop_scales[r][:, width * half : width * (half + 1)],
                         start=(half == 0 and n == 0),
                         stop=(half == 1 and n == shared - 1),
                     )
-            for tile0 in (0, 2):
-                result = held("result%d_%d" % (r, tile0), [P, 2, width], F32)
+            result_banks[r] = banks
+
+        def store_results(r, tile0, on_vector, tag=None):
+            j0, width = starts[r], ROUNDS[r]
+            banks = result_banks[r]
+            shared = 4 // len(banks)
+            result = held(tag or "result%d_%d" % (r, tile0), [P, 2, width], F32)
+            if len(on_vector) == 2:
+                nc.vector.tensor_tensor(
+                    result[:],
+                    banks[tile0 // 2][:, 0 : 2 * width].rearrange("p (w c) -> p w c", w=2),
+                    gains[:, tile0 : tile0 + 2].unsqueeze(2).to_broadcast([P, 2, width]),
+                    MULT,
+                )
+            else:
                 for n in range(2):
                     tile = tile0 + n
                     sums = banks[tile // shared][:, width * (tile % shared) : width * (tile % shared + 1)]
-                    if j0 + width == S and n == 1:
+                    if n in on_vector:
                         nc.vector.tensor_scalar(result[:, n, :], sums, gains[:, tile : tile + 1], None, MULT)
                     else:
                         nc.scalar.activation(result[:, n, :], sums, ACT.Copy, scale=gains[:, tile : tile + 1])
-                nc.sync.dma_start(
-                    out.rearrange("(q w) j -> q w j", w=4)[:, tile0 : tile0 + 2, j0 : j0 + width], result[:]
-                )
+            nc.sync.dma_start(
+                out.rearrange("(q w) j -> q w j", w=4)[:, tile0 : tile0 + 2, j0 : j0 + width], result[:]
+            )
 
         h_banks = [take_bank(n) for n in range(BANKS)]
         quantise_wb(0, "wb_codes0")
@@ -384,10 +409,12 @@ def tile_list_chromatin_loop_map_kernel(
         occs = held("occs", [P, 2, 4], F32)
         gains = held("gains", [P, 4], F32)
         nc.sync.dma_start(occs[:], occ.rearrange("(h p t) -> p h t", h=2, t=4))
-        occ_run = held("occ_run", [P, 64, 4], F32)
-        nc.scalar.copy(occ_run[:], occs[:, 0:1, :].to_broadcast([P, 64, 4]))
+        occ_rows = wb_raw[1][3][:].rearrange("p i c -> p (i c)")
+        nc.sync.dma_start(occ_rows[0:2, 0:PASS], occ.rearrange("(h c) -> h c", h=2))
+        occ_run = held("occ_run", [P, 16, 4], F32)
+        nc.scalar.copy(occ_run[:], occs[:, 0:1, :].to_broadcast([P, 16, 4]))
         nc.sync.dma_start(gains[:], gain.rearrange("(q r) -> q r", r=4))
-        sigs, loop_woven, loop_mx = {}, {}, {}
+        sigs, result_banks, occ_bank = {}, {}, []
 
         for number in range(EARLY_BANKS):
             motif_passes(0, number, True)
@@ -397,50 +424,65 @@ def tile_list_chromatin_loop_map_kernel(
         quantise_b(0)
         for number in range(4):
             dwell_product(number)
+        quantise_h(held("b_woven0", [P, S // 2], U32)[:], S // 2)
         for number in range(4, 8):
             finish_b(number)
-        weave_b(4)
-        weave_b(5)
-        sigmoids(0, 0)
-        weave_b(6)
-        weave_b(7)
+            weave_b(number)
+        quantise_b(1)
         for number in range(4, 8):
             dwell_product(number)
-
-        first_woven = held("loop_woven0_0", [P, ROUNDS[0], 4], BF16)
-        nc.gpsimd.tensor_tensor(
-            first_woven[:, 0:P, :].rearrange("p (n c) t -> p n (c t)", c=64),
-            sigs[0, 0][:, 0:P, :].rearrange("p (n c) t -> p n (c t)", c=64),
-            occ_run[:].rearrange("p c t -> p (c t)").unsqueeze(1).to_broadcast([P, P // 64, 256]),
-            MULT,
-        )
-        loop_woven[0, 0] = first_woven
-
-        quantise_b(1)
-        nc.vector.tensor_tensor(
-            first_woven[:, P:, :], sigs[0, 0][:, P:, :], occs[:, 0:1, :].to_broadcast([P, P, 4]), MULT
-        )
-        quantise_h(held(SHARED, [P, S // 2], U32)[:], S // 2)
+        sigmoids(0, 0)
         sigmoids(1, 0)
-        c_woven = [turn_c(0, [nc.scalar.copy, nc.scalar.copy])]
         sigmoids(0, 1)
+        for g in range(2):
+            weave_c(nc.vector.tensor_copy, 0, g, turn_c(0, g))
         sigmoids(1, 1)
-        c_woven.append(turn_c(1, [nc.scalar.copy, nc.scalar.copy]))
-        sigmoids(2, 0)
-        sigmoids(2, 1)
-        for r in (3, 4):
+        occ_bank.append(take_bank(OCC_BANK))
+        for t in range(4):
+            nc.tensor.transpose(occ_bank[0][:, P * t : P * (t + 1)], occ_rows[:, t:PASS:4], ident[:])
+        for g in range(2):
+            weave_c(nc.scalar.copy, 1, g, turn_c(1, g))
+        for r in (2, 3):
             sigmoids(r, 0)
             sigmoids(r, 1)
 
-        units = [(1, 0), (0, 1), (1, 1), (2, 0), (2, 1), (3, 0), (3, 1), (4, 0), (4, 1)]
-        occ_product(*units[0])
-        quantise_c(0, c_woven[0])
-        loop_quantise(0, 0)
-        for n, (r, half) in enumerate(units):
-            if n + 1 < len(units):
-                occ_product(*units[n + 1])
-            loop_quantise(r, half)
-            if (r, half) == (0, 1):
-                quantise_c(1, c_woven[1])
-            if half == 1:
-                read_back(r)
+        woven = [held(tag, [P, 4 * P, 4], BF16) for tag in (SHARED, "woven1")]
+        for r in range(2):
+            side_product(woven[r][:, 0 : 2 * P, :], sigs[r, 0][:])
+            occ_product(woven[r][:, 2 * P :, :], sigs[r, 1][:], 1)
+        quantise_c(0)
+        loop_quantise(0, 0, woven[0])
+        quantise_c(1)
+        read_back(0)
+        store_results(0, 0, [])
+        store_results(0, 2, [])
+        sigmoids(4, 0)
+        sigmoids(4, 1)
+        loop_quantise(1, 0, woven[1])
+
+        woven20 = held("woven1", [P, 2 * P, 4], BF16)
+        side_product(woven20[:], sigs[2, 0][:])
+        woven21 = held("woven21", [P, 2 * P, 4], BF16)
+        occ_product(woven21[:], sigs[2, 1][:], 1)
+        woven3 = held("woven3", [P, 2 * P, 4], BF16)
+        for half in range(2):
+            occ_product(woven3[:, P * half : P * (half + 1), :], sigs[3, half][:], half)
+        loop_quantise(2, 0, woven20)
+        loop_quantise(2, 2 * P, woven21)
+        read_back(1)
+        read_back(2)
+        loop_quantise(3, 0, woven3)
+        read_back(3)
+        last = [held("woven4%d" % half, [P, P, 4], BF16) for half in range(2)]
+        for half in range(2):
+            occ_product(last[half][:], sigs[4, half][:], half)
+        for half in range(2):
+            loop_quantise(4, P * half, last[half])
+        read_back(4)
+        for r in (1, 2):
+            store_results(r, 0, [])
+            store_results(r, 2, [])
+        store_results(3, 0, [])
+        store_results(3, 2, [0, 1], "woven40")
+        store_results(4, 0, [1])
+        store_results(4, 2, [1])

@@ -27,6 +27,7 @@ ROUNDS = [256, 256, 256, 128, 128]
 SCORE_BANKS = [[[0, 1], [0, 1]], [[2, 3], [2, 3]], [[7, 2], [3, 4]], [[5], [0]], [[1], [7]]]
 RESULT_BANKS = [[1, 7], [2, 3], [4, 5], [1, 7], [0, 6, 2, 3]]
 OCC_BANK = 6
+SIDE = [256, 192, 192]
 TURN_BANKS = [[4, 5], [0, 1]]
 DWELL_BANKS = [6, 7]
 EARLY_BANKS = 6
@@ -326,9 +327,9 @@ def tile_list_chromatin_loop_map_kernel(
         def side_product(woven, sig):
             width = sig.shape[1]
             nc.gpsimd.tensor_tensor(
-                woven.rearrange("p (n c) t -> p n (c t)", c=16),
-                sig.rearrange("p (n c) t -> p n (c t)", c=16),
-                occ_run[:].rearrange("p c t -> p (c t)").unsqueeze(1).to_broadcast([P, width // 16, 64]),
+                woven.rearrange("p (n c) t -> p n (c t)", c=64),
+                sig.rearrange("p (n c) t -> p n (c t)", c=64),
+                occ_run[:].rearrange("p c t -> p (c t)").unsqueeze(1).to_broadcast([P, width // 64, 256]),
                 MULT,
             )
 
@@ -411,8 +412,8 @@ def tile_list_chromatin_loop_map_kernel(
         nc.sync.dma_start(occs[:], occ.rearrange("(h p t) -> p h t", h=2, t=4))
         occ_rows = wb_raw[1][3][:].rearrange("p i c -> p (i c)")
         nc.sync.dma_start(occ_rows[0:2, 0:PASS], occ.rearrange("(h c) -> h c", h=2))
-        occ_run = held("occ_run", [P, 16, 4], F32)
-        nc.scalar.copy(occ_run[:], occs[:, 0:1, :].to_broadcast([P, 16, 4]))
+        occ_run = held("occ_run", [P, 64, 4], F32)
+        nc.scalar.copy(occ_run[:], occs[:, 0:1, :].to_broadcast([P, 64, 4]))
         nc.sync.dma_start(gains[:], gain.rearrange("(q r) -> q r", r=4))
         sigs, result_banks, occ_bank = {}, {}, []
 
@@ -448,7 +449,9 @@ def tile_list_chromatin_loop_map_kernel(
 
         woven = [held(tag, [P, 4 * P, 4], BF16) for tag in (SHARED, "woven1")]
         for r in range(2):
-            side_product(woven[r][:, 0 : 2 * P, :], sigs[r, 0][:])
+            side_product(woven[r][:, 0 : SIDE[r], :], sigs[r, 0][:, 0 : SIDE[r], :])
+        occ_product(woven[1][:, SIDE[1] : 2 * P, :], sigs[1, 0][:, SIDE[1] :, :], 0)
+        for r in range(2):
             occ_product(woven[r][:, 2 * P :, :], sigs[r, 1][:], 1)
         quantise_c(0)
         loop_quantise(0, 0, woven[0])
@@ -461,9 +464,10 @@ def tile_list_chromatin_loop_map_kernel(
         loop_quantise(1, 0, woven[1])
 
         woven20 = held("woven1", [P, 2 * P, 4], BF16)
-        side_product(woven20[:], sigs[2, 0][:])
+        side_product(woven20[:, 0 : SIDE[2], :], sigs[2, 0][:, 0 : SIDE[2], :])
         woven21 = held("woven21", [P, 2 * P, 4], BF16)
         occ_product(woven21[:], sigs[2, 1][:], 1)
+        occ_product(woven20[:, SIDE[2] :, :], sigs[2, 0][:, SIDE[2] :, :], 0)
         woven3 = held("woven3", [P, 2 * P, 4], BF16)
         for half in range(2):
             occ_product(woven3[:, P * half : P * (half + 1), :], sigs[3, half][:], half)

@@ -16,6 +16,7 @@ FP8X4 = mybir.dt.float8_e4m3fn_x4
 FP4X4 = mybir.dt.float4_e2m1fn_x4
 ACT = mybir.ActivationFunctionType
 MULT = mybir.AluOpType.mult
+ADD = mybir.AluOpType.add
 
 P = 128
 PASSES = 2
@@ -43,6 +44,7 @@ PLACES = {
     "sig1_0": 35 * KIB,
     "c_codes": 32 * KIB,
     "loop_codes0": 36 * KIB,
+    "occ_run": 24 * KIB,
     "tab2_second": 20 * KIB,
     "occs": 0,
     "gains": 1 * KIB,
@@ -321,7 +323,7 @@ def tile_list_chromatin_loop_map_kernel(
         loop_scales = [held("loop_scales%d" % r, [P, 2 * width], U8) for r, width in enumerate(ROUNDS)]
 
         def occ_product(woven, sig, half):
-            factors = occ_bank[0][:].rearrange("p (t x) -> p x t", t=4)[:, half : half + 1, :]
+            factors = occ_bank[0][:].rearrange("p (x t) -> p x t", t=4)[:, half : half + 1, :]
             nc.vector.tensor_tensor(woven, sig, factors.to_broadcast(list(sig.shape)), MULT)
 
         def side_product(woven, sig):
@@ -413,7 +415,7 @@ def tile_list_chromatin_loop_map_kernel(
         occ_rows = wb_raw[1][3][:].rearrange("p i c -> p (i c)")
         nc.sync.dma_start(occ_rows[0:2, 0:PASS], occ.rearrange("(h c) -> h c", h=2))
         occ_run = held("occ_run", [P, 64, 4], F32)
-        nc.scalar.copy(occ_run[:], occs[:, 0:1, :].to_broadcast([P, 64, 4]))
+        nc.gpsimd.tensor_scalar(occ_run[:], occs[:, 0:1, :].to_broadcast([P, 64, 4]), 1.0, 0.0, MULT, ADD)
         nc.sync.dma_start(gains[:], gain.rearrange("(q r) -> q r", r=4))
         sigs, result_banks, occ_bank = {}, {}, []
 
@@ -440,7 +442,7 @@ def tile_list_chromatin_loop_map_kernel(
         sigmoids(1, 1)
         occ_bank.append(take_bank(OCC_BANK))
         for t in range(4):
-            nc.tensor.transpose(occ_bank[0][:, P * t : P * (t + 1)], occ_rows[:, t:PASS:4], ident[:])
+            nc.tensor.transpose(occ_bank[0][:, t:PASS:4], occ_rows[:, t:PASS:4], ident[:])
         for g in range(2):
             weave_c(nc.scalar.copy, 1, g, turn_c(1, g))
         for r in (2, 3):

@@ -409,13 +409,13 @@ def tile_list_chromatin_loop_map_kernel(
         quantise_h(held("h_codes0", [P, S // 2], U32)[:], 0)
         quantise_wb(1, "wb_codes1")
         motifs.append(motif_gathers(1))
-        occs = held("occs", [P, 2, 4], F32)
+        occs = held("occs", [P, 4], F32)
         gains = held("gains", [P, 4], F32)
-        nc.sync.dma_start(occs[:], occ.rearrange("(h p t) -> p h t", h=2, t=4))
+        nc.sync.dma_start(occs[:], occ[0:PASS].rearrange("(p t) -> p t", t=4))
         occ_rows = wb_raw[1][3][:].rearrange("p i c -> p (i c)")
         nc.sync.dma_start(occ_rows[0:2, 0:PASS], occ.rearrange("(h c) -> h c", h=2))
         occ_run = held("occ_run", [P, 64, 4], F32)
-        nc.gpsimd.tensor_scalar(occ_run[:], occs[:, 0:1, :].to_broadcast([P, 64, 4]), 1.0, 0.0, MULT, ADD)
+        nc.gpsimd.tensor_scalar(occ_run[:], occs[:].unsqueeze(1).to_broadcast([P, 64, 4]), 1.0, 0.0, MULT, ADD)
         nc.sync.dma_start(gains[:], gain.rearrange("(q r) -> q r", r=4))
         sigs, result_banks, occ_bank = {}, {}, []
 
@@ -468,20 +468,20 @@ def tile_list_chromatin_loop_map_kernel(
         woven20 = held("woven1", [P, 2 * P, 4], BF16)
         side_product(woven20[:, 0 : SIDE[2], :], sigs[2, 0][:, 0 : SIDE[2], :])
         woven21 = held("woven21", [P, 2 * P, 4], BF16)
-        occ_product(woven21[:], sigs[2, 1][:], 1)
         occ_product(woven20[:, SIDE[2] :, :], sigs[2, 0][:, SIDE[2] :, :], 0)
+        occ_product(woven21[:], sigs[2, 1][:], 1)
         woven3 = held("woven3", [P, 2 * P, 4], BF16)
-        for half in range(2):
-            occ_product(woven3[:, P * half : P * (half + 1), :], sigs[3, half][:], half)
+        occ_product(woven3[:, 0:P, :], sigs[3, 0][:], 0)
         loop_quantise(2, 0, woven20)
         loop_quantise(2, 2 * P, woven21)
         read_back(1)
         read_back(2)
+        occ_product(woven3[:, P:, :], sigs[3, 1][:], 1)
+        last = [held("woven4%d" % half, [P, P, 4], BF16) for half in range(2)]
+        occ_product(last[0][:], sigs[4, 0][:], 0)
         loop_quantise(3, 0, woven3)
         read_back(3)
-        last = [held("woven4%d" % half, [P, P, 4], BF16) for half in range(2)]
-        for half in range(2):
-            occ_product(last[half][:], sigs[4, half][:], half)
+        occ_product(last[1][:], sigs[4, 1][:], 1)
         for half in range(2):
             loop_quantise(4, P * half, last[half])
         read_back(4)

@@ -23,12 +23,12 @@ PASSES = 2
 PASS = 512
 BANKS = 8
 ANCHORS = 256
-MOTIF_GATHERS = [[512, 512], [256, 256, 512]]
+MOTIF_GATHERS = [[512, 512], [128, 128, 256, 512]]
 ROUNDS = [256, 256, 256, 128, 128]
-SCORE_BANKS = [[[0, 1], [0, 1]], [[2, 3], [2, 3]], [[7, 2], [3, 4]], [[5], [0]], [[1], [7]]]
+SCORE_BANKS = [[[0, 1], [0, 1]], [[2, 3], [2, 3]], [[7, 2], [3, 4]], [[5], [0]], [[2], [1]]]
 RESULT_BANKS = [[1, 7], [2, 3], [4, 5], [1, 7], [0, 6, 2, 3]]
 OCC_BANK = 6
-SIDE = [256, 192, 192]
+SIDE = [256, 192, 128, 64]
 TURN_BANKS = [[4, 5], [0, 1]]
 DWELL_BANKS = [6, 7]
 EARLY_BANKS = 6
@@ -455,40 +455,42 @@ def tile_list_chromatin_loop_map_kernel(
         occ_product(woven[1][:, SIDE[1] : 2 * P, :], sigs[1, 0][:, SIDE[1] :, :], 0)
         for r in range(2):
             occ_product(woven[r][:, 2 * P :, :], sigs[r, 1][:], 1)
+        sigmoids(4, 0)
         quantise_c(0)
         loop_quantise(0, 0, woven[0])
         quantise_c(1)
         read_back(0)
         store_results(0, 0, [])
         store_results(0, 2, [])
-        sigmoids(4, 0)
         sigmoids(4, 1)
         loop_quantise(1, 0, woven[1])
+        read_back(1)
+        store_results(1, 0, [])
+        store_results(1, 2, [])
 
         woven20 = held("woven1", [P, 2 * P, 4], BF16)
         side_product(woven20[:, 0 : SIDE[2], :], sigs[2, 0][:, 0 : SIDE[2], :])
         woven21 = held("woven21", [P, 2 * P, 4], BF16)
         occ_product(woven20[:, SIDE[2] :, :], sigs[2, 0][:, SIDE[2] :, :], 0)
         occ_product(woven21[:], sigs[2, 1][:], 1)
-        woven3 = held("woven3", [P, 2 * P, 4], BF16)
-        occ_product(woven3[:, 0:P, :], sigs[3, 0][:], 0)
         loop_quantise(2, 0, woven20)
         loop_quantise(2, 2 * P, woven21)
-        read_back(1)
         read_back(2)
-        occ_product(woven3[:, P:, :], sigs[3, 1][:], 1)
-        last = [held("woven4%d" % half, [P, P, 4], BF16) for half in range(2)]
-        occ_product(last[0][:], sigs[4, 0][:], 0)
+        last = [held(tag, [P, P, 4], BF16) for tag in ("woven21", "woven41")]
+        side_product(last[0][:, 0 : SIDE[3], :], sigs[4, 0][:, 0 : SIDE[3], :])
+        woven3 = held("woven3", [P, 2 * P, 4], BF16)
+        for half in range(2):
+            occ_product(woven3[:, P * half : P * (half + 1), :], sigs[3, half][:], half)
+        occ_product(last[0][:, SIDE[3] :, :], sigs[4, 0][:, SIDE[3] :, :], 0)
         loop_quantise(3, 0, woven3)
         read_back(3)
         occ_product(last[1][:], sigs[4, 1][:], 1)
         for half in range(2):
             loop_quantise(4, P * half, last[half])
         read_back(4)
-        for r in (1, 2):
-            store_results(r, 0, [])
-            store_results(r, 2, [])
+        store_results(2, 0, [])
+        store_results(2, 2, [])
         store_results(3, 0, [])
-        store_results(3, 2, [0, 1], "woven40")
+        store_results(3, 2, [0, 1], "woven21")
         store_results(4, 0, [1])
         store_results(4, 2, [1])

@@ -340,7 +340,7 @@ def tile_list_chromatin_loop_map_kernel(
             nc.vector.quantize_mx(
                 out=loop_codes[r][:, cols].bitcast(FP8X4),
                 scales=loop_scales[r][:, cols],
-                in_=woven[:].rearrange("p c t -> p (c t)"),
+                in_=woven.rearrange("p c t -> p (c t)"),
             )
 
         def read_back(r):
@@ -457,13 +457,13 @@ def tile_list_chromatin_loop_map_kernel(
             occ_product(woven[r][:, 2 * P :, :], sigs[r, 1][:], 1)
         sigmoids(4, 0)
         quantise_c(0)
-        loop_quantise(0, 0, woven[0])
+        loop_quantise(0, 0, woven[0][:])
         quantise_c(1)
         read_back(0)
         store_results(0, 0, [])
         store_results(0, 2, [])
         sigmoids(4, 1)
-        loop_quantise(1, 0, woven[1])
+        loop_quantise(1, 0, woven[1][:])
         read_back(1)
         store_results(1, 0, [])
         store_results(1, 2, [])
@@ -473,24 +473,31 @@ def tile_list_chromatin_loop_map_kernel(
         woven21 = held("woven21", [P, 2 * P, 4], BF16)
         occ_product(woven20[:, SIDE[2] :, :], sigs[2, 0][:, SIDE[2] :, :], 0)
         occ_product(woven21[:], sigs[2, 1][:], 1)
-        loop_quantise(2, 0, woven20)
-        loop_quantise(2, 2 * P, woven21)
+        loop_quantise(2, 0, woven20[:])
+        loop_quantise(2, 2 * P, woven21[:])
         read_back(2)
         last = [held(tag, [P, P, 4], BF16) for tag in ("woven21", "woven41")]
         side_product(last[0][:, 0 : SIDE[3], :], sigs[4, 0][:, 0 : SIDE[3], :])
         woven3 = held("woven3", [P, 2 * P, 4], BF16)
         for half in range(2):
             occ_product(woven3[:, P * half : P * (half + 1), :], sigs[3, half][:], half)
+        loop_quantise(3, 0, woven3[:, 0:P, :])
         occ_product(last[0][:, SIDE[3] :, :], sigs[4, 0][:, SIDE[3] :, :], 0)
-        loop_quantise(3, 0, woven3)
+        loop_quantise(3, P, woven3[:, P:, :])
         read_back(3)
         occ_product(last[1][:], sigs[4, 1][:], 1)
         for half in range(2):
-            loop_quantise(4, P * half, last[half])
+            loop_quantise(4, P * half, last[half][:])
         read_back(4)
         store_results(2, 0, [])
         store_results(2, 2, [])
         store_results(3, 0, [])
         store_results(3, 2, [0, 1], "woven21")
-        store_results(4, 0, [1])
-        store_results(4, 2, [1])
+        j0, width = starts[4], ROUNDS[4]
+        for tile, bank in enumerate(result_banks[4]):
+            result = held("last_result%d" % tile, [P, width], F32)
+            if tile % 2 == 1:
+                nc.vector.tensor_scalar(result[:], bank[:, 0:width], gains[:, tile : tile + 1], None, MULT)
+            else:
+                nc.scalar.activation(result[:], bank[:, 0:width], ACT.Copy, scale=gains[:, tile : tile + 1])
+            nc.sync.dma_start(out.rearrange("(q w) j -> q w j", w=4)[:, tile, j0 : j0 + width], result[:])

@@ -31,6 +31,7 @@ OCC_BANK = 6
 SIDE = [256, 192, 128, 64]
 TURN_BANKS = [[4, 5], [0, 1]]
 DWELL_BANKS = [6, 7]
+OCC_TURN_BANK = 6
 EARLY_BANKS = 6
 
 KIB = 1024
@@ -46,7 +47,6 @@ PLACES = {
     "loop_codes0": 36 * KIB,
     "occ_run": 24 * KIB,
     "tab2_second": 20 * KIB,
-    "occs": 0,
     "gains": 1 * KIB,
 }
 SHARED = "shared"
@@ -323,7 +323,7 @@ def tile_list_chromatin_loop_map_kernel(
         loop_scales = [held("loop_scales%d" % r, [P, 2 * width], U8) for r, width in enumerate(ROUNDS)]
 
         def occ_product(woven, sig, half):
-            factors = occ_bank[0][:].rearrange("p (x t) -> p x t", t=4)[:, half : half + 1, :]
+            factors = occ_bank[0][:, 0:8].rearrange("p (x t) -> p x t", t=4)[:, half : half + 1, :]
             nc.vector.tensor_tensor(woven, sig, factors.to_broadcast(list(sig.shape)), MULT)
 
         def side_product(woven, sig):
@@ -409,18 +409,20 @@ def tile_list_chromatin_loop_map_kernel(
         quantise_h(held("h_codes0", [P, S // 2], U32)[:], 0)
         quantise_wb(1, "wb_codes1")
         motifs.append(motif_gathers(1))
-        occs = held("occs", [P, 4], F32)
+        occs = wb_raw[1][3][:, 0, 0:P]
         gains = held("gains", [P, 4], F32)
-        nc.sync.dma_start(occs[:], occ[0:PASS].rearrange("(p t) -> p t", t=4))
-        occ_rows = wb_raw[1][3][:].rearrange("p i c -> p (i c)")
-        nc.sync.dma_start(occ_rows[0:2, 0:PASS], occ.rearrange("(h c) -> h c", h=2))
+        nc.sync.dma_start(occs[:, 0:8].rearrange("p (h t) -> p h t", t=4), occ.rearrange("(h p t) -> p h t", h=2, t=4))
         occ_run = held("occ_run", [P, 64, 4], F32)
-        nc.gpsimd.tensor_scalar(occ_run[:], occs[:].unsqueeze(1).to_broadcast([P, 64, 4]), 1.0, 0.0, MULT, ADD)
+        nc.gpsimd.tensor_scalar(occ_run[:], occs[:, 0:4].unsqueeze(1).to_broadcast([P, 64, 4]), 1.0, 0.0, MULT, ADD)
         nc.sync.dma_start(gains[:], gain.rearrange("(q r) -> q r", r=4))
         sigs, result_banks, occ_bank = {}, {}, []
 
         for number in range(EARLY_BANKS):
             motif_passes(0, number, True)
+        occ_turned = held("occ_turned", [P, P], F32)
+        bank = take_bank(OCC_TURN_BANK)
+        nc.tensor.transpose(bank[:, 0:P], occs, ident[:])
+        nc.scalar.copy(occ_turned[:], bank[:, 0:P])
         for number in range(4):
             finish_b(number)
             weave_b(number)
@@ -441,8 +443,7 @@ def tile_list_chromatin_loop_map_kernel(
             weave_c(nc.vector.tensor_copy, 0, g, turn_c(0, g))
         sigmoids(1, 1)
         occ_bank.append(take_bank(OCC_BANK))
-        for t in range(4):
-            nc.tensor.transpose(occ_bank[0][:, t:PASS:4], occ_rows[:, t:PASS:4], ident[:])
+        nc.tensor.transpose(occ_bank[0][:, 0:P], occ_turned[:], ident[:])
         for g in range(2):
             weave_c(nc.scalar.copy, 1, g, turn_c(1, g))
         for r in (2, 3):

@@ -343,11 +343,11 @@ def tile_list_chromatin_loop_map_kernel(
                 in_=woven.rearrange("p c t -> p (c t)"),
             )
 
-        def read_back(r):
+        def read_back(r, halves=(0, 1)):
             j0, width = starts[r], ROUNDS[r]
             banks = [take_bank(number) for number in RESULT_BANKS[r]]
             shared = 4 // len(banks)
-            for half in range(2):
+            for half in halves:
                 for tile in range(4):
                     cols = slice(H * half + P * tile, H * half + P * (tile + 1))
                     n = tile % shared
@@ -357,8 +357,8 @@ def tile_list_chromatin_loop_map_kernel(
                         lhsT_scale=c_scales[:, cols],
                         rhs=loop_codes[r][:, width * half : width * (half + 1)].bitcast(FP8X4),
                         rhs_scale=loop_scales[r][:, width * half : width * (half + 1)],
-                        start=(half == 0 and n == 0),
-                        stop=(half == 1 and n == shared - 1),
+                        start=(half == halves[0] and n == 0),
+                        stop=(half == halves[1] and n == shared - 1),
                     )
             result_banks[r] = banks
 
@@ -472,12 +472,12 @@ def tile_list_chromatin_loop_map_kernel(
         woven20 = held("woven1", [P, 2 * P, 4], BF16)
         side_product(woven20[:, 0 : SIDE[2], :], sigs[2, 0][:, 0 : SIDE[2], :])
         woven21 = held("woven21", [P, 2 * P, 4], BF16)
-        occ_product(woven20[:, SIDE[2] :, :], sigs[2, 0][:, SIDE[2] :, :], 0)
         occ_product(woven21[:], sigs[2, 1][:], 1)
-        loop_quantise(2, 0, woven20[:])
+        occ_product(woven20[:, SIDE[2] :, :], sigs[2, 0][:, SIDE[2] :, :], 0)
         loop_quantise(2, 2 * P, woven21[:])
-        read_back(2)
-        last = [held(tag, [P, P, 4], BF16) for tag in ("woven21", "woven41")]
+        loop_quantise(2, 0, woven20[:])
+        read_back(2, (1, 0))
+        last = [held(tag, [P, P, 4], BF16) for tag in ("woven1", "woven41")]
         side_product(last[0][:, 0 : SIDE[3], :], sigs[4, 0][:, 0 : SIDE[3], :])
         woven3 = held("woven3", [P, 2 * P, 4], BF16)
         for half in range(2):
@@ -493,7 +493,7 @@ def tile_list_chromatin_loop_map_kernel(
         store_results(2, 0, [])
         store_results(2, 2, [])
         store_results(3, 0, [])
-        store_results(3, 2, [0, 1], "woven21")
+        store_results(3, 2, [0, 1], "woven1")
         j0, width = starts[4], ROUNDS[4]
         for tile, bank in enumerate(result_banks[4]):
             result = held("last_result%d" % tile, [P, width], F32)

@@ -25,7 +25,7 @@ BANKS = 8
 ANCHORS = 256
 MOTIF_GATHERS = [[512, 512], [128, 128, 256, 512]]
 ROUNDS = [256, 256, 256, 128, 128]
-SCORE_BANKS = [[[0, 1], [0, 1]], [[2, 3], [2, 3]], [[7, 2], [3, 4]], [[5], [0]], [[2], [1]]]
+SCORE_BANKS = [[[0, 1], [0, 1]], [[2, 3], [2, 3]], [[7, 2], [3, 4]], [[5], [0]], [[2], [0]]]
 RESULT_BANKS = [[1, 7], [2, 3], [4, 5], [1, 7], [0, 6, 2, 3]]
 OCC_BANK = 6
 SIDE = [256, 192, 128, 64]
@@ -419,11 +419,14 @@ def tile_list_chromatin_loop_map_kernel(
 
         for number in range(EARLY_BANKS):
             motif_passes(0, number, True)
+        for number in range(2):
+            finish_b(number)
+            weave_b(number)
         occ_turned = held("occ_turned", [P, P], F32)
         bank = take_bank(OCC_TURN_BANK)
         nc.tensor.transpose(bank[:, 0:P], occs, ident[:])
         nc.scalar.copy(occ_turned[:], bank[:, 0:P])
-        for number in range(4):
+        for number in range(2, 4):
             finish_b(number)
             weave_b(number)
         quantise_b(0)
@@ -497,8 +500,9 @@ def tile_list_chromatin_loop_map_kernel(
         j0, width = starts[4], ROUNDS[4]
         for tile, bank in enumerate(result_banks[4]):
             result = held("last_result%d" % tile, [P, width], F32)
-            if tile % 2 == 1:
+            if tile % 2 == 0:
                 nc.vector.tensor_scalar(result[:], bank[:, 0:width], gains[:, tile : tile + 1], None, MULT)
             else:
                 nc.scalar.activation(result[:], bank[:, 0:width], ACT.Copy, scale=gains[:, tile : tile + 1])
-            nc.sync.dma_start(out.rearrange("(q w) j -> q w j", w=4)[:, tile, j0 : j0 + width], result[:])
+            queue = nc.scalar if tile == 3 else nc.sync
+            queue.dma_start(out.rearrange("(q w) j -> q w j", w=4)[:, tile, j0 : j0 + width], result[:])

@@ -504,5 +504,4 @@ def tile_list_chromatin_loop_map_kernel(
                 nc.vector.tensor_scalar(result[:], bank[:, 0:width], gains[:, tile : tile + 1], None, MULT)
             else:
                 nc.scalar.activation(result[:], bank[:, 0:width], ACT.Copy, scale=gains[:, tile : tile + 1])
-            queue = nc.scalar if tile == 3 else nc.sync
-            queue.dma_start(out.rearrange("(q w) j -> q w j", w=4)[:, tile, j0 : j0 + width], result[:])
+            nc.sync.dma_start(out.rearrange("(q w) j -> q w j", w=4)[:, tile, j0 : j0 + width], result[:])

from contextlib import ExitStack

import concourse.mybir as mybir
from concourse.masks import make_identity

K, H, T, S = 1024, 512, 2048, 1024
FLOPS = 2 * (K * H * S + K * H * S + H * S * S + S * H * S)

F32 = mybir.dt.float32
BF16 = mybir.dt.bfloat16
I32 = mybir.dt.int32
U32 = mybir.dt.uint32
U16 = mybir.dt.uint16
U8 = mybir.dt.uint8
FP8X4 = mybir.dt.float8_e4m3fn_x4
FP4X4 = mybir.dt.float4_e2m1fn_x4
ACT = mybir.ActivationFunctionType
MULT = mybir.AluOpType.mult
ADD = mybir.AluOpType.add

P = 128
PASSES = 2
PASS = 512
BANKS = 8
ANCHORS = 256
MOTIF_GATHERS = [[512, 512], [128, 128, 256, 512]]
ROUNDS = [256, 256, 256, 128, 128]
SCORE_BANKS = [[[0, 1], [0, 1]], [[2, 3], [2, 3]], [[7, 2], [3, 4]], [[5], [0]], [[2], [0]]]
RESULT_BANKS = [[1, 7], [2, 3], [4, 5], [1, 7], [0, 6, 2, 3]]
OCC_BANK = 6
SIDE = [256, 192, 128, 64]
TURN_BANKS = [[4, 5], [0, 1]]
DWELL_BANKS = [6, 7]
OCC_TURN_BANK = 6
EARLY_BANKS = 6

KIB = 1024
PLACES = {
    "scale_rows1": 7 * KIB,
    "tab_second": 0,
    "tab2_first": 8 * KIB,
    "wb_first": 16 * KIB,
    "wb_last": 16 * KIB,
    "h_woven1": 16 * KIB,
    "sig1_0": 35 * KIB,
    "c_codes": 32 * KIB,
    "loop_codes0": 36 * KIB,
    "occ_run": 24 * KIB,
    "tab2_second": 20 * KIB,
    "gains": 1 * KIB,
}
SHARED = "shared"
MOTIF_PLANE = 8


def tile_list_chromatin_loop_map_kernel(
    tc, tab_words, tab_scales, tab2_words, tab2_scales, wm_words, wm_scales, wb, occ, dwell, gain, offs, offs2, out
):
    nc = tc.nc
    with ExitStack() as ctx:
        keep = ctx.enter_context(tc.tile_pool(name="keep", bufs=1))
        psum = ctx.enter_context(tc.psum_pool(name="psum", bufs=1))

        def take_bank(number):
            return psum.tile([P, 512], F32, name="bank%d" % number)

        reused = ctx.enter_context(tc.tile_pool(name="reused", bufs=1))

        def held(tag, shape, dtype):
            if tag in PLACES:
                return reused.tile(shape, dtype, name=tag, align_bytes=64, offset=PLACES[tag])
            return keep.tile(shape, dtype, name=tag, align_bytes=64)

        lists = held("lists", [P, S // 16], U16)
        list2 = held("list2", [P, S // 16], U16)
        scale_rows1 = held("scale_rows1", [P, T], U8)
        scale_rows2 = held("scale_rows2", [P, T], U8)
        planes1 = held("planes1", [P, PASSES * S], U8)
        planes2 = held("planes2", [P, PASSES * S], U8)
        wm_scale_rows = held("wm_scale_rows", [P, PASSES * H], U8)
        ident = held("ident", [P, P], F32)
        dwell_rows = held("dwell_rows", [P, 8], F32)

        warm = held("warm", [P, 2], F32)
        nc.vector.memset(scale_rows1[:].bitcast(I32), 0)
        nc.vector.memset(warm[:, 0:1], 0.0)
        nc.vector.memset(scale_rows2[:].bitcast(I32), 0)
        nc.vector.memset(wm_scale_rows[:].bitcast(I32), 0)
        nc.vector.memset(planes1[:].bitcast(I32), 0)
        nc.vector.memset(planes2[:].bitcast(I32), 0)
        nc.scalar.activation(warm[:, 1:2], warm[:, 0:1], ACT.Sigmoid)

        def load_words(tag, table, a):
            words = held(tag, [P, T], I32)
            nc.sync.dma_start(words[:], table[a].rearrange("p t i -> p (t i)").bitcast(I32))
            return words

        def load_wb(tag, a, c0, width):
            raw = held(tag, [P, 4, width], F32)
            nc.sync.dma_start(raw[:], wb[PASS * a : PASS * (a + 1), c0 : c0 + width].rearrange("(p i) c -> p i c", i=4))
            return a, c0, width, raw

        nc.gpsimd.dma_start(dwell_rows[:], dwell.rearrange("(n c) -> n c", c=8))
        make_identity(nc, ident[:])

        nc.sync.dma_start(lists[:], offs)
        nc.sync.dma_start(list2[:], offs2)
        wm_raw = held("wm_raw", [P, PASSES, 2 * H], U8)
        nc.sync.dma_start(wm_raw[:].bitcast(I32), wm_words.rearrange("a p c -> p a c").bitcast(I32))
        nc.sync.dma_start(scale_rows1[0:P:4, :].bitcast(I32), tab_scales.rearrange("a q t -> q a t").bitcast(I32))
        words1 = [load_words("tab_first", tab_words, 0)]
        nc.sync.dma_start(scale_rows2[0:P:4, :].bitcast(I32), tab2_scales.rearrange("a q t -> q a t").bitcast(I32))
        for d in range(4):
            nc.sync.dma_start(
                wm_scale_rows[32 * d : 32 * d + 4, :].bitcast(I32).rearrange("i (a c) -> i a c", a=PASSES),
                wm_scales[:, 4 * d : 4 * d + 4, :].rearrange("a i c -> i a c").bitcast(I32),
            )
        wb_raw = [load_wb("wb_first", 0, 0, H)]
        wb_raw.append(load_wb("wb_middle", 1, 0, H // 2))

        picked1 = held("picked1", [P, S], U8)
        nc.vector.tensor_copy(picked1[:], scale_rows1[:].indirect(lists[:]))
        for d in range(4):
            nc.sync.dma_start(
                planes1[32 * d : 32 * d + 4, :].bitcast(I32), picked1[32 * d : 32 * d + 32 : 4, :].bitcast(I32)
            )
        first_pass = held("anchors0", [P, S], U32)
        nc.vector.tensor_copy(first_pass[:], words1[0][:].bitcast(U32).indirect(lists[:]))

        words1.append(load_words("tab_second", tab_words, 1))
        words2 = [load_words("tab2_first", tab2_words, 0)]
        picked2 = held("picked2", [P, S], U8)
        nc.vector.tensor_copy(picked2[:], scale_rows2[:].indirect(list2[:]))
        for d in range(4):
            row = 32 * d + MOTIF_PLANE
            nc.sync.dma_start(
                planes2[row : row + 4, :].bitcast(I32), picked2[32 * d : 32 * d + 32 : 4, :].bitcast(I32)
            )

        wm_codes = held("wm_codes", [P, PASSES * 2 * H], U8)
        nc.scalar.copy(
            wm_codes[:].bitcast(U32).rearrange("p (a t i w) -> p a t i w", a=PASSES, t=4, w=4),
            wm_raw[:].bitcast(U32).rearrange("p a (i t w) -> p a t i w", t=4, w=4),
        )
        wm_planes = held("wm_planes", [P, PASSES * H], U8)
        nc.scalar.copy(
            wm_planes[:].bitcast(U32).rearrange("p (a t i w) -> p a t i w", a=PASSES, t=4, w=2),
            wm_scale_rows[:].bitcast(U32).rearrange("p (a i t w) -> p a t i w", a=PASSES, t=4, w=2),
        )
        wb_raw.append(load_wb("wb_last", 1, H // 2, H // 2))
        words2.append(load_words("tab2_second", tab2_words, 1))

        wb_woven = [held("wb_woven%d" % a, [P, H * 4], BF16) for a in range(PASSES)]

        def weave_wb(copy, a, c0, width, raw):
            dealt = wb_woven[a][:].rearrange("p (t i g n k) -> p g i t k n", t=4, g=2, n=4, k=4)
            for g in range(2):
                copy(
                    dealt[:, g, c0 // 32 : (c0 + width) // 32],
                    raw[:].rearrange("p k (i t g n) -> p g i t k n", t=4, g=2, n=4)[:, g],
                )

        for raw in wb_raw:
            weave_wb(nc.scalar.copy, *raw)

        dwells = held("dwells", [P, 8, 2, 64], F32)
        for u in range(2):
            bank = take_bank(DWELL_BANKS[u])
            for g in range(2):
                for e in range(2):
                    c = 4 * g + 2 * u + e
                    col = P * (2 * g + e)
                    nc.tensor.transpose(bank[:, col : col + P], dwell_rows[:, c : c + 1].to_broadcast([P, P]), ident[:])
            nc.scalar.copy(
                dwells[:, :, u, :].rearrange("p b (n g e) -> p b n g e", g=2, e=2),
                bank[:].rearrange("p (g e b n) -> p b n g e", g=2, e=2, b=8),
            )

        wb_codes = []
        wb_scales = held("wb_scales", [P, PASSES * H], U8)

        def quantise_wb(a, tag):
            wb_codes.append(held(tag, [P, H], U32))
            nc.vector.quantize_mx(
                out=wb_codes[a][:].bitcast(FP8X4), scales=wb_scales[:, H * a : H * (a + 1)], in_=wb_woven[a][:]
            )

        def motif_gathers(a):
            slices = []
            for width in MOTIF_GATHERS[a]:
                m0 = P * len(slices)
                picked = held("motifs%d_%d" % (a, m0), [P, width], U32)
                offsets = list2[:, m0 // 16 : (m0 + width) // 16]
                nc.vector.tensor_copy(picked[:], words2[a][:].bitcast(U32).indirect(offsets))
                slices.extend([picked[:, j : j + P] for j in range(0, width, P)])
            return slices

        b_codes = held("b_codes", [P, S], U32)
        b_scales = held("b_scales", [P, S], U8)
        c_codes = held("c_codes", [P, 2 * H], U32)
        c_scales = held("c_scales", [P, 2 * H], U8)

        b_woven = [held(tag, [P, 4, P, 4], BF16) for tag in ("b_woven0", SHARED)]
        c_pairs = [held("c_pairs%d" % half, [P, 2, 4, 256], BF16) for half in range(2)]
        b_banks = {}

        def motif_passes(a, number, first):
            if first:
                b_banks[number] = take_bank(number)
            m0 = P * number
            for t in range(4):
                nc.tensor.matmul_mx(
                    out=b_banks[number][:, P * t : P * (t + 1)],
                    lhsT=wb_codes[a][:, P * t : P * (t + 1)].bitcast(FP8X4),
                    lhsT_scale=wb_scales[:, H * a + P * t : H * a + P * (t + 1)],
                    rhs=motifs[a][number].bitcast(FP8X4),
                    rhs_scale=planes2[MOTIF_PLANE:P, S * a + m0 : S * a + m0 + P],
                    start=(first and t == 0),
                    stop=(not first and t == 3),
                )

        def finish_b(number):
            late = number >= EARLY_BANKS
            motif_passes(1, number, late)
            if late:
                motif_passes(0, number, False)

        def weave_b(number):
            half, n = divmod(number, 4)
            nc.scalar.copy(
                b_woven[half][:, :, 32 * n : 32 * (n + 1), :],
                b_banks[number][:].rearrange("p (t q v) -> p v q t", t=4, v=4),
            )

        def quantise_b(half):
            nc.vector.quantize_mx(
                out=b_codes[:, PASS * half : PASS * (half + 1)].bitcast(FP8X4),
                scales=b_scales[:, PASS * half : PASS * (half + 1)],
                in_=b_woven[half][:].rearrange("p v q t -> p (v q t)"),
            )

        def dwell_product(number):
            half, n = divmod(number, 4)
            factors = dwells[:, number, :, :].unsqueeze(2).to_broadcast([P, 2, 4, 64])
            nc.vector.tensor_tensor(
                c_pairs[half][:, :, :, 64 * n : 64 * (n + 1)].rearrange("p u t (q e) -> p u t q e", e=2),
                b_banks[number][:].rearrange("p (t q u e) -> p u t q e", t=4, u=2, e=2),
                factors.rearrange("p u t (q e) -> p u t q e", e=2),
                MULT,
            )

        c_woven = [held("c_woven%d" % half, [P, H * 4], BF16) for half in range(2)]

        def turn_c(half, g):
            pairs = c_pairs[half][:].bitcast(F32)
            bank = take_bank(TURN_BANKS[half][g])
            for u in range(2):
                for x in range(2):
                    col = P * (2 * u + x)
                    nc.tensor.transpose(bank[:, col : col + P], pairs[:, u, 2 * g + x, :], ident[:])
            return bank

        def weave_c(copy, half, g, bank):
            dealt = c_woven[half][:].bitcast(F32).rearrange("p (w i g x y u) -> p g w x i y u", w=4, g=2, x=2, y=2, u=2)
            copy(dealt[:, g], bank[:].rearrange("p (u x i y w) -> p w x i y u", u=2, x=2, y=2, w=4))

        def quantise_c(half):
            nc.vector.quantize_mx(
                out=c_codes[:, H * half : H * (half + 1)].bitcast(FP8X4),
                scales=c_scales[:, H * half : H * (half + 1)],
                in_=c_woven[half][:],
            )

        h_scales = held("h_scales", [P, S], U8)
        h_woven = [held("h_woven%d" % half, [P, S // 2, 4], BF16) for half in range(2)]

        def anchor_passes(a, bank, j, picked):
            for t in range(4):
                nc.tensor.matmul_mx(
                    out=bank[:, P * t : P * (t + 1)],
                    lhsT=wm_codes[:, 2 * (H * a + P * t) : 2 * (H * a + P * (t + 1))].bitcast(FP4X4),
                    lhsT_scale=wm_planes[:, H * a + P * t : H * a + P * (t + 1)],
                    rhs=picked.bitcast(FP8X4),
                    rhs_scale=planes1[:, S * a + j : S * a + j + P],
                    start=(a == 0 and t == 0),
                    stop=(a == PASSES - 1 and t == 3),
                )

        def anchor_second_pass(j0, banks):
            picked = held("anchors1_%d" % j0, [P, ANCHORS], U32)
            nc.vector.tensor_copy(
                picked[:], words1[1][:].bitcast(U32).indirect(lists[:, j0 // 16 : (j0 + ANCHORS) // 16])
            )
            for n, bank in enumerate(banks):
                j = j0 + P * n
                anchor_passes(1, bank, j, picked[:, P * n : P * (n + 1)])
                nc.scalar.copy(
                    h_woven[j // PASS][:, j % PASS : j % PASS + P, :], bank[:].rearrange("p (t c) -> p c t", t=4)
                )

        starts = [sum(ROUNDS[:r]) for r in range(len(ROUNDS))]

        def sigmoids(r, half):
            j0, width = starts[r], ROUNDS[r]
            sig = held("sig%d_%d" % (r, half), [P, width, 4], F32)
            for j, number in zip(range(0, width, P), SCORE_BANKS[r][half]):
                bank = take_bank(number)
                for t in range(4):
                    cols = slice(PASS * half + P * t, PASS * half + P * (t + 1))
                    nc.tensor.matmul_mx(
                        out=bank[:, P * t : P * (t + 1)],
                        lhsT=b_codes[:, cols].bitcast(FP8X4),
                        lhsT_scale=b_scales[:, cols],
                        rhs=h_codes[j0 + j].bitcast(FP8X4),
                        rhs_scale=h_scales[:, j0 + j : j0 + j + P],
                        start=True,
                        stop=True,
                    )
                nc.scalar.activation(sig[:, j : j + P, :], bank[:].rearrange("p (t c) -> p c t", t=4), ACT.Sigmoid)
            sigs[r, half] = sig

        loop_codes = [held("loop_codes%d" % r, [P, 2 * width], U32) for r, width in enumerate(ROUNDS)]
        loop_scales = [held("loop_scales%d" % r, [P, 2 * width], U8) for r, width in enumerate(ROUNDS)]

        def occ_product(woven, sig, half):
            factors = occ_bank[0][:, 0:8].rearrange("p (x t) -> p x t", t=4)[:, half : half + 1, :]
            nc.vector.tensor_tensor(woven, sig, factors.to_broadcast(list(sig.shape)), MULT)

        def side_product(woven, sig):
            width = sig.shape[1]
            nc.gpsimd.tensor_tensor(
                woven.rearrange("p (n c) t -> p n (c t)", c=64),
                sig.rearrange("p (n c) t -> p n (c t)", c=64),
                occ_run[:].rearrange("p c t -> p (c t)").unsqueeze(1).to_broadcast([P, width // 64, 256]),
                MULT,
            )

        def loop_quantise(r, first, woven):
            cols = slice(first, first + woven.shape[1])
            nc.vector.quantize_mx(
                out=loop_codes[r][:, cols].bitcast(FP8X4),
                scales=loop_scales[r][:, cols],
                in_=woven.rearrange("p c t -> p (c t)"),
            )

        def read_back(r, halves=(0, 1)):
            j0, width = starts[r], ROUNDS[r]
            banks = [take_bank(number) for number in RESULT_BANKS[r]]
            shared = 4 // len(banks)
            for half in halves:
                for tile in range(4):
                    cols = slice(H * half + P * tile, H * half + P * (tile + 1))
                    n = tile % shared
                    nc.tensor.matmul_mx(
                        out=banks[tile // shared][:, width * n : width * (n + 1)],
                        lhsT=c_codes[:, cols].bitcast(FP8X4),
                        lhsT_scale=c_scales[:, cols],
                        rhs=loop_codes[r][:, width * half : width * (half + 1)].bitcast(FP8X4),
                        rhs_scale=loop_scales[r][:, width * half : width * (half + 1)],
                        start=(half == halves[0] and n == 0),
                        stop=(half == halves[1] and n == shared - 1),
                    )
            result_banks[r] = banks

        def store_results(r, tile0, on_vector, tag=None):
            j0, width = starts[r], ROUNDS[r]
            banks = result_banks[r]
            shared = 4 // len(banks)
            result = held(tag or "result%d_%d" % (r, tile0), [P, 2, width], F32)
            if len(on_vector) == 2:
                nc.vector.tensor_tensor(
                    result[:],
                    banks[tile0 // 2][:, 0 : 2 * width].rearrange("p (w c) -> p w c", w=2),
                    gains[:, tile0 : tile0 + 2].unsqueeze(2).to_broadcast([P, 2, width]),
                    MULT,
                )
            else:
                for n in range(2):
                    tile = tile0 + n
                    sums = banks[tile // shared][:, width * (tile % shared) : width * (tile % shared + 1)]
                    if n in on_vector:
                        nc.vector.tensor_scalar(result[:, n, :], sums, gains[:, tile : tile + 1], None, MULT)
                    else:
                        nc.scalar.activation(result[:, n, :], sums, ACT.Copy, scale=gains[:, tile : tile + 1])
            nc.sync.dma_start(
                out.rearrange("(q w) j -> q w j", w=4)[:, tile0 : tile0 + 2, j0 : j0 + width], result[:]
            )

        h_banks = [take_bank(n) for n in range(BANKS)]
        quantise_wb(0, "wb_codes0")
        for n, bank in enumerate(h_banks):
            anchor_passes(0, bank, P * n, first_pass[:, P * n : P * (n + 1)])
        for j0 in range(0, S, ANCHORS):
            anchor_second_pass(j0, h_banks[j0 // P : (j0 + ANCHORS) // P])
        motifs = [motif_gathers(0)]

        h_codes = {}

        def quantise_h(codes, j0):
            width = codes.shape[1]
            nc.vector.quantize_mx(
                out=codes.bitcast(FP8X4),
                scales=h_scales[:, j0 : j0 + width],
                in_=h_woven[j0 // PASS][:].rearrange("p c t -> p (c t)"),
            )
            for j in range(0, width, P):
                h_codes[j0 + j] = codes[:, j : j + P]

        quantise_h(held("h_codes0", [P, S // 2], U32)[:], 0)
        quantise_wb(1, "wb_codes1")
        motifs.append(motif_gathers(1))
        occs = wb_raw[1][3][:, 0, 0:P]
        gains = held("gains", [P, 4], F32)
        nc.sync.dma_start(occs[:, 0:8].rearrange("p (h t) -> p h t", t=4), occ.rearrange("(h p t) -> p h t", h=2, t=4))
        occ_run = held("occ_run", [P, 64, 4], F32)
        nc.gpsimd.tensor_scalar(occ_run[:], occs[:, 0:4].unsqueeze(1).to_broadcast([P, 64, 4]), 1.0, 0.0, MULT, ADD)
        nc.sync.dma_start(gains[:], gain.rearrange("(q r) -> q r", r=4))
        sigs, result_banks, occ_bank = {}, {}, []

        for number in range(EARLY_BANKS):
            motif_passes(0, number, True)
        for number in range(2):
            finish_b(number)
            weave_b(number)
        occ_turned = held("occ_turned", [P, P], F32)
        bank = take_bank(OCC_TURN_BANK)
        nc.tensor.transpose(bank[:, 0:P], occs, ident[:])
        nc.scalar.copy(occ_turned[:], bank[:, 0:P])
        for number in range(2, 4):
            finish_b(number)
            weave_b(number)
        quantise_b(0)
        for number in range(4):
            dwell_product(number)
        quantise_h(held("b_woven0", [P, S // 2], U32)[:], S // 2)
        for number in range(4, 8):
            finish_b(number)
            weave_b(number)
        quantise_b(1)
        for number in range(4, 8):
            dwell_product(number)
        sigmoids(0, 0)
        sigmoids(1, 0)
        sigmoids(0, 1)
        for g in range(2):
            weave_c(nc.vector.tensor_copy, 0, g, turn_c(0, g))
        sigmoids(1, 1)
        occ_bank.append(take_bank(OCC_BANK))
        nc.tensor.transpose(occ_bank[0][:, 0:P], occ_turned[:], ident[:])
        for g in range(2):
            weave_c(nc.scalar.copy, 1, g, turn_c(1, g))
        for r in (2, 3):
            sigmoids(r, 0)
            sigmoids(r, 1)

        woven = [held(tag, [P, 4 * P, 4], BF16) for tag in (SHARED, "woven1")]
        for r in range(2):
            side_product(woven[r][:, 0 : SIDE[r], :], sigs[r, 0][:, 0 : SIDE[r], :])
        occ_product(woven[1][:, SIDE[1] : 2 * P, :], sigs[1, 0][:, SIDE[1] :, :], 0)
        for r in range(2):
            occ_product(woven[r][:, 2 * P :, :], sigs[r, 1][:], 1)
        sigmoids(4, 0)
        quantise_c(0)
        loop_quantise(0, 0, woven[0][:])
        quantise_c(1)
        read_back(0)
        store_results(0, 0, [])
        store_results(0, 2, [])
        sigmoids(4, 1)
        loop_quantise(1, 0, woven[1][:])
        read_back(1)
        store_results(1, 0, [])
        store_results(1, 2, [])

        woven20 = held("woven1", [P, 2 * P, 4], BF16)
        side_product(woven20[:, 0 : SIDE[2], :], sigs[2, 0][:, 0 : SIDE[2], :])
        woven21 = held("woven21", [P, 2 * P, 4], BF16)
        occ_product(woven21[:], sigs[2, 1][:], 1)
        occ_product(woven20[:, SIDE[2] :, :], sigs[2, 0][:, SIDE[2] :, :], 0)
        loop_quantise(2, 2 * P, woven21[:])
        loop_quantise(2, 0, woven20[:])
        read_back(2, (1, 0))
        last = [held(tag, [P, P, 4], BF16) for tag in ("woven1", "woven41")]
        side_product(last[0][:, 0 : SIDE[3], :], sigs[4, 0][:, 0 : SIDE[3], :])
        woven3 = held("woven3", [P, 2 * P, 4], BF16)
        for half in range(2):
            occ_product(woven3[:, P * half : P * (half + 1), :], sigs[3, half][:], half)
        loop_quantise(3, 0, woven3[:, 0:P, :])
        occ_product(last[0][:, SIDE[3] :, :], sigs[4, 0][:, SIDE[3] :, :], 0)
        loop_quantise(3, P, woven3[:, P:, :])
        read_back(3)
        occ_product(last[1][:], sigs[4, 1][:], 1)
        for half in range(2):
            loop_quantise(4, P * half, last[half][:])
        read_back(4)
        store_results(2, 0, [])
        store_results(2, 2, [])
        store_results(3, 0, [])
        store_results(3, 2, [0, 1], "woven1")
        j0, width = starts[4], ROUNDS[4]
        for tile, bank in enumerate(result_banks[4]):
            result = held("last_result%d" % tile, [P, width], F32)
            if tile % 2 == 0:
                nc.vector.tensor_scalar(result[:], bank[:, 0:width], gains[:, tile : tile + 1], None, MULT)
            else:
                nc.scalar.activation(result[:], bank[:, 0:width], ACT.Copy, scale=gains[:, tile : tile + 1])
            nc.sync.dma_start(out.rearrange("(q w) j -> q w j", w=4)[:, tile, j0 : j0 + width], result[:])
